import numpy as np
import ml_dtypes


def mxq(x, axis, fmt="e4m3"):
    dtype, down = {"e4m3": (ml_dtypes.float8_e4m3fn, 7), "e5m2": (ml_dtypes.float8_e5m2, 14)}[fmt]
    v = np.moveaxis(np.asarray(x, np.float32).astype(ml_dtypes.bfloat16).astype(np.float64), axis, -1)
    blocks = v.reshape(v.shape[:-1] + (-1, 32))
    amax = np.abs(blocks).max(-1, keepdims=True)
    byte = np.maximum(np.where(amax > 0, np.frexp(amax)[1] - 1 + 127, 0) - down, 1)
    scale = np.exp2(byte - 127.0)
    codes = (blocks / scale).astype(np.float32).astype(dtype).astype(np.float64)
    return np.moveaxis((codes * scale).reshape(v.shape), -1, axis)


WIDE = False


def mx_kscale(k):
    if not WIDE:
        return np.ones(k)
    levels = np.array([18, -18])
    if k % 512:
        return np.exp2(np.random.permutation(np.resize(levels, k // 32))).repeat(32)
    a = np.empty((k // 512, 16))
    for p in range(k // 512):
        a[p, :8] = np.random.permutation(np.resize(levels, 8))
        for g in range(8):
            far = levels[np.abs(levels - a[p, g]) >= 10]
            a[p, g + 8] = far[np.random.randint(len(far))]
    return np.exp2(a.ravel()).repeat(32)


def f64(x):
    return np.asarray(x).astype(np.float64)


def striped(idx):
    return np.tile(np.asarray(idx).reshape(-1, 16).T, (8, 1)).astype(np.uint16)


def unstriped(offs):
    return offs[:16].T.reshape(-1).astype(np.int64)

def planes(y):
    n, m = y.shape
    v = y.astype(np.float32).astype(ml_dtypes.bfloat16).astype(np.float64).reshape(n // 32, 32, m)
    top = np.abs(v).max(1)
    byte = np.clip(np.where(top > 0, np.frexp(top)[1] - 1 + 127 - 7, 1), 1, 254)
    codes = (v * np.exp2(127.0 - byte)[:, None, :]).reshape(n, m).astype(np.float32).astype(ml_dtypes.float8_e4m3fn).view(np.uint8)
    words = codes.reshape(n // 512, 128, 4, m).transpose(0, 1, 3, 2)
    return np.ascontiguousarray(words), np.ascontiguousarray(byte.astype(np.uint8).reshape(n // 512, 16, m))


def setup_inputs():
    n = np.random.standard_normal
    uni = np.random.uniform
    idx = np.random.permutation(2048)[:512]
    act = np.random.permutation(2048)[:512]
    f_d = mx_kscale(512)
    return {
        "x2": (n((512, 512)) * f_d[:, None]).astype(np.float32),
        "x": (n((512, 512))).astype(np.float32),
        "w0": (n((512, 2048)) / np.sqrt(512) / f_d[:, None]).astype(np.float32),
        "wT": (n((512, 2048)) / np.sqrt(512)).astype(np.float32),
        "us": (uni(0.75, 1.3, (512, 1))).astype(np.float32),
        "ts": np.tile(uni(0.75, 1.3, 2048), (128, 1)).astype(np.float32),
        "rw": (n((512, 1))).astype(np.float32),
        "wt": (uni(0.75, 1.3, (512, 1))).astype(np.float32),
        "offs": striped(idx),
        "aoffs": striped(act),
    }


def reference(x2, x, w0, wT, us, ts, rw, wt, offs, aoffs):
    idx = unstriped(offs)
    act = unstriped(aoffs)
    w0_i = f64(w0)[:, idx]
    w = f64(wT)[:, act]
    ts_i = f64(ts)[:1][:, idx]
    wr = w.T
    q = (f64(x) * wr).sum(-1, keepdims=True)
    a = mxq(f64(x2), 0, "e4m3").T @ mxq(w0_i, 0, "e4m3")
    z = f64(us) * ts_i * a
    m = (z).max(-1, keepdims=True)
    e = f64(wt) * (q - (f64(rw) + 0.9 * m))
    gr = e * f64(x)
    gT = gr.T
    out_0 = np.zeros((512, 2048))
    out_0[:, act] = gT
    return (out_0,) + planes(out_0)

@@ -1,0 +1,230 @@
+from contextlib import ExitStack
+
+import concourse.mybir as mybir
+from concourse.masks import make_identity
+
+D, R, I, T = 512, 512, 512, 2048
+FLOPS = 2 * D * R * I
+BYTES = 4 * (2 * D * R + 2 * D * T + T + 3 * R + D * T) + 2 * 2 * 128 * 32 + D * T + 16 * T
+
+F32 = mybir.dt.float32
+BF16 = mybir.dt.bfloat16
+U32 = mybir.dt.uint32
+I32 = mybir.dt.int32
+U16 = mybir.dt.uint16
+U8 = mybir.dt.uint8
+FP8X4 = mybir.dt.float8_e4m3fn_x4
+ALU = mybir.AluOpType
+COPY = mybir.ActivationFunctionType.Copy
+
+P = 128
+PACK = 4
+BLOCKS = 4
+HALF = R // 2
+CHUNKS = (256, 256, 512, 512, 256, 256)
+VECTOR_CHUNKS = 4
+
+
+def block(b):
+    return slice(P * b, P * (b + 1))
+
+
+def tile_attend_gtd_pl_kernel(tc, x2, x, w0, wT, us, ts, rw, wt, offs, aoffs, out_0, out_1, out_2):
+    nc = tc.nc
+    with ExitStack() as ctx:
+        lists = ctx.enter_context(tc.tile_pool(name="lists", bufs=1))
+        keep = ctx.enter_context(tc.tile_pool(name="keep", bufs=1))
+        spare = ctx.enter_context(tc.tile_pool(name="spare", bufs=2))
+        psum = ctx.enter_context(tc.psum_pool(name="psum", bufs=1))
+
+        def sb(name, shape, dtype):
+            return keep.tile(shape, dtype, name=name, align_bytes=64)
+
+        def bank(tag, name):
+            return psum.tile([P, 512], F32, name=name, tag=tag)
+
+        slots = lists.tile([P, I // 16], U16, name="slots")
+        taken = lists.tile([P, R // 16], U16, name="taken")
+        nc.sync.dma_start(slots[:], offs)
+
+        vecs = sb("vecs", [P, P], F32)
+        nc.vector.memset(vecs[:], 0.0)
+        ts_cut = sb("ts_cut", [P, 16], F32)
+        nc.sync.dma_start(out=ts_cut[:], in_=ts[0].rearrange("(p m) -> p m", m=16))
+
+        w0_planes = w0.rearrange("(p t) c -> t p c", t=PACK)
+        w0_sb = [sb("w0_%d" % t, [P, T], F32) for t in range(PACK)]
+        for t in range(PACK):
+            nc.sync.dma_start(out=w0_sb[t][:], in_=w0_planes[t])
+            if t == 0:
+                for k, v in enumerate((us, rw, wt)):
+                    nc.sync.dma_start(out=vecs[4 * k : 4 * k + 4, :], in_=v.rearrange("(b p) o -> b (p o)", p=P))
+        nc.sync.dma_start(taken[:], aoffs)
+        x2_sb = sb("x2_sb", [P, PACK, R], F32)
+        nc.sync.dma_start(out=x2_sb[:], in_=x2.rearrange("(p t) r -> p t r", t=PACK))
+        wT_sb = [sb("wT_%d" % j, [P, T], F32) for j in range(BLOCKS)]
+        for j in range(BLOCKS):
+            nc.sync.dma_start(out=wT_sb[j][:], in_=wT[block(j), :])
+        x_sb = [sb("x_%d" % b, [P, D], F32) for b in range(BLOCKS)]
+        for b in range(BLOCKS):
+            nc.sync.dma_start(out=x_sb[b][:], in_=x[block(b), :])
+
+        ident = sb("ident", [P, P], F32)
+        make_identity(nc, ident[:])
+
+        windows = [sb("window_%d" % t, [P, T], F32) for t in range(PACK)]
+        for t in range(PACK):
+            nc.vector.memset(windows[t][:], 0.0)
+
+        ts_all = sb("ts_all", [P, T], F32)
+        ts_view = ts_all[:].rearrange("q (p g m) -> q p g m", g=4, m=4)
+        for g in range(4):
+            ts_bank = bank("b%d" % g, "ts_bank%d" % g)
+            for m in range(4):
+                col = 4 * g + m
+                nc.tensor.transpose(ts_bank[:, block(m)], ts_cut[:, col : col + 1].to_broadcast([P, P]), ident[:])
+            nc.scalar.activation(ts_view[:, :, g, :], ts_bank[:].rearrange("q (m p) -> q p m", m=4), COPY)
+
+        vec_bank = bank("a0", "vec_bank")
+        nc.tensor.transpose(vec_bank[:, 0:P], vecs[:], ident[:])
+        cols = sb("cols", [P, 12], F32)
+        nc.scalar.activation(cols[:], vec_bank[:, 0:12], COPY)
+
+        w0_bf = sb("w0_bf", [P, I, PACK], BF16)
+        ts_listed = sb("ts_listed", [P, I], F32)
+        for t in range(PACK):
+            nc.vector.tensor_copy(w0_bf[:, :, t], w0_sb[t][:].indirect(slots[:]))
+            if t == 1:
+                nc.vector.tensor_copy(ts_listed[:], ts_all[:].indirect(slots[:]))
+        w0_codes = sb("w0_codes", [P, I], U32)
+        w0_scales = sb("w0_scales", [P, I], U8)
+        nc.vector.quantize_mx(out=w0_codes[:].bitcast(FP8X4), scales=w0_scales[:], in_=w0_bf[:].rearrange("p i t -> p (i t)"))
+
+        tscol_bank = bank("a1", "tscol_bank")
+        for j in range(BLOCKS):
+            nc.tensor.transpose(tscol_bank[:, block(j)], ts_listed[:, block(j)], ident[:])
+        ts_col = sb("ts_col", [P, BLOCKS], F32)
+        nc.scalar.activation(ts_col[:], tscol_bank[:].rearrange("p (j q) -> p j q", j=BLOCKS)[:, :, 0], COPY)
+
+        x2_codes = sb("x2_codes", [P, R], U32)
+        x2_scales = sb("x2_scales", [P, R], U8)
+        x2_bf = [sb("x2_bf%d" % h, [P, HALF, PACK], BF16) for h in range(2)]
+        for h in range(2):
+            src = x2_sb[:, :, HALF * h : HALF * (h + 1)].rearrange("p t (c i) -> p c t i", i=4)
+            dst = x2_bf[h][:].rearrange("p (c i) t -> p c t i", i=4)
+            if h == 0:
+                nc.vector.tensor_copy(dst, src)
+            else:
+                nc.scalar.copy(dst, src)
+        for h in range(2):
+            cut = slice(HALF * h, HALF * (h + 1))
+            nc.vector.quantize_mx(out=x2_codes[:, cut].bitcast(FP8X4), scales=x2_scales[:, cut], in_=x2_bf[h][:].rearrange("p r t -> p (r t)"))
+
+        scaled = [sb("scaled%d" % j, [P, R], F32) for j in range(BLOCKS)]
+        for j in range(BLOCKS):
+            a_bank = bank("a%d" % j, "a_bank%d" % j)
+            nc.tensor.matmul_mx(out=a_bank[:], lhsT=w0_codes[:, block(j)].bitcast(FP8X4), lhsT_scale=w0_scales[:, block(j)],
+                                rhs=x2_codes[:].bitcast(FP8X4), rhs_scale=x2_scales[:], start=True, stop=True)
+            nc.scalar.activation(scaled[j][:], a_bank[:], COPY, scale=ts_col[:, j : j + 1])
+
+        wT_listed = [sb("wT_listed%d" % j, [P, R], F32) for j in range(BLOCKS)]
+        q_banks = [bank("b%d" % b, "q_bank%d" % b) for b in range(BLOCKS)]
+
+        def look_up_taken(j):
+            nc.vector.tensor_copy(wT_listed[j][:], wT_sb[j][:].indirect(taken[:]))
+            for b in range(BLOCKS):
+                nc.tensor.transpose(q_banks[b][:, block(j)], wT_listed[j][:, block(b)], ident[:])
+
+        largest = sb("largest", [P, BLOCKS], F32)
+
+        def row_maximum(b):
+            z_bank = bank("a%d" % b, "z_bank%d" % b)
+            for j in range(BLOCKS):
+                nc.tensor.transpose(z_bank[:, block(j)], scaled[j][:, block(b)], ident[:])
+            z = spare.tile([P, I], F32, name="unread", tag="unread")
+            nc.vector.tensor_scalar(out=z[:], in0=z_bank[:], scalar1=cols[:, b : b + 1], scalar2=None, op0=ALU.mult, op1=ALU.max,
+                                    accum_out=largest[:, b : b + 1])
+
+        look_up_taken(0)
+        look_up_taken(1)
+        row_maximum(0)
+        row_maximum(1)
+        look_up_taken(2)
+        row_maximum(2)
+        row_maximum(3)
+        target = sb("target", [P, BLOCKS], F32)
+        nc.vector.scalar_tensor_tensor(out=target[:], in0=largest[:], scalar=-0.9, in1=cols[:, 4:8], op0=ALU.mult, op1=ALU.subtract)
+        look_up_taken(3)
+        wtarget = sb("wtarget", [P, BLOCKS], F32)
+        nc.vector.tensor_tensor(wtarget[:], target[:], cols[:, 8:12], ALU.mult)
+
+        xT = [sb("xT%d" % t, [P, R], F32) for t in range(PACK)]
+
+        def turn_x(t, xt_bank, b):
+            nc.tensor.transpose(xt_bank[:, block(b)], x_sb[b][:].rearrange("r (p t) -> r t p", t=PACK)[:, t, :], ident[:])
+
+        wq = sb("wq", [P, BLOCKS], F32)
+        err = sb("err", [P, R], F32)
+        xt0_banks = [bank("a%d" % h, "xt0_bank%d" % h) for h in range(2)]
+        for h in range(2):
+            cut = slice(HALF * h, HALF * (h + 1))
+            for b in (2 * h, 2 * h + 1):
+                turn_x(0, xt0_banks[h], b)
+                prod = spare.tile([P, D], F32, name="unread", tag="unread")
+                nc.vector.scalar_tensor_tensor(out=prod[:], in0=q_banks[b][:], scalar=cols[:, 8 + b : 9 + b], in1=x_sb[b][:],
+                                               op0=ALU.mult, op1=ALU.mult, accum_out=wq[:, b : b + 1])
+            nc.scalar.copy(xT[0][:, cut], xt0_banks[h][:, cut])
+        for h in range(2):
+            cut = slice(HALF * h, HALF * (h + 1))
+            e_bank = bank("b%d" % h, "e_bank%d" % h)
+            for b in (2 * h, 2 * h + 1):
+                nc.tensor.matmul(e_bank[:, block(b)], lhsT=wtarget[:, b : b + 1].to_broadcast([P, P]), rhs=ident[:], is_transpose=True, start=True, stop=False)
+                nc.tensor.matmul(e_bank[:, block(b)], lhsT=wq[:, b : b + 1].to_broadcast([P, P]), rhs=ident[:], is_transpose=True, start=False, stop=True)
+            nc.scalar.copy(err[:, cut], e_bank[:, cut])
+        for t in range(1, PACK):
+            xt_bank = bank("a%d" % ((t + 1) % 4), "xt_bank%d" % t)
+            for b in range(BLOCKS):
+                turn_x(t, xt_bank, b)
+            nc.scalar.copy(xT[t][:], xt_bank[:])
+
+        starts = [sum(CHUNKS[:k]) for k in range(len(CHUNKS))]
+        pairs = [sb("pairs%d" % k, [P, 2, w, 2], BF16) for k, w in enumerate(CHUNKS)]
+        out_planes = out_0.rearrange("(p t) c -> t p c", t=PACK)
+        for t in range(PACK):
+            if t == 0:
+                for h in range(2):
+                    cut = slice(HALF * h, HALF * (h + 1))
+                    nc.vector.tensor_tensor(windows[t][:].indirect(taken[:, 16 * h : 16 * (h + 1)]), xT[t][:, cut], err[:, cut], ALU.mult)
+            else:
+                nc.vector.tensor_tensor(windows[t][:].indirect(taken[:]), xT[t][:], err[:], ALU.mult)
+            nc.sync.dma_start(out=out_planes[t], in_=windows[t][:])
+            for k, w in enumerate(CHUNKS):
+                nc.scalar.copy(pairs[k][:, t // 2, :, t % 2], windows[t][:, starts[k] : starts[k] + w])
+
+        out_words = out_1[0].rearrange("p c l -> p (c l)").bitcast(I32)
+        out_scales = out_2[0].bitcast(I32)
+        y_scales = sb("y_scales", [P, T], U8)
+        grouped = [sb("grouped%d" % k, [P, w * PACK], BF16) for k, w in enumerate(CHUNKS)]
+        y_codes = [sb("y_codes%d" % k, [P, w], U32) for k, w in enumerate(CHUNKS)]
+
+        def interleave(k):
+            src = pairs[k][:].rearrange("p u c e -> p u (c e)").bitcast(F32).rearrange("p u (c i) -> p c u i", i=4)
+            dst = grouped[k][:].bitcast(F32).rearrange("p (c i u) -> p c u i", i=4, u=2)
+            if k < VECTOR_CHUNKS:
+                nc.vector.tensor_copy(dst, src)
+            else:
+                nc.scalar.copy(dst, src)
+
+        def quantise(k):
+            cut = slice(starts[k], starts[k] + CHUNKS[k])
+            nc.vector.quantize_mx(out=y_codes[k][:].bitcast(FP8X4), scales=y_scales[:, cut], in_=grouped[k][:])
+            nc.sync.dma_start(out=out_words[:, cut], in_=y_codes[k][:].bitcast(I32))
+
+        interleave(0)
+        for k in range(len(CHUNKS)):
+            if k + 1 < len(CHUNKS):
+                interleave(k + 1)
+            quantise(k)
+        for quad in range(4):
+            queue = nc.scalar if quad % 2 else nc.sync
+            queue.dma_start(out=out_scales[4 * quad : 4 * quad + 4, :], in_=y_scales[32 * quad : 32 * quad + 4, :].bitcast(I32))

@@ -21,8 +21,10 @@ P = 128
 PACK = 4
 BLOCKS = 4
 HALF = R // 2
-CHUNKS = (256, 256, 512, 512, 256, 256)
-VECTOR_CHUNKS = 4
+WIDTH = 256
+CHUNKS = T // WIDTH
+VECTOR_ROUNDS = 2
+VECTOR_WEAVES = 5
 
 
 def block(b):
@@ -34,7 +36,7 @@ def tile_attend_gtd_pl_kernel(tc, x2, x, w0, wT, us, ts, rw, wt, offs, aoffs, ou
     with ExitStack() as ctx:
         lists = ctx.enter_context(tc.tile_pool(name="lists", bufs=1))
         keep = ctx.enter_context(tc.tile_pool(name="keep", bufs=1))
-        spare = ctx.enter_context(tc.tile_pool(name="spare", bufs=2))
+        spare = ctx.enter_context(tc.tile_pool(name="spare", bufs=4))
         psum = ctx.enter_context(tc.psum_pool(name="psum", bufs=1))
 
         def sb(name, shape, dtype):
@@ -45,41 +47,37 @@ def tile_attend_gtd_pl_kernel(tc, x2, x, w0, wT, us, ts, rw, wt, offs, aoffs, ou
 
         slots = lists.tile([P, I // 16], U16, name="slots")
         taken = lists.tile([P, R // 16], U16, name="taken")
-        nc.sync.dma_start(slots[:], offs)
-
         vecs = sb("vecs", [P, P], F32)
         nc.vector.memset(vecs[:], 0.0)
         ts_cut = sb("ts_cut", [P, 16], F32)
-        nc.sync.dma_start(out=ts_cut[:], in_=ts[0].rearrange("(p m) -> p m", m=16))
 
         w0_planes = w0.rearrange("(p t) c -> t p c", t=PACK)
         w0_sb = [sb("w0_%d" % t, [P, T], F32) for t in range(PACK)]
         for t in range(PACK):
             nc.sync.dma_start(out=w0_sb[t][:], in_=w0_planes[t])
             if t == 0:
+                nc.sync.dma_start(out=ts_cut[:], in_=ts[0].rearrange("(p m) -> p m", m=16))
+                nc.sync.dma_start(slots[:], offs)
                 for k, v in enumerate((us, rw, wt)):
                     nc.sync.dma_start(out=vecs[4 * k : 4 * k + 4, :], in_=v.rearrange("(b p) o -> b (p o)", p=P))
         nc.sync.dma_start(taken[:], aoffs)
         x2_sb = sb("x2_sb", [P, PACK, R], F32)
         nc.sync.dma_start(out=x2_sb[:], in_=x2.rearrange("(p t) r -> p t r", t=PACK))
-        wT_sb = [sb("wT_%d" % j, [P, T], F32) for j in range(BLOCKS)]
-        for j in range(BLOCKS):
-            nc.sync.dma_start(out=wT_sb[j][:], in_=wT[block(j), :])
-        x_sb = [sb("x_%d" % b, [P, D], F32) for b in range(BLOCKS)]
-        for b in range(BLOCKS):
-            nc.sync.dma_start(out=x_sb[b][:], in_=x[block(b), :])
+        x_sb = sb("x_sb", [P, BLOCKS, D], F32)
+        nc.sync.dma_start(out=x_sb[:], in_=x.rearrange("(b p) d -> p b d", p=P))
+        wT_planes = wT.rearrange("(p t) c -> t p c", t=PACK)
+        wT_sb = [keep.tile([P, T], F32, name="wT_%d" % t, tag="table%d" % t, align_bytes=64) for t in range(PACK)]
+        for t in range(PACK):
+            nc.sync.dma_start(out=wT_sb[t][:], in_=wT_planes[t])
 
         ident = sb("ident", [P, P], F32)
         make_identity(nc, ident[:])
 
-        windows = [sb("window_%d" % t, [P, T], F32) for t in range(PACK)]
-        for t in range(PACK):
-            nc.vector.memset(windows[t][:], 0.0)
 
         ts_all = sb("ts_all", [P, T], F32)
         ts_view = ts_all[:].rearrange("q (p g m) -> q p g m", g=4, m=4)
         for g in range(4):
-            ts_bank = bank("b%d" % g, "ts_bank%d" % g)
+            ts_bank = bank("q%d" % g, "ts_bank%d" % g)
             for m in range(4):
                 col = 4 * g + m
                 nc.tensor.transpose(ts_bank[:, block(m)], ts_cut[:, col : col + 1].to_broadcast([P, P]), ident[:])
@@ -106,8 +104,8 @@ def tile_attend_gtd_pl_kernel(tc, x2, x, w0, wT, us, ts, rw, wt, offs, aoffs, ou
         ts_col = sb("ts_col", [P, BLOCKS], F32)
         nc.scalar.activation(ts_col[:], tscol_bank[:].rearrange("p (j q) -> p j q", j=BLOCKS)[:, :, 0], COPY)
 
-        x2_codes = sb("x2_codes", [P, R], U32)
-        x2_scales = sb("x2_scales", [P, R], U8)
+        x2_codes = [sb("x2_codes%d" % h, [P, HALF], U32) for h in range(2)]
+        x2_scales = [sb("x2_scales%d" % h, [P, HALF], U8) for h in range(2)]
         x2_bf = [sb("x2_bf%d" % h, [P, HALF, PACK], BF16) for h in range(2)]
         for h in range(2):
             src = x2_sb[:, :, HALF * h : HALF * (h + 1)].rearrange("p t (c i) -> p c t i", i=4)
@@ -117,78 +115,94 @@ def tile_attend_gtd_pl_kernel(tc, x2, x, w0, wT, us, ts, rw, wt, offs, aoffs, ou
             else:
                 nc.scalar.copy(dst, src)
         for h in range(2):
-            cut = slice(HALF * h, HALF * (h + 1))
-            nc.vector.quantize_mx(out=x2_codes[:, cut].bitcast(FP8X4), scales=x2_scales[:, cut], in_=x2_bf[h][:].rearrange("p r t -> p (r t)"))
-
-        scaled = [sb("scaled%d" % j, [P, R], F32) for j in range(BLOCKS)]
-        for j in range(BLOCKS):
-            a_bank = bank("a%d" % j, "a_bank%d" % j)
-            nc.tensor.matmul_mx(out=a_bank[:], lhsT=w0_codes[:, block(j)].bitcast(FP8X4), lhsT_scale=w0_scales[:, block(j)],
-                                rhs=x2_codes[:].bitcast(FP8X4), rhs_scale=x2_scales[:], start=True, stop=True)
-            nc.scalar.activation(scaled[j][:], a_bank[:], COPY, scale=ts_col[:, j : j + 1])
-
-        wT_listed = [sb("wT_listed%d" % j, [P, R], F32) for j in range(BLOCKS)]
-        q_banks = [bank("b%d" % b, "q_bank%d" % b) for b in range(BLOCKS)]
-
-        def look_up_taken(j):
-            nc.vector.tensor_copy(wT_listed[j][:], wT_sb[j][:].indirect(taken[:]))
-            for b in range(BLOCKS):
-                nc.tensor.transpose(q_banks[b][:, block(j)], wT_listed[j][:, block(b)], ident[:])
-
-        largest = sb("largest", [P, BLOCKS], F32)
-
-        def row_maximum(b):
-            z_bank = bank("a%d" % b, "z_bank%d" % b)
-            for j in range(BLOCKS):
-                nc.tensor.transpose(z_bank[:, block(j)], scaled[j][:, block(b)], ident[:])
-            z = spare.tile([P, I], F32, name="unread", tag="unread")
-            nc.vector.tensor_scalar(out=z[:], in0=z_bank[:], scalar1=cols[:, b : b + 1], scalar2=None, op0=ALU.mult, op1=ALU.max,
-                                    accum_out=largest[:, b : b + 1])
-
-        look_up_taken(0)
-        look_up_taken(1)
-        row_maximum(0)
-        row_maximum(1)
-        look_up_taken(2)
-        row_maximum(2)
-        row_maximum(3)
-        target = sb("target", [P, BLOCKS], F32)
-        nc.vector.scalar_tensor_tensor(out=target[:], in0=largest[:], scalar=-0.9, in1=cols[:, 4:8], op0=ALU.mult, op1=ALU.subtract)
-        look_up_taken(3)
-        wtarget = sb("wtarget", [P, BLOCKS], F32)
-        nc.vector.tensor_tensor(wtarget[:], target[:], cols[:, 8:12], ALU.mult)
+            nc.vector.quantize_mx(out=x2_codes[h][:].bitcast(FP8X4), scales=x2_scales[h][:], in_=x2_bf[h][:].rearrange("p r t -> p (r t)"))
 
         xT = [sb("xT%d" % t, [P, R], F32) for t in range(PACK)]
 
-        def turn_x(t, xt_bank, b):
-            nc.tensor.transpose(xt_bank[:, block(b)], x_sb[b][:].rearrange("r (p t) -> r t p", t=PACK)[:, t, :], ident[:])
-
-        wq = sb("wq", [P, BLOCKS], F32)
-        err = sb("err", [P, R], F32)
-        xt0_banks = [bank("a%d" % h, "xt0_bank%d" % h) for h in range(2)]
-        for h in range(2):
-            cut = slice(HALF * h, HALF * (h + 1))
-            for b in (2 * h, 2 * h + 1):
-                turn_x(0, xt0_banks[h], b)
-                prod = spare.tile([P, D], F32, name="unread", tag="unread")
-                nc.vector.scalar_tensor_tensor(out=prod[:], in0=q_banks[b][:], scalar=cols[:, 8 + b : 9 + b], in1=x_sb[b][:],
-                                               op0=ALU.mult, op1=ALU.mult, accum_out=wq[:, b : b + 1])
-            nc.scalar.copy(xT[0][:, cut], xt0_banks[h][:, cut])
-        for h in range(2):
-            cut = slice(HALF * h, HALF * (h + 1))
-            e_bank = bank("b%d" % h, "e_bank%d" % h)
-            for b in (2 * h, 2 * h + 1):
-                nc.tensor.matmul(e_bank[:, block(b)], lhsT=wtarget[:, b : b + 1].to_broadcast([P, P]), rhs=ident[:], is_transpose=True, start=True, stop=False)
-                nc.tensor.matmul(e_bank[:, block(b)], lhsT=wq[:, b : b + 1].to_broadcast([P, P]), rhs=ident[:], is_transpose=True, start=False, stop=True)
-            nc.scalar.copy(err[:, cut], e_bank[:, cut])
-        for t in range(1, PACK):
-            xt_bank = bank("a%d" % ((t + 1) % 4), "xt_bank%d" % t)
+        def turn_x(t):
+            xt_bank = bank("c%d" % (t % 2), "xt_bank%d" % t)
             for b in range(BLOCKS):
-                turn_x(t, xt_bank, b)
+                nc.tensor.transpose(xt_bank[:, block(b)], x_sb[:, b, :].rearrange("r (p t) -> r t p", t=PACK)[:, t, :], ident[:])
             nc.scalar.copy(xT[t][:], xt_bank[:])
 
-        starts = [sum(CHUNKS[:k]) for k in range(len(CHUNKS))]
-        pairs = [sb("pairs%d" % k, [P, 2, w, 2], BF16) for k, w in enumerate(CHUNKS)]
+        terms = [sb("terms%d" % t, [P, R], F32) for t in range(PACK)]
+        q_banks = [bank("q%d" % b, "q_bank%d" % b) for b in range(BLOCKS)]
+
+        def turn_terms(t, blocks):
+            for b in blocks:
+                nc.tensor.matmul(q_banks[b][:, 0:P], lhsT=terms[t][:, block(b)], rhs=ident[:], is_transpose=True, start=(t == 0), stop=(t == PACK - 1))
+
+        def look_up_taken(t):
+            nc.vector.tensor_tensor(terms[t][:], wT_sb[t][:].indirect(taken[:]), xT[t][:], ALU.mult)
+            turn_terms(t, range(BLOCKS))
+
+        largest = sb("largest", [P, BLOCKS], F32)
+
+        def row_maximum(b, scores):
+            z = spare.tile([P, I], F32, name="unread", tag="unread")
+            nc.vector.tensor_scalar(out=z[:], in0=scores, scalar1=cols[:, b : b + 1], scalar2=None, op0=ALU.mult, op1=ALU.max,
+                                    accum_out=largest[:, b : b + 1])
+
+        row_banks = [bank("a%d" % b, "row_bank%d" % b) for b in range(2)]
+        for b in range(2):
+            nc.tensor.matmul_mx(out=row_banks[b][:], lhsT=x2_codes[0][:, block(b)].bitcast(FP8X4), lhsT_scale=x2_scales[0][:, block(b)],
+                                rhs=w0_codes[:].bitcast(FP8X4), rhs_scale=w0_scales[:], start=True, stop=True)
+        turn_x(0)
+        scaled_rows = [sb("scaled_rows%d" % b, [P, I], F32) for b in range(2)]
+        for b in range(2):
+            nc.vector.tensor_tensor(scaled_rows[b][:], row_banks[b][:], ts_listed[:], ALU.mult)
+        for b in range(2):
+            row_maximum(b, scaled_rows[b][:])
+
+        scaled_slots = [sb("scaled_slots%d" % j, [P, HALF], F32) for j in range(BLOCKS)]
+        for j in range(BLOCKS):
+            slot_bank = bank("q%d" % j, "slot_bank%d" % j)
+            nc.tensor.matmul_mx(out=slot_bank[:, 0:HALF], lhsT=w0_codes[:, block(j)].bitcast(FP8X4), lhsT_scale=w0_scales[:, block(j)],
+                                rhs=x2_codes[1][:].bitcast(FP8X4), rhs_scale=x2_scales[1][:], start=True, stop=True)
+            nc.scalar.activation(scaled_slots[j][:], slot_bank[:, 0:HALF], COPY, scale=ts_col[:, j : j + 1])
+        z_banks = [bank("a%d" % k, "z_bank%d" % k) for k in range(2)]
+        for k in range(2):
+            for j in range(BLOCKS):
+                nc.tensor.transpose(z_banks[k][:, block(j)], scaled_slots[j][:, block(k)], ident[:])
+        turn_x(1)
+        look_up_taken(0)
+        for k in range(2):
+            row_maximum(2 + k, z_banks[k][:])
+        turn_x(2)
+        look_up_taken(1)
+        turn_x(3)
+        target = sb("target", [P, BLOCKS], F32)
+        nc.vector.scalar_tensor_tensor(out=target[:], in0=largest[:], scalar=-0.9, in1=cols[:, 4:8], op0=ALU.mult, op1=ALU.subtract)
+        look_up_taken(2)
+        wtarget = sb("wtarget", [P, BLOCKS], F32)
+        nc.vector.tensor_tensor(wtarget[:], target[:], cols[:, 8:12], ALU.mult)
+        last = PACK - 1
+        for h in range(2):
+            cut = slice(HALF * h, HALF * (h + 1))
+            nc.vector.tensor_tensor(terms[last][:, cut], wT_sb[last][:].indirect(taken[:, 16 * h : 16 * (h + 1)]), xT[last][:, cut], ALU.mult)
+            turn_terms(last, (2 * h, 2 * h + 1))
+
+        wq = [sb("wq%d" % h, [P, 2], F32) for h in range(2)]
+        err = sb("err", [P, R], F32)
+        for h in range(2):
+            cut = slice(HALF * h, HALF * (h + 1))
+            e_bank = bank("a%d" % h, "e_bank%d" % h)
+            for k in range(2):
+                b = 2 * h + k
+                summed = spare.tile([P, P], F32, name="summed", tag="summed")
+                if h == 0:
+                    nc.scalar.activation(summed[:], q_banks[b][:, 0:P], COPY, scale=cols[:, 8 + b : 9 + b], accum_out=wq[h][:, k : k + 1])
+                else:
+                    nc.vector.tensor_scalar(out=summed[:], in0=q_banks[b][:, 0:P], scalar1=cols[:, 8 + b : 9 + b], scalar2=None, op0=ALU.mult, op1=ALU.add,
+                                            accum_out=wq[h][:, k : k + 1])
+                nc.tensor.matmul(e_bank[:, block(b)], lhsT=wtarget[:, b : b + 1].to_broadcast([P, P]), rhs=ident[:], is_transpose=True, start=True, stop=False)
+                nc.tensor.matmul(e_bank[:, block(b)], lhsT=wq[h][:, k : k + 1].to_broadcast([P, P]), rhs=ident[:], is_transpose=True, start=False, stop=True)
+            nc.scalar.copy(err[:, cut], e_bank[:, cut])
+
+        windows = [keep.tile([P, T], F32, name="window_%d" % t, tag="table%d" % t, align_bytes=64) for t in range(PACK)]
+        for t in range(PACK):
+            nc.gpsimd.memset(windows[t][:], 0.0)
+        pairs = sb("pairs", [P, CHUNKS, 2, WIDTH, 2], BF16)
         out_planes = out_0.rearrange("(p t) c -> t p c", t=PACK)
         for t in range(PACK):
             if t == 0:
@@ -198,33 +212,49 @@ def tile_attend_gtd_pl_kernel(tc, x2, x, w0, wT, us, ts, rw, wt, offs, aoffs, ou
             else:
                 nc.vector.tensor_tensor(windows[t][:].indirect(taken[:]), xT[t][:], err[:], ALU.mult)
             nc.sync.dma_start(out=out_planes[t], in_=windows[t][:])
-            for k, w in enumerate(CHUNKS):
-                nc.scalar.copy(pairs[k][:, t // 2, :, t % 2], windows[t][:, starts[k] : starts[k] + w])
+            chunked = windows[t][:].rearrange("p (k c) -> p k c", c=WIDTH)
+            if t < 2:
+                nc.scalar.copy(pairs[:, :, 0, :, t], chunked)
+            elif t == 2:
+                nc.scalar.copy(pairs[:, VECTOR_ROUNDS:, 1, :, 0], chunked[:, VECTOR_ROUNDS:, :])
+            else:
+                for k in range(VECTOR_ROUNDS, CHUNKS):
+                    nc.scalar.copy(pairs[:, k, 1, :, 1], chunked[:, k, :])
+        for t in (2, 3):
+            nc.vector.tensor_copy(pairs[:, 0:VECTOR_ROUNDS, 1, :, t - 2], windows[t][:, 0 : VECTOR_ROUNDS * WIDTH].rearrange("p (k c) -> p k c", c=WIDTH))
 
         out_words = out_1[0].rearrange("p c l -> p (c l)").bitcast(I32)
-        out_scales = out_2[0].bitcast(I32)
-        y_scales = sb("y_scales", [P, T], U8)
-        grouped = [sb("grouped%d" % k, [P, w * PACK], BF16) for k, w in enumerate(CHUNKS)]
-        y_codes = [sb("y_codes%d" % k, [P, w], U32) for k, w in enumerate(CHUNKS)]
+        y_scales = sb("y_scales", [P, 2 * WIDTH], U8)
+        grouped = sb("grouped", [P, T * PACK], BF16)
+        y_codes = sb("y_codes", [P, T], U32)
 
-        def interleave(k):
-            src = pairs[k][:].rearrange("p u c e -> p u (c e)").bitcast(F32).rearrange("p u (c i) -> p c u i", i=4)
-            dst = grouped[k][:].bitcast(F32).rearrange("p (c i u) -> p c u i", i=4, u=2)
-            if k < VECTOR_CHUNKS:
-                nc.vector.tensor_copy(dst, src)
+        def weave(first, count):
+            dst = grouped[:, first * WIDTH * PACK : (first + count) * WIDTH * PACK]
+            src = pairs[:, first : first + count]
+            if first < VECTOR_WEAVES:
+                nc.vector.tensor_copy(dst.rearrange("p (k c u e) -> p k c u e", k=count, u=2, e=2), src.rearrange("p k u c e -> p k c u e"))
             else:
-                nc.scalar.copy(dst, src)
+                words = src.rearrange("p k u c e -> p k u (c e)").bitcast(F32).rearrange("p k u c -> p k c u")
+                nc.scalar.copy(dst.bitcast(F32).rearrange("p (k c u) -> p k c u", k=count, u=2), words)
 
-        def quantise(k):
-            cut = slice(starts[k], starts[k] + CHUNKS[k])
-            nc.vector.quantize_mx(out=y_codes[k][:].bitcast(FP8X4), scales=y_scales[:, cut], in_=grouped[k][:])
-            nc.sync.dma_start(out=out_words[:, cut], in_=y_codes[k][:].bitcast(I32))
+        def quantise(first, count):
+            cut = slice(first * WIDTH, (first + count) * WIDTH)
+            half = first % 2
+            nc.vector.quantize_mx(out=y_codes[:, cut].bitcast(FP8X4), scales=y_scales[4 * (first // 2) : P, half * WIDTH : (half + count) * WIDTH],
+                                  in_=grouped[:, first * WIDTH * PACK : (first + count) * WIDTH * PACK])
+            nc.sync.dma_start(out=out_words[:, cut], in_=y_codes[:, cut].bitcast(I32))
 
-        interleave(0)
-        for k in range(len(CHUNKS)):
-            if k + 1 < len(CHUNKS):
-                interleave(k + 1)
-            quantise(k)
+        weave(0, 2)
+        weave(2, 2)
+        quantise(0, 2)
+        weave(4, 1)
+        quantise(2, 2)
+        for k in range(VECTOR_WEAVES, CHUNKS):
+            weave(k, 1)
+        quantise(4, 2)
+        quantise(6, 1)
+        quantise(7, 1)
+        out_scales = out_2[0].bitcast(I32).rearrange("f (g c) -> g f c", g=4)
         for quad in range(4):
             queue = nc.scalar if quad % 2 else nc.sync
-            queue.dma_start(out=out_scales[4 * quad : 4 * quad + 4, :], in_=y_scales[32 * quad : 32 * quad + 4, :].bitcast(I32))
+            queue.dma_start(out=out_scales[:, 4 * quad : 4 * quad + 4, :], in_=y_scales[32 * quad : 32 * quad + 16, :].bitcast(I32))

@@ -16,6 +16,7 @@ U8 = mybir.dt.uint8
 FP8X4 = mybir.dt.float8_e4m3fn_x4
 ALU = mybir.AluOpType
 COPY = mybir.ActivationFunctionType.Copy
+IDENTITY = mybir.ActivationFunctionType.Identity
 
 P = 128
 PACK = 4
@@ -25,6 +26,7 @@ WIDTH = 256
 CHUNKS = T // WIDTH
 VECTOR_ROUNDS = 2
 VECTOR_WEAVES = 5
+EARLY = 1
 
 
 def block(b):
@@ -63,12 +65,15 @@ def tile_attend_gtd_pl_kernel(tc, x2, x, w0, wT, us, ts, rw, wt, offs, aoffs, ou
         nc.sync.dma_start(taken[:], aoffs)
         x2_sb = sb("x2_sb", [P, PACK, R], F32)
         nc.sync.dma_start(out=x2_sb[:], in_=x2.rearrange("(p t) r -> p t r", t=PACK))
-        x_sb = sb("x_sb", [P, BLOCKS, D], F32)
-        nc.sync.dma_start(out=x_sb[:], in_=x.rearrange("(b p) d -> p b d", p=P))
+        x_sb = [sb("x_sb%d" % b, [P, D], F32) for b in range(BLOCKS)]
+        for b in range(EARLY):
+            nc.sync.dma_start(out=x_sb[b][:], in_=x[block(b), :])
         wT_planes = wT.rearrange("(p t) c -> t p c", t=PACK)
         wT_sb = [keep.tile([P, T], F32, name="wT_%d" % t, tag="table%d" % t, align_bytes=64) for t in range(PACK)]
         for t in range(PACK):
             nc.sync.dma_start(out=wT_sb[t][:], in_=wT_planes[t])
+        for b in range(EARLY, BLOCKS):
+            nc.sync.dma_start(out=x_sb[b][:], in_=x[block(b), :])
 
         ident = sb("ident", [P, P], F32)
         make_identity(nc, ident[:])
@@ -77,16 +82,26 @@ def tile_attend_gtd_pl_kernel(tc, x2, x, w0, wT, us, ts, rw, wt, offs, aoffs, ou
         ts_all = sb("ts_all", [P, T], F32)
         ts_view = ts_all[:].rearrange("q (p g m) -> q p g m", g=4, m=4)
         for g in range(4):
-            ts_bank = bank("q%d" % g, "ts_bank%d" % g)
+            ts_bank = bank("b%d" % g, "ts_bank%d" % g)
             for m in range(4):
                 col = 4 * g + m
                 nc.tensor.transpose(ts_bank[:, block(m)], ts_cut[:, col : col + 1].to_broadcast([P, P]), ident[:])
             nc.scalar.activation(ts_view[:, :, g, :], ts_bank[:].rearrange("q (m p) -> q p m", m=4), COPY)
 
-        vec_bank = bank("a0", "vec_bank")
+        vec_bank = bank("b4", "vec_bank")
         nc.tensor.transpose(vec_bank[:, 0:P], vecs[:], ident[:])
         cols = sb("cols", [P, 12], F32)
         nc.scalar.activation(cols[:], vec_bank[:, 0:12], COPY)
+        xT = [sb("xT%d" % t, [P, R], F32) for t in range(PACK)]
+        wt_bank = bank("b5", "wt_bank")
+        for b in range(EARLY, BLOCKS):
+            nc.tensor.transpose(wt_bank[:, block(b)], cols[:, 8 + b : 9 + b].to_broadcast([P, P]), ident[:])
+        for t in range(PACK):
+            nc.scalar.copy(xT[t][:, EARLY * P : R], wt_bank[:, EARLY * P : R])
+        slope = sb("slope", [P, BLOCKS], F32)
+        nc.vector.tensor_scalar(out=slope[:], in0=cols[:, 8:12], scalar1=-0.9, scalar2=None, op0=ALU.mult)
+        base = sb("base", [P, BLOCKS], F32)
+        nc.vector.scalar_tensor_tensor(out=base[:], in0=cols[:, 4:8], scalar=-1.0, in1=cols[:, 8:12], op0=ALU.mult, op1=ALU.mult)
 
         w0_bf = sb("w0_bf", [P, I, PACK], BF16)
         ts_listed = sb("ts_listed", [P, I], F32)
@@ -98,14 +113,14 @@ def tile_attend_gtd_pl_kernel(tc, x2, x, w0, wT, us, ts, rw, wt, offs, aoffs, ou
         w0_scales = sb("w0_scales", [P, I], U8)
         nc.vector.quantize_mx(out=w0_codes[:].bitcast(FP8X4), scales=w0_scales[:], in_=w0_bf[:].rearrange("p i t -> p (i t)"))
 
-        tscol_bank = bank("a1", "tscol_bank")
+        tscol_bank = bank("b4", "tscol_bank")
         for j in range(BLOCKS):
             nc.tensor.transpose(tscol_bank[:, block(j)], ts_listed[:, block(j)], ident[:])
         ts_col = sb("ts_col", [P, BLOCKS], F32)
         nc.scalar.activation(ts_col[:], tscol_bank[:].rearrange("p (j q) -> p j q", j=BLOCKS)[:, :, 0], COPY)
 
-        x2_codes = [sb("x2_codes%d" % h, [P, HALF], U32) for h in range(2)]
-        x2_scales = [sb("x2_scales%d" % h, [P, HALF], U8) for h in range(2)]
+        x2_codes = sb("x2_codes", [P, R], U32)
+        x2_scales = sb("x2_scales", [P, R], U8)
         x2_bf = [sb("x2_bf%d" % h, [P, HALF, PACK], BF16) for h in range(2)]
         for h in range(2):
             src = x2_sb[:, :, HALF * h : HALF * (h + 1)].rearrange("p t (c i) -> p c t i", i=4)
@@ -115,27 +130,18 @@ def tile_attend_gtd_pl_kernel(tc, x2, x, w0, wT, us, ts, rw, wt, offs, aoffs, ou
             else:
                 nc.scalar.copy(dst, src)
         for h in range(2):
-            nc.vector.quantize_mx(out=x2_codes[h][:].bitcast(FP8X4), scales=x2_scales[h][:], in_=x2_bf[h][:].rearrange("p r t -> p (r t)"))
+            cut = slice(HALF * h, HALF * (h + 1))
+            nc.vector.quantize_mx(out=x2_codes[:, cut].bitcast(FP8X4), scales=x2_scales[:, cut], in_=x2_bf[h][:].rearrange("p r t -> p (r t)"))
 
-        xT = [sb("xT%d" % t, [P, R], F32) for t in range(PACK)]
-
-        def turn_x(t):
-            xt_bank = bank("c%d" % (t % 2), "xt_bank%d" % t)
-            for b in range(BLOCKS):
-                nc.tensor.transpose(xt_bank[:, block(b)], x_sb[:, b, :].rearrange("r (p t) -> r t p", t=PACK)[:, t, :], ident[:])
-            nc.scalar.copy(xT[t][:], xt_bank[:])
-
-        terms = [sb("terms%d" % t, [P, R], F32) for t in range(PACK)]
-        q_banks = [bank("q%d" % b, "q_bank%d" % b) for b in range(BLOCKS)]
-
-        def turn_terms(t, blocks):
+        def turn_x(t, blocks, tag):
+            xt_bank = bank(tag, "xt_bank%d_%d" % (t, blocks[0]))
             for b in blocks:
-                nc.tensor.matmul(q_banks[b][:, 0:P], lhsT=terms[t][:, block(b)], rhs=ident[:], is_transpose=True, start=(t == 0), stop=(t == PACK - 1))
+                nc.tensor.transpose(xt_bank[:, block(b)], x_sb[b][:].rearrange("r (p t) -> r t p", t=PACK)[:, t, :], ident[:])
+            cut = slice(P * blocks[0], P * (blocks[-1] + 1))
+            nc.scalar.copy(xT[t][:, cut], xt_bank[:, cut])
 
-        def look_up_taken(t):
-            nc.vector.tensor_tensor(terms[t][:], wT_sb[t][:].indirect(taken[:]), xT[t][:], ALU.mult)
-            turn_terms(t, range(BLOCKS))
-
+        early = tuple(range(EARLY))
+        late = tuple(range(EARLY, BLOCKS))
         largest = sb("largest", [P, BLOCKS], F32)
 
         def row_maximum(b, scores):
@@ -143,61 +149,79 @@ def tile_attend_gtd_pl_kernel(tc, x2, x, w0, wT, us, ts, rw, wt, offs, aoffs, ou
             nc.vector.tensor_scalar(out=z[:], in0=scores, scalar1=cols[:, b : b + 1], scalar2=None, op0=ALU.mult, op1=ALU.max,
                                     accum_out=largest[:, b : b + 1])
 
-        row_banks = [bank("a%d" % b, "row_bank%d" % b) for b in range(2)]
+        row_banks = [bank("b%d" % (4 + b), "row_bank%d" % b) for b in range(2)]
         for b in range(2):
-            nc.tensor.matmul_mx(out=row_banks[b][:], lhsT=x2_codes[0][:, block(b)].bitcast(FP8X4), lhsT_scale=x2_scales[0][:, block(b)],
+            nc.tensor.matmul_mx(out=row_banks[b][:], lhsT=x2_codes[:, block(b)].bitcast(FP8X4), lhsT_scale=x2_scales[:, block(b)],
                                 rhs=w0_codes[:].bitcast(FP8X4), rhs_scale=w0_scales[:], start=True, stop=True)
-        turn_x(0)
+        turn_x(0, early, "b6")
         scaled_rows = [sb("scaled_rows%d" % b, [P, I], F32) for b in range(2)]
         for b in range(2):
             nc.vector.tensor_tensor(scaled_rows[b][:], row_banks[b][:], ts_listed[:], ALU.mult)
         for b in range(2):
             row_maximum(b, scaled_rows[b][:])
-
         scaled_slots = [sb("scaled_slots%d" % j, [P, HALF], F32) for j in range(BLOCKS)]
         for j in range(BLOCKS):
-            slot_bank = bank("q%d" % j, "slot_bank%d" % j)
+            slot_bank = bank("b%d" % j, "slot_bank%d" % j)
             nc.tensor.matmul_mx(out=slot_bank[:, 0:HALF], lhsT=w0_codes[:, block(j)].bitcast(FP8X4), lhsT_scale=w0_scales[:, block(j)],
-                                rhs=x2_codes[1][:].bitcast(FP8X4), rhs_scale=x2_scales[1][:], start=True, stop=True)
+                                rhs=x2_codes[:, HALF:R].bitcast(FP8X4), rhs_scale=x2_scales[:, HALF:R], start=True, stop=True)
             nc.scalar.activation(scaled_slots[j][:], slot_bank[:, 0:HALF], COPY, scale=ts_col[:, j : j + 1])
-        z_banks = [bank("a%d" % k, "z_bank%d" % k) for k in range(2)]
+        turn_x(1, early, "b7")
+        z_banks = [bank("b%d" % (4 + k), "z_bank%d" % k) for k in range(2)]
         for k in range(2):
             for j in range(BLOCKS):
                 nc.tensor.transpose(z_banks[k][:, block(j)], scaled_slots[j][:, block(k)], ident[:])
-        turn_x(1)
-        look_up_taken(0)
+
+        terms = [sb("terms%d" % t, [P, R], F32) for t in range(PACK)]
+        q_banks = [bank("b%d" % b, "q_bank%d" % b) for b in range(BLOCKS)]
+
+        def look_up(t, blocks):
+            cut = slice(P * blocks[0], P * (blocks[-1] + 1))
+            nc.vector.tensor_tensor(terms[t][:, cut], wT_sb[t][:].indirect(taken[:, 8 * blocks[0] : 8 * (blocks[-1] + 1)]), xT[t][:, cut], ALU.mult)
+            for b in blocks:
+                if b < EARLY:
+                    nc.tensor.matmul(q_banks[b][:, 0:P], lhsT=terms[t][:, block(b)], rhs=ident[:], is_transpose=True, start=(t == 0), stop=(t == PACK - 1))
+                else:
+                    nc.tensor.transpose(q_banks[b][:, block(t)], terms[t][:, block(b)], ident[:])
+
+        turn_x(2, early, "b6")
+        turn_x(3, early, "b7")
+        look_up(0, range(BLOCKS))
+        look_up(1, range(BLOCKS))
         for k in range(2):
             row_maximum(2 + k, z_banks[k][:])
-        turn_x(2)
-        look_up_taken(1)
-        turn_x(3)
-        target = sb("target", [P, BLOCKS], F32)
-        nc.vector.scalar_tensor_tensor(out=target[:], in0=largest[:], scalar=-0.9, in1=cols[:, 4:8], op0=ALU.mult, op1=ALU.subtract)
-        look_up_taken(2)
-        wtarget = sb("wtarget", [P, BLOCKS], F32)
-        nc.vector.tensor_tensor(wtarget[:], target[:], cols[:, 8:12], ALU.mult)
-        last = PACK - 1
-        for h in range(2):
-            cut = slice(HALF * h, HALF * (h + 1))
-            nc.vector.tensor_tensor(terms[last][:, cut], wT_sb[last][:].indirect(taken[:, 16 * h : 16 * (h + 1)]), xT[last][:, cut], ALU.mult)
-            turn_terms(last, (2 * h, 2 * h + 1))
+        wtarget = [sb("wtarget%d" % b, [P, 1], F32) for b in range(BLOCKS)]
+        for b in range(BLOCKS):
+            nc.scalar.activation(wtarget[b][:], largest[:, b : b + 1], IDENTITY, scale=slope[:, b : b + 1], bias=base[:, b : b + 1])
+        look_up(2, range(BLOCKS))
+        look_up(3, (0, 1))
+        look_up(3, (2, 3))
 
-        wq = [sb("wq%d" % h, [P, 2], F32) for h in range(2)]
+        wq = [sb("wq%d" % b, [P, 1], F32) for b in range(BLOCKS)]
         err = sb("err", [P, R], F32)
-        for h in range(2):
-            cut = slice(HALF * h, HALF * (h + 1))
-            e_bank = bank("a%d" % h, "e_bank%d" % h)
-            for k in range(2):
-                b = 2 * h + k
-                summed = spare.tile([P, P], F32, name="summed", tag="summed")
-                if h == 0:
-                    nc.scalar.activation(summed[:], q_banks[b][:, 0:P], COPY, scale=cols[:, 8 + b : 9 + b], accum_out=wq[h][:, k : k + 1])
-                else:
-                    nc.vector.tensor_scalar(out=summed[:], in0=q_banks[b][:, 0:P], scalar1=cols[:, 8 + b : 9 + b], scalar2=None, op0=ALU.mult, op1=ALU.add,
-                                            accum_out=wq[h][:, k : k + 1])
-                nc.tensor.matmul(e_bank[:, block(b)], lhsT=wtarget[:, b : b + 1].to_broadcast([P, P]), rhs=ident[:], is_transpose=True, start=True, stop=False)
-                nc.tensor.matmul(e_bank[:, block(b)], lhsT=wq[h][:, k : k + 1].to_broadcast([P, P]), rhs=ident[:], is_transpose=True, start=False, stop=True)
-            nc.scalar.copy(err[:, cut], e_bank[:, cut])
+        e_banks = [bank("b%d" % (4 + h), "e_bank%d" % h) for h in range(2)]
+
+        def sum_q(b):
+            products = spare.tile([P, D], F32, name="unread", tag="unread")
+            if b < EARLY:
+                nc.scalar.activation(products[:, 0:P], q_banks[b][:, 0:P], COPY, scale=cols[:, 8 + b : 9 + b], accum_out=wq[b][:])
+            else:
+                nc.vector.scalar_tensor_tensor(out=products[:].rearrange("r (p t) -> r p t", t=PACK), in0=q_banks[b][:].rearrange("r (t p) -> r p t", t=PACK),
+                                               scalar=1.0, in1=x_sb[b][:].rearrange("r (p t) -> r p t", t=PACK), op0=ALU.mult, op1=ALU.mult, accum_out=wq[b][:])
+            out = e_banks[b // 2][:, block(b % 2)]
+            nc.tensor.matmul(out, lhsT=wtarget[b][:].to_broadcast([P, P]), rhs=ident[:], is_transpose=True, start=True, stop=False)
+            nc.tensor.matmul(out, lhsT=wq[b][:].to_broadcast([P, P]), rhs=ident[:], is_transpose=True, start=False, stop=True)
+
+        sum_q(0)
+        turn_x(0, (1,), "b6")
+        sum_q(1)
+        nc.scalar.copy(err[:, 0:HALF], e_banks[0][:, 0:HALF])
+        sum_q(2)
+        turn_x(0, (2, 3), "b2")
+        sum_q(3)
+        nc.scalar.copy(err[:, HALF:R], e_banks[1][:, 0:HALF])
+        turn_x(1, late, "b1")
+        turn_x(2, late, "b3")
+        turn_x(3, late, "b4")
 
         windows = [keep.tile([P, T], F32, name="window_%d" % t, tag="table%d" % t, align_bytes=64) for t in range(PACK)]
         for t in range(PACK):

@@ -24,9 +24,9 @@ BLOCKS = 4
 HALF = R // 2
 WIDTH = 256
 CHUNKS = T // WIDTH
-VECTOR_ROUNDS = 2
-VECTOR_WEAVES = 5
-EARLY = 1
+VECTOR_ROUNDS = 1
+VECTOR_WEAVES = 6
+EARLY = 2
 
 
 def block(b):
@@ -66,12 +66,13 @@ def tile_attend_gtd_pl_kernel(tc, x2, x, w0, wT, us, ts, rw, wt, offs, aoffs, ou
         x2_sb = sb("x2_sb", [P, PACK, R], F32)
         nc.sync.dma_start(out=x2_sb[:], in_=x2.rearrange("(p t) r -> p t r", t=PACK))
         x_sb = [sb("x_sb%d" % b, [P, D], F32) for b in range(BLOCKS)]
-        for b in range(EARLY):
-            nc.sync.dma_start(out=x_sb[b][:], in_=x[block(b), :])
         wT_planes = wT.rearrange("(p t) c -> t p c", t=PACK)
         wT_sb = [keep.tile([P, T], F32, name="wT_%d" % t, tag="table%d" % t, align_bytes=64) for t in range(PACK)]
         for t in range(PACK):
             nc.sync.dma_start(out=wT_sb[t][:], in_=wT_planes[t])
+            if t == 0:
+                for b in range(EARLY):
+                    nc.sync.dma_start(out=x_sb[b][:], in_=x[block(b), :])
         for b in range(EARLY, BLOCKS):
             nc.sync.dma_start(out=x_sb[b][:], in_=x[block(b), :])
 
@@ -154,11 +155,10 @@ def tile_attend_gtd_pl_kernel(tc, x2, x, w0, wT, us, ts, rw, wt, offs, aoffs, ou
             nc.tensor.matmul_mx(out=row_banks[b][:], lhsT=x2_codes[:, block(b)].bitcast(FP8X4), lhsT_scale=x2_scales[:, block(b)],
                                 rhs=w0_codes[:].bitcast(FP8X4), rhs_scale=w0_scales[:], start=True, stop=True)
         turn_x(0, early, "b6")
-        scaled_rows = [sb("scaled_rows%d" % b, [P, I], F32) for b in range(2)]
+        scaled_rows = sb("scaled_rows", [P, 2, I], F32)
         for b in range(2):
-            nc.vector.tensor_tensor(scaled_rows[b][:], row_banks[b][:], ts_listed[:], ALU.mult)
-        for b in range(2):
-            row_maximum(b, scaled_rows[b][:])
+            nc.vector.scalar_tensor_tensor(out=scaled_rows[:, b, :], in0=row_banks[b][:], scalar=cols[:, b : b + 1], in1=ts_listed[:], op0=ALU.mult, op1=ALU.mult)
+        nc.vector.tensor_reduce(out=largest[:, 0:2], in_=scaled_rows[:], axis=mybir.AxisListType.X, op=ALU.max)
         scaled_slots = [sb("scaled_slots%d" % j, [P, HALF], F32) for j in range(BLOCKS)]
         for j in range(BLOCKS):
             slot_bank = bank("b%d" % j, "slot_bank%d" % j)
@@ -185,7 +185,8 @@ def tile_attend_gtd_pl_kernel(tc, x2, x, w0, wT, us, ts, rw, wt, offs, aoffs, ou
 
         turn_x(2, early, "b6")
         turn_x(3, early, "b7")
-        look_up(0, range(BLOCKS))
+        look_up(0, late)
+        look_up(0, early)
         look_up(1, range(BLOCKS))
         for k in range(2):
             row_maximum(2 + k, z_banks[k][:])
@@ -194,7 +195,8 @@ def tile_attend_gtd_pl_kernel(tc, x2, x, w0, wT, us, ts, rw, wt, offs, aoffs, ou
             nc.scalar.activation(wtarget[b][:], largest[:, b : b + 1], IDENTITY, scale=slope[:, b : b + 1], bias=base[:, b : b + 1])
         look_up(2, range(BLOCKS))
         look_up(3, (0, 1))
-        look_up(3, (2, 3))
+        look_up(3, (2,))
+        look_up(3, (3,))
 
         wq = [sb("wq%d" % b, [P, 1], F32) for b in range(BLOCKS)]
         err = sb("err", [P, R], F32)
@@ -212,7 +214,6 @@ def tile_attend_gtd_pl_kernel(tc, x2, x, w0, wT, us, ts, rw, wt, offs, aoffs, ou
             nc.tensor.matmul(out, lhsT=wq[b][:].to_broadcast([P, P]), rhs=ident[:], is_transpose=True, start=False, stop=True)
 
         sum_q(0)
-        turn_x(0, (1,), "b6")
         sum_q(1)
         nc.scalar.copy(err[:, 0:HALF], e_banks[0][:, 0:HALF])
         sum_q(2)
@@ -271,7 +272,7 @@ def tile_attend_gtd_pl_kernel(tc, x2, x, w0, wT, us, ts, rw, wt, offs, aoffs, ou
         weave(0, 2)
         weave(2, 2)
         quantise(0, 2)
-        weave(4, 1)
+        weave(4, 2)
         quantise(2, 2)
         for k in range(VECTOR_WEAVES, CHUNKS):
             weave(k, 1)

@@ -193,6 +193,9 @@ def tile_attend_gtd_pl_kernel(tc, x2, x, w0, wT, us, ts, rw, wt, offs, aoffs, ou
         wtarget = [sb("wtarget%d" % b, [P, 1], F32) for b in range(BLOCKS)]
         for b in range(BLOCKS):
             nc.scalar.activation(wtarget[b][:], largest[:, b : b + 1], IDENTITY, scale=slope[:, b : b + 1], bias=base[:, b : b + 1])
+        share = [sb("share%d" % b, [P, 1], F32) for b in early]
+        for b in early:
+            nc.scalar.activation(share[b][:], wtarget[b][:], COPY, scale=1.0 / P)
         look_up(2, range(BLOCKS))
         look_up(3, (0, 1))
         look_up(3, (2,))
@@ -205,13 +208,14 @@ def tile_attend_gtd_pl_kernel(tc, x2, x, w0, wT, us, ts, rw, wt, offs, aoffs, ou
         def sum_q(b):
             products = spare.tile([P, D], F32, name="unread", tag="unread")
             if b < EARLY:
-                nc.scalar.activation(products[:, 0:P], q_banks[b][:, 0:P], COPY, scale=cols[:, 8 + b : 9 + b], accum_out=wq[b][:])
+                nc.scalar.activation(products[:, 0:P], q_banks[b][:, 0:P], IDENTITY, scale=cols[:, 8 + b : 9 + b], bias=share[b][:], accum_out=wq[b][:])
             else:
                 nc.vector.scalar_tensor_tensor(out=products[:].rearrange("r (p t) -> r p t", t=PACK), in0=q_banks[b][:].rearrange("r (t p) -> r p t", t=PACK),
                                                scalar=1.0, in1=x_sb[b][:].rearrange("r (p t) -> r p t", t=PACK), op0=ALU.mult, op1=ALU.mult, accum_out=wq[b][:])
             out = e_banks[b // 2][:, block(b % 2)]
-            nc.tensor.matmul(out, lhsT=wtarget[b][:].to_broadcast([P, P]), rhs=ident[:], is_transpose=True, start=True, stop=False)
-            nc.tensor.matmul(out, lhsT=wq[b][:].to_broadcast([P, P]), rhs=ident[:], is_transpose=True, start=False, stop=True)
+            if b >= EARLY:
+                nc.tensor.matmul(out, lhsT=wtarget[b][:].to_broadcast([P, P]), rhs=ident[:], is_transpose=True, start=True, stop=False)
+            nc.tensor.matmul(out, lhsT=wq[b][:].to_broadcast([P, P]), rhs=ident[:], is_transpose=True, start=(b < EARLY), stop=True)
 
         sum_q(0)
         sum_q(1)
@@ -220,9 +224,9 @@ def tile_attend_gtd_pl_kernel(tc, x2, x, w0, wT, us, ts, rw, wt, offs, aoffs, ou
         turn_x(0, (2, 3), "b2")
         sum_q(3)
         nc.scalar.copy(err[:, HALF:R], e_banks[1][:, 0:HALF])
-        turn_x(1, late, "b1")
+        turn_x(1, late, "b4")
         turn_x(2, late, "b3")
-        turn_x(3, late, "b4")
+        turn_x(3, late, "b2")
 
         windows = [keep.tile([P, T], F32, name="window_%d" % t, tag="table%d" % t, align_bytes=64) for t in range(PACK)]
         for t in range(PACK):
@@ -249,7 +253,7 @@ def tile_attend_gtd_pl_kernel(tc, x2, x, w0, wT, us, ts, rw, wt, offs, aoffs, ou
             nc.vector.tensor_copy(pairs[:, 0:VECTOR_ROUNDS, 1, :, t - 2], windows[t][:, 0 : VECTOR_ROUNDS * WIDTH].rearrange("p (k c) -> p k c", c=WIDTH))
 
         out_words = out_1[0].rearrange("p c l -> p (c l)").bitcast(I32)
-        y_scales = sb("y_scales", [P, 2 * WIDTH], U8)
+        y_scales = sb("y_scales", [P, T // 2], U8)
         grouped = sb("grouped", [P, T * PACK], BF16)
         y_codes = sb("y_codes", [P, T], U32)
 
@@ -264,8 +268,8 @@ def tile_attend_gtd_pl_kernel(tc, x2, x, w0, wT, us, ts, rw, wt, offs, aoffs, ou
 
         def quantise(first, count):
             cut = slice(first * WIDTH, (first + count) * WIDTH)
-            half = first % 2
-            nc.vector.quantize_mx(out=y_codes[:, cut].bitcast(FP8X4), scales=y_scales[4 * (first // 2) : P, half * WIDTH : (half + count) * WIDTH],
+            place = first % 4
+            nc.vector.quantize_mx(out=y_codes[:, cut].bitcast(FP8X4), scales=y_scales[4 * (first // 4) : P, place * WIDTH : (place + count) * WIDTH],
                                   in_=grouped[:, first * WIDTH * PACK : (first + count) * WIDTH * PACK])
             nc.sync.dma_start(out=out_words[:, cut], in_=y_codes[:, cut].bitcast(I32))
 
@@ -279,7 +283,7 @@ def tile_attend_gtd_pl_kernel(tc, x2, x, w0, wT, us, ts, rw, wt, offs, aoffs, ou
         quantise(4, 2)
         quantise(6, 1)
         quantise(7, 1)
-        out_scales = out_2[0].bitcast(I32).rearrange("f (g c) -> g f c", g=4)
+        out_scales = out_2[0].bitcast(I32).rearrange("f (g c) -> g f c", g=2)
         for quad in range(4):
             queue = nc.scalar if quad % 2 else nc.sync
-            queue.dma_start(out=out_scales[:, 4 * quad : 4 * quad + 4, :], in_=y_scales[32 * quad : 32 * quad + 16, :].bitcast(I32))
+            queue.dma_start(out=out_scales[:, 4 * quad : 4 * quad + 4, :], in_=y_scales[32 * quad : 32 * quad + 8, :].bitcast(I32))

@@ -22,15 +22,25 @@ P = 128
 PACK = 4
 BLOCKS = 4
 HALF = R // 2
-WIDTH = 256
-CHUNKS = T // WIDTH
-VECTOR_ROUNDS = 1
-VECTOR_WEAVES = 6
+LIST_COLUMNS = P // 16
+DISCOUNT = 0.9
 EARLY = 2
+EARLY_BLOCKS = tuple(range(EARLY))
+LATE_BLOCKS = tuple(range(EARLY, BLOCKS))
+WIDTH = 128
+CHUNKS = T // WIDTH
+VECTOR_ROUNDS = 2
+VECTOR_WEAVES = 10
+SCALE_CHUNKS = CHUNKS // 2
+US, RW, WT = 0, BLOCKS, 2 * BLOCKS
 
 
 def block(b):
     return slice(P * b, P * (b + 1))
+
+
+def span(blocks):
+    return slice(P * blocks[0], P * (blocks[-1] + 1))
 
 
 def tile_attend_gtd_pl_kernel(tc, x2, x, w0, wT, us, ts, rw, wt, offs, aoffs, out_0, out_1, out_2):
@@ -38,30 +48,30 @@ def tile_attend_gtd_pl_kernel(tc, x2, x, w0, wT, us, ts, rw, wt, offs, aoffs, ou
     with ExitStack() as ctx:
         lists = ctx.enter_context(tc.tile_pool(name="lists", bufs=1))
         keep = ctx.enter_context(tc.tile_pool(name="keep", bufs=1))
-        spare = ctx.enter_context(tc.tile_pool(name="spare", bufs=4))
+        spare = ctx.enter_context(tc.tile_pool(name="spare", bufs=BLOCKS))
         psum = ctx.enter_context(tc.psum_pool(name="psum", bufs=1))
 
         def sb(name, shape, dtype):
             return keep.tile(shape, dtype, name=name, align_bytes=64)
 
-        def bank(tag, name):
-            return psum.tile([P, 512], F32, name=name, tag=tag)
+        def bank(number, name):
+            return psum.tile([P, 512], F32, name=name, tag="b%d" % number)
 
         slots = lists.tile([P, I // 16], U16, name="slots")
         taken = lists.tile([P, R // 16], U16, name="taken")
         vecs = sb("vecs", [P, P], F32)
         nc.vector.memset(vecs[:], 0.0)
-        ts_cut = sb("ts_cut", [P, 16], F32)
+        ts_cut = sb("ts_cut", [P, T // P], F32)
 
         w0_planes = w0.rearrange("(p t) c -> t p c", t=PACK)
         w0_sb = [sb("w0_%d" % t, [P, T], F32) for t in range(PACK)]
         for t in range(PACK):
             nc.sync.dma_start(out=w0_sb[t][:], in_=w0_planes[t])
             if t == 0:
-                nc.sync.dma_start(out=ts_cut[:], in_=ts[0].rearrange("(p m) -> p m", m=16))
+                nc.sync.dma_start(out=ts_cut[:], in_=ts[0].rearrange("(p m) -> p m", m=T // P))
                 nc.sync.dma_start(slots[:], offs)
-                for k, v in enumerate((us, rw, wt)):
-                    nc.sync.dma_start(out=vecs[4 * k : 4 * k + 4, :], in_=v.rearrange("(b p) o -> b (p o)", p=P))
+                for first, vec in ((US, us), (RW, rw), (WT, wt)):
+                    nc.sync.dma_start(out=vecs[first : first + BLOCKS, :], in_=vec.rearrange("(b p) o -> b (p o)", p=P))
         nc.sync.dma_start(taken[:], aoffs)
         x2_sb = sb("x2_sb", [P, PACK, R], F32)
         nc.sync.dma_start(out=x2_sb[:], in_=x2.rearrange("(p t) r -> p t r", t=PACK))
@@ -71,38 +81,39 @@ def tile_attend_gtd_pl_kernel(tc, x2, x, w0, wT, us, ts, rw, wt, offs, aoffs, ou
         for t in range(PACK):
             nc.sync.dma_start(out=wT_sb[t][:], in_=wT_planes[t])
             if t == 0:
-                for b in range(EARLY):
+                for b in EARLY_BLOCKS:
                     nc.sync.dma_start(out=x_sb[b][:], in_=x[block(b), :])
-        for b in range(EARLY, BLOCKS):
+        for b in LATE_BLOCKS:
             nc.sync.dma_start(out=x_sb[b][:], in_=x[block(b), :])
 
         ident = sb("ident", [P, P], F32)
         make_identity(nc, ident[:])
 
-
         ts_all = sb("ts_all", [P, T], F32)
         ts_view = ts_all[:].rearrange("q (p g m) -> q p g m", g=4, m=4)
         for g in range(4):
-            ts_bank = bank("b%d" % g, "ts_bank%d" % g)
+            ts_bank = bank(g, "ts_bank%d" % g)
             for m in range(4):
                 col = 4 * g + m
                 nc.tensor.transpose(ts_bank[:, block(m)], ts_cut[:, col : col + 1].to_broadcast([P, P]), ident[:])
             nc.scalar.activation(ts_view[:, :, g, :], ts_bank[:].rearrange("q (m p) -> q p m", m=4), COPY)
 
-        vec_bank = bank("b4", "vec_bank")
+        vec_bank = bank(4, "vec_bank")
         nc.tensor.transpose(vec_bank[:, 0:P], vecs[:], ident[:])
-        cols = sb("cols", [P, 12], F32)
-        nc.scalar.activation(cols[:], vec_bank[:, 0:12], COPY)
+        cols = sb("cols", [P, 3 * BLOCKS], F32)
+        nc.scalar.activation(cols[:], vec_bank[:, 0 : 3 * BLOCKS], COPY)
+
         xT = [sb("xT%d" % t, [P, R], F32) for t in range(PACK)]
-        wt_bank = bank("b5", "wt_bank")
-        for b in range(EARLY, BLOCKS):
-            nc.tensor.transpose(wt_bank[:, block(b)], cols[:, 8 + b : 9 + b].to_broadcast([P, P]), ident[:])
+        wt_bank = bank(5, "wt_bank")
+        for b in LATE_BLOCKS:
+            nc.tensor.transpose(wt_bank[:, block(b)], cols[:, WT + b : WT + b + 1].to_broadcast([P, P]), ident[:])
         for t in range(PACK):
-            nc.scalar.copy(xT[t][:, EARLY * P : R], wt_bank[:, EARLY * P : R])
+            nc.scalar.copy(xT[t][:, span(LATE_BLOCKS)], wt_bank[:, span(LATE_BLOCKS)])
         slope = sb("slope", [P, BLOCKS], F32)
-        nc.vector.tensor_scalar(out=slope[:], in0=cols[:, 8:12], scalar1=-0.9, scalar2=None, op0=ALU.mult)
+        nc.vector.tensor_scalar(out=slope[:], in0=cols[:, WT : WT + BLOCKS], scalar1=-DISCOUNT, scalar2=None, op0=ALU.mult)
         base = sb("base", [P, BLOCKS], F32)
-        nc.vector.scalar_tensor_tensor(out=base[:], in0=cols[:, 4:8], scalar=-1.0, in1=cols[:, 8:12], op0=ALU.mult, op1=ALU.mult)
+        nc.vector.scalar_tensor_tensor(out=base[:], in0=cols[:, RW : RW + BLOCKS], scalar=-1.0, in1=cols[:, WT : WT + BLOCKS],
+                                       op0=ALU.mult, op1=ALU.mult)
 
         w0_bf = sb("w0_bf", [P, I, PACK], BF16)
         ts_listed = sb("ts_listed", [P, I], F32)
@@ -114,7 +125,7 @@ def tile_attend_gtd_pl_kernel(tc, x2, x, w0, wT, us, ts, rw, wt, offs, aoffs, ou
         w0_scales = sb("w0_scales", [P, I], U8)
         nc.vector.quantize_mx(out=w0_codes[:].bitcast(FP8X4), scales=w0_scales[:], in_=w0_bf[:].rearrange("p i t -> p (i t)"))
 
-        tscol_bank = bank("b4", "tscol_bank")
+        tscol_bank = bank(4, "tscol_bank")
         for j in range(BLOCKS):
             nc.tensor.transpose(tscol_bank[:, block(j)], ts_listed[:, block(j)], ident[:])
         ts_col = sb("ts_col", [P, BLOCKS], F32)
@@ -123,110 +134,104 @@ def tile_attend_gtd_pl_kernel(tc, x2, x, w0, wT, us, ts, rw, wt, offs, aoffs, ou
         x2_codes = sb("x2_codes", [P, R], U32)
         x2_scales = sb("x2_scales", [P, R], U8)
         x2_bf = [sb("x2_bf%d" % h, [P, HALF, PACK], BF16) for h in range(2)]
-        for h in range(2):
+        for h, copy in enumerate((nc.vector.tensor_copy, nc.scalar.copy)):
             src = x2_sb[:, :, HALF * h : HALF * (h + 1)].rearrange("p t (c i) -> p c t i", i=4)
-            dst = x2_bf[h][:].rearrange("p (c i) t -> p c t i", i=4)
-            if h == 0:
-                nc.vector.tensor_copy(dst, src)
-            else:
-                nc.scalar.copy(dst, src)
+            copy(x2_bf[h][:].rearrange("p (c i) t -> p c t i", i=4), src)
         for h in range(2):
             cut = slice(HALF * h, HALF * (h + 1))
             nc.vector.quantize_mx(out=x2_codes[:, cut].bitcast(FP8X4), scales=x2_scales[:, cut], in_=x2_bf[h][:].rearrange("p r t -> p (r t)"))
 
-        def turn_x(t, blocks, tag):
-            xt_bank = bank(tag, "xt_bank%d_%d" % (t, blocks[0]))
+        def turn_x(t, blocks, number):
+            xt_bank = bank(number, "xt_bank%d_%d" % (t, blocks[0]))
             for b in blocks:
                 nc.tensor.transpose(xt_bank[:, block(b)], x_sb[b][:].rearrange("r (p t) -> r t p", t=PACK)[:, t, :], ident[:])
-            cut = slice(P * blocks[0], P * (blocks[-1] + 1))
-            nc.scalar.copy(xT[t][:, cut], xt_bank[:, cut])
+            nc.scalar.copy(xT[t][:, span(blocks)], xt_bank[:, span(blocks)])
 
-        early = tuple(range(EARLY))
-        late = tuple(range(EARLY, BLOCKS))
         largest = sb("largest", [P, BLOCKS], F32)
-
-        def row_maximum(b, scores):
-            z = spare.tile([P, I], F32, name="unread", tag="unread")
-            nc.vector.tensor_scalar(out=z[:], in0=scores, scalar1=cols[:, b : b + 1], scalar2=None, op0=ALU.mult, op1=ALU.max,
-                                    accum_out=largest[:, b : b + 1])
-
-        row_banks = [bank("b%d" % (4 + b), "row_bank%d" % b) for b in range(2)]
+        row_banks = [bank(4 + b, "row_bank%d" % b) for b in range(2)]
         for b in range(2):
             nc.tensor.matmul_mx(out=row_banks[b][:], lhsT=x2_codes[:, block(b)].bitcast(FP8X4), lhsT_scale=x2_scales[:, block(b)],
                                 rhs=w0_codes[:].bitcast(FP8X4), rhs_scale=w0_scales[:], start=True, stop=True)
-        turn_x(0, early, "b6")
+        turn_x(0, EARLY_BLOCKS, 6)
         scaled_rows = sb("scaled_rows", [P, 2, I], F32)
         for b in range(2):
-            nc.vector.scalar_tensor_tensor(out=scaled_rows[:, b, :], in0=row_banks[b][:], scalar=cols[:, b : b + 1], in1=ts_listed[:], op0=ALU.mult, op1=ALU.mult)
+            nc.vector.scalar_tensor_tensor(out=scaled_rows[:, b, :], in0=row_banks[b][:], scalar=cols[:, US + b : US + b + 1],
+                                           in1=ts_listed[:], op0=ALU.mult, op1=ALU.mult)
         nc.vector.tensor_reduce(out=largest[:, 0:2], in_=scaled_rows[:], axis=mybir.AxisListType.X, op=ALU.max)
         scaled_slots = [sb("scaled_slots%d" % j, [P, HALF], F32) for j in range(BLOCKS)]
         for j in range(BLOCKS):
-            slot_bank = bank("b%d" % j, "slot_bank%d" % j)
+            slot_bank = bank(j, "slot_bank%d" % j)
             nc.tensor.matmul_mx(out=slot_bank[:, 0:HALF], lhsT=w0_codes[:, block(j)].bitcast(FP8X4), lhsT_scale=w0_scales[:, block(j)],
                                 rhs=x2_codes[:, HALF:R].bitcast(FP8X4), rhs_scale=x2_scales[:, HALF:R], start=True, stop=True)
             nc.scalar.activation(scaled_slots[j][:], slot_bank[:, 0:HALF], COPY, scale=ts_col[:, j : j + 1])
-        turn_x(1, early, "b7")
-        z_banks = [bank("b%d" % (4 + k), "z_bank%d" % k) for k in range(2)]
+        turn_x(1, EARLY_BLOCKS, 7)
+        z_banks = [bank(4 + k, "z_bank%d" % k) for k in range(2)]
         for k in range(2):
             for j in range(BLOCKS):
                 nc.tensor.transpose(z_banks[k][:, block(j)], scaled_slots[j][:, block(k)], ident[:])
 
         terms = [sb("terms%d" % t, [P, R], F32) for t in range(PACK)]
-        q_banks = [bank("b%d" % b, "q_bank%d" % b) for b in range(BLOCKS)]
+        q_banks = [bank(b, "q_bank%d" % b) for b in range(BLOCKS)]
 
         def look_up(t, blocks):
-            cut = slice(P * blocks[0], P * (blocks[-1] + 1))
-            nc.vector.tensor_tensor(terms[t][:, cut], wT_sb[t][:].indirect(taken[:, 8 * blocks[0] : 8 * (blocks[-1] + 1)]), xT[t][:, cut], ALU.mult)
+            entries = taken[:, LIST_COLUMNS * blocks[0] : LIST_COLUMNS * (blocks[-1] + 1)]
+            nc.vector.tensor_tensor(terms[t][:, span(blocks)], wT_sb[t][:].indirect(entries), xT[t][:, span(blocks)], ALU.mult)
             for b in blocks:
-                if b < EARLY:
-                    nc.tensor.matmul(q_banks[b][:, 0:P], lhsT=terms[t][:, block(b)], rhs=ident[:], is_transpose=True, start=(t == 0), stop=(t == PACK - 1))
+                if b in EARLY_BLOCKS:
+                    nc.tensor.matmul(q_banks[b][:, 0:P], lhsT=terms[t][:, block(b)], rhs=ident[:], is_transpose=True,
+                                     start=(t == 0), stop=(t == PACK - 1))
                 else:
                     nc.tensor.transpose(q_banks[b][:, block(t)], terms[t][:, block(b)], ident[:])
 
-        turn_x(2, early, "b6")
-        turn_x(3, early, "b7")
-        look_up(0, late)
-        look_up(0, early)
+        turn_x(2, EARLY_BLOCKS, 6)
+        turn_x(3, EARLY_BLOCKS, 7)
+        look_up(0, LATE_BLOCKS)
+        look_up(0, EARLY_BLOCKS)
         look_up(1, range(BLOCKS))
         for k in range(2):
-            row_maximum(2 + k, z_banks[k][:])
+            b = 2 + k
+            unread = spare.tile([P, I], F32, name="unread", tag="unread")
+            nc.vector.tensor_scalar(out=unread[:], in0=z_banks[k][:], scalar1=cols[:, US + b : US + b + 1], scalar2=None,
+                                    op0=ALU.mult, op1=ALU.max, accum_out=largest[:, b : b + 1])
         wtarget = [sb("wtarget%d" % b, [P, 1], F32) for b in range(BLOCKS)]
         for b in range(BLOCKS):
             nc.scalar.activation(wtarget[b][:], largest[:, b : b + 1], IDENTITY, scale=slope[:, b : b + 1], bias=base[:, b : b + 1])
-        share = [sb("share%d" % b, [P, 1], F32) for b in early]
-        for b in early:
+        share = [sb("share%d" % b, [P, 1], F32) for b in EARLY_BLOCKS]
+        for b in EARLY_BLOCKS:
             nc.scalar.activation(share[b][:], wtarget[b][:], COPY, scale=1.0 / P)
         look_up(2, range(BLOCKS))
-        look_up(3, (0, 1))
-        look_up(3, (2,))
-        look_up(3, (3,))
+        look_up(3, EARLY_BLOCKS)
+        for b in LATE_BLOCKS:
+            look_up(3, (b,))
 
-        wq = [sb("wq%d" % b, [P, 1], F32) for b in range(BLOCKS)]
+        row_sum = [sb("row_sum%d" % b, [P, 1], F32) for b in range(BLOCKS)]
         err = sb("err", [P, R], F32)
-        e_banks = [bank("b%d" % (4 + h), "e_bank%d" % h) for h in range(2)]
+        e_banks = [bank(number, "e_bank%d" % b) for b, number in enumerate((4, 7, 5, 6))]
 
-        def sum_q(b):
-            products = spare.tile([P, D], F32, name="unread", tag="unread")
-            if b < EARLY:
-                nc.scalar.activation(products[:, 0:P], q_banks[b][:, 0:P], IDENTITY, scale=cols[:, 8 + b : 9 + b], bias=share[b][:], accum_out=wq[b][:])
+        def spread_e(b):
+            unread = spare.tile([P, D], F32, name="unread", tag="unread")
+            spread = e_banks[b][:, 0:P]
+            if b in EARLY_BLOCKS:
+                nc.scalar.activation(unread[:, 0:P], q_banks[b][:, 0:P], IDENTITY, scale=cols[:, WT + b : WT + b + 1], bias=share[b][:],
+                                     accum_out=row_sum[b][:])
             else:
-                nc.vector.scalar_tensor_tensor(out=products[:].rearrange("r (p t) -> r p t", t=PACK), in0=q_banks[b][:].rearrange("r (t p) -> r p t", t=PACK),
-                                               scalar=1.0, in1=x_sb[b][:].rearrange("r (p t) -> r p t", t=PACK), op0=ALU.mult, op1=ALU.mult, accum_out=wq[b][:])
-            out = e_banks[b // 2][:, block(b % 2)]
-            if b >= EARLY:
-                nc.tensor.matmul(out, lhsT=wtarget[b][:].to_broadcast([P, P]), rhs=ident[:], is_transpose=True, start=True, stop=False)
-            nc.tensor.matmul(out, lhsT=wq[b][:].to_broadcast([P, P]), rhs=ident[:], is_transpose=True, start=(b < EARLY), stop=True)
+                nc.vector.scalar_tensor_tensor(out=unread[:].rearrange("r (p t) -> r p t", t=PACK),
+                                               in0=q_banks[b][:].rearrange("r (t p) -> r p t", t=PACK), scalar=1.0,
+                                               in1=x_sb[b][:].rearrange("r (p t) -> r p t", t=PACK),
+                                               op0=ALU.mult, op1=ALU.mult, accum_out=row_sum[b][:])
+                nc.tensor.matmul(spread, lhsT=wtarget[b][:].to_broadcast([P, P]), rhs=ident[:], is_transpose=True, start=True, stop=False)
+            nc.tensor.matmul(spread, lhsT=row_sum[b][:].to_broadcast([P, P]), rhs=ident[:], is_transpose=True,
+                             start=(b in EARLY_BLOCKS), stop=True)
+            nc.scalar.copy(err[:, block(b)], spread)
 
-        sum_q(0)
-        sum_q(1)
-        nc.scalar.copy(err[:, 0:HALF], e_banks[0][:, 0:HALF])
-        sum_q(2)
-        turn_x(0, (2, 3), "b2")
-        sum_q(3)
-        nc.scalar.copy(err[:, HALF:R], e_banks[1][:, 0:HALF])
-        turn_x(1, late, "b4")
-        turn_x(2, late, "b3")
-        turn_x(3, late, "b2")
+        spread_e(0)
+        spread_e(1)
+        spread_e(2)
+        turn_x(0, LATE_BLOCKS, 2)
+        spread_e(3)
+        turn_x(1, LATE_BLOCKS, 7)
+        turn_x(2, LATE_BLOCKS, 5)
+        turn_x(3, LATE_BLOCKS, 2)
 
         windows = [keep.tile([P, T], F32, name="window_%d" % t, tag="table%d" % t, align_bytes=64) for t in range(PACK)]
         for t in range(PACK):
@@ -237,7 +242,8 @@ def tile_attend_gtd_pl_kernel(tc, x2, x, w0, wT, us, ts, rw, wt, offs, aoffs, ou
             if t == 0:
                 for h in range(2):
                     cut = slice(HALF * h, HALF * (h + 1))
-                    nc.vector.tensor_tensor(windows[t][:].indirect(taken[:, 16 * h : 16 * (h + 1)]), xT[t][:, cut], err[:, cut], ALU.mult)
+                    entries = taken[:, 2 * LIST_COLUMNS * h : 2 * LIST_COLUMNS * (h + 1)]
+                    nc.vector.tensor_tensor(windows[t][:].indirect(entries), xT[t][:, cut], err[:, cut], ALU.mult)
             else:
                 nc.vector.tensor_tensor(windows[t][:].indirect(taken[:]), xT[t][:], err[:], ALU.mult)
             nc.sync.dma_start(out=out_planes[t], in_=windows[t][:])
@@ -247,13 +253,14 @@ def tile_attend_gtd_pl_kernel(tc, x2, x, w0, wT, us, ts, rw, wt, offs, aoffs, ou
             elif t == 2:
                 nc.scalar.copy(pairs[:, VECTOR_ROUNDS:, 1, :, 0], chunked[:, VECTOR_ROUNDS:, :])
             else:
-                for k in range(VECTOR_ROUNDS, CHUNKS):
-                    nc.scalar.copy(pairs[:, k, 1, :, 1], chunked[:, k, :])
+                for k in range(VECTOR_ROUNDS, CHUNKS, 2):
+                    nc.scalar.copy(pairs[:, k : k + 2, 1, :, 1], chunked[:, k : k + 2, :])
         for t in (2, 3):
-            nc.vector.tensor_copy(pairs[:, 0:VECTOR_ROUNDS, 1, :, t - 2], windows[t][:, 0 : VECTOR_ROUNDS * WIDTH].rearrange("p (k c) -> p k c", c=WIDTH))
+            first_chunks = windows[t][:, 0 : VECTOR_ROUNDS * WIDTH].rearrange("p (k c) -> p k c", c=WIDTH)
+            nc.vector.tensor_copy(pairs[:, 0:VECTOR_ROUNDS, 1, :, t - 2], first_chunks)
 
         out_words = out_1[0].rearrange("p c l -> p (c l)").bitcast(I32)
-        y_scales = sb("y_scales", [P, T // 2], U8)
+        y_scales = sb("y_scales", [P, SCALE_CHUNKS * WIDTH], U8)
         grouped = sb("grouped", [P, T * PACK], BF16)
         y_codes = sb("y_codes", [P, T], U32)
 
@@ -268,21 +275,33 @@ def tile_attend_gtd_pl_kernel(tc, x2, x, w0, wT, us, ts, rw, wt, offs, aoffs, ou
 
         def quantise(first, count):
             cut = slice(first * WIDTH, (first + count) * WIDTH)
-            place = first % 4
-            nc.vector.quantize_mx(out=y_codes[:, cut].bitcast(FP8X4), scales=y_scales[4 * (first // 4) : P, place * WIDTH : (place + count) * WIDTH],
+            place = first % SCALE_CHUNKS
+            nc.vector.quantize_mx(out=y_codes[:, cut].bitcast(FP8X4),
+                                  scales=y_scales[4 * (first // SCALE_CHUNKS) : P, place * WIDTH : (place + count) * WIDTH],
                                   in_=grouped[:, first * WIDTH * PACK : (first + count) * WIDTH * PACK])
+
+        def store_codes(first, count):
+            cut = slice(first * WIDTH, (first + count) * WIDTH)
             nc.sync.dma_start(out=out_words[:, cut], in_=y_codes[:, cut].bitcast(I32))
 
-        weave(0, 2)
-        weave(2, 2)
-        quantise(0, 2)
-        weave(4, 2)
-        quantise(2, 2)
-        for k in range(VECTOR_WEAVES, CHUNKS):
-            weave(k, 1)
-        quantise(4, 2)
-        quantise(6, 1)
-        quantise(7, 1)
+        weave(0, 4)
+        weave(4, 4)
+        quantise(0, 4)
+        store_codes(0, 4)
+        weave(8, 2)
+        quantise(4, 4)
+        store_codes(4, 4)
+        weave(10, 2)
+        weave(12, 2)
+        weave(14, 1)
+        weave(15, 1)
+        quantise(8, 4)
+        store_codes(8, 4)
+        quantise(12, 2)
+        quantise(14, 1)
+        store_codes(12, 3)
+        quantise(15, 1)
+        store_codes(15, 1)
         out_scales = out_2[0].bitcast(I32).rearrange("f (g c) -> g f c", g=2)
         for quad in range(4):
             queue = nc.scalar if quad % 2 else nc.sync

@@ -30,7 +30,7 @@ LATE_BLOCKS = tuple(range(EARLY, BLOCKS))
 WIDTH = 128
 CHUNKS = T // WIDTH
 VECTOR_ROUNDS = 2
-VECTOR_WEAVES = 10
+VECTOR_WEAVES = 12
 SCALE_CHUNKS = CHUNKS // 2
 US, RW, WT = 0, BLOCKS, 2 * BLOCKS
 
@@ -75,16 +75,17 @@ def tile_attend_gtd_pl_kernel(tc, x2, x, w0, wT, us, ts, rw, wt, offs, aoffs, ou
         nc.sync.dma_start(taken[:], aoffs)
         x2_sb = sb("x2_sb", [P, PACK, R], F32)
         nc.sync.dma_start(out=x2_sb[:], in_=x2.rearrange("(p t) r -> p t r", t=PACK))
-        x_sb = [sb("x_sb%d" % b, [P, D], F32) for b in range(BLOCKS)]
+        x_early = sb("x_early", [P, EARLY, D], F32)
+        x_late = [sb("x_late%d" % b, [P, D], F32) for b in LATE_BLOCKS]
+        x_sb = [x_early[:, b, :] for b in EARLY_BLOCKS] + [tile[:] for tile in x_late]
         wT_planes = wT.rearrange("(p t) c -> t p c", t=PACK)
         wT_sb = [keep.tile([P, T], F32, name="wT_%d" % t, tag="table%d" % t, align_bytes=64) for t in range(PACK)]
         for t in range(PACK):
             nc.sync.dma_start(out=wT_sb[t][:], in_=wT_planes[t])
             if t == 0:
-                for b in EARLY_BLOCKS:
-                    nc.sync.dma_start(out=x_sb[b][:], in_=x[block(b), :])
+                nc.sync.dma_start(out=x_early[:], in_=x[span(EARLY_BLOCKS), :].rearrange("(b p) d -> p b d", p=P))
         for b in LATE_BLOCKS:
-            nc.sync.dma_start(out=x_sb[b][:], in_=x[block(b), :])
+            nc.sync.dma_start(out=x_sb[b], in_=x[block(b), :])
 
         ident = sb("ident", [P, P], F32)
         make_identity(nc, ident[:])
@@ -144,7 +145,7 @@ def tile_attend_gtd_pl_kernel(tc, x2, x, w0, wT, us, ts, rw, wt, offs, aoffs, ou
         def turn_x(t, blocks, number):
             xt_bank = bank(number, "xt_bank%d_%d" % (t, blocks[0]))
             for b in blocks:
-                nc.tensor.transpose(xt_bank[:, block(b)], x_sb[b][:].rearrange("r (p t) -> r t p", t=PACK)[:, t, :], ident[:])
+                nc.tensor.transpose(xt_bank[:, block(b)], x_sb[b].rearrange("r (p t) -> r t p", t=PACK)[:, t, :], ident[:])
             nc.scalar.copy(xT[t][:, span(blocks)], xt_bank[:, span(blocks)])
 
         largest = sb("largest", [P, BLOCKS], F32)
@@ -217,7 +218,7 @@ def tile_attend_gtd_pl_kernel(tc, x2, x, w0, wT, us, ts, rw, wt, offs, aoffs, ou
             else:
                 nc.vector.scalar_tensor_tensor(out=unread[:].rearrange("r (p t) -> r p t", t=PACK),
                                                in0=q_banks[b][:].rearrange("r (t p) -> r p t", t=PACK), scalar=1.0,
-                                               in1=x_sb[b][:].rearrange("r (p t) -> r p t", t=PACK),
+                                               in1=x_sb[b].rearrange("r (p t) -> r p t", t=PACK),
                                                op0=ALU.mult, op1=ALU.mult, accum_out=row_sum[b][:])
                 nc.tensor.matmul(spread, lhsT=wtarget[b][:].to_broadcast([P, P]), rhs=ident[:], is_transpose=True, start=True, stop=False)
             nc.tensor.matmul(spread, lhsT=row_sum[b][:].to_broadcast([P, P]), rhs=ident[:], is_transpose=True,
@@ -288,10 +289,9 @@ def tile_attend_gtd_pl_kernel(tc, x2, x, w0, wT, us, ts, rw, wt, offs, aoffs, ou
         weave(4, 4)
         quantise(0, 4)
         store_codes(0, 4)
-        weave(8, 2)
+        weave(8, 4)
         quantise(4, 4)
         store_codes(4, 4)
-        weave(10, 2)
         weave(12, 2)
         weave(14, 1)
         weave(15, 1)

@@ -31,7 +31,7 @@ WIDTH = 128
 CHUNKS = T // WIDTH
 VECTOR_ROUNDS = 2
 VECTOR_WEAVES = 12
-SCALE_CHUNKS = CHUNKS // 2
+SCALE_CHUNKS = CHUNKS // 4
 US, RW, WT = 0, BLOCKS, 2 * BLOCKS
 
 
@@ -285,24 +285,27 @@ def tile_attend_gtd_pl_kernel(tc, x2, x, w0, wT, us, ts, rw, wt, offs, aoffs, ou
             cut = slice(first * WIDTH, (first + count) * WIDTH)
             nc.sync.dma_start(out=out_words[:, cut], in_=y_codes[:, cut].bitcast(I32))
 
-        weave(0, 4)
+        weave(0, 2)
+        weave(2, 2)
         weave(4, 4)
         quantise(0, 4)
         store_codes(0, 4)
-        weave(8, 4)
+        weave(8, 2)
         quantise(4, 4)
+        weave(10, 2)
         store_codes(4, 4)
         weave(12, 2)
         weave(14, 1)
         weave(15, 1)
-        quantise(8, 4)
+        quantise(8, 2)
+        quantise(10, 2)
         store_codes(8, 4)
         quantise(12, 2)
         quantise(14, 1)
         store_codes(12, 3)
         quantise(15, 1)
         store_codes(15, 1)
-        out_scales = out_2[0].bitcast(I32).rearrange("f (g c) -> g f c", g=2)
+        out_scales = out_2[0].bitcast(I32).rearrange("f (g c) -> g f c", g=4)
         for quad in range(4):
             queue = nc.scalar if quad % 2 else nc.sync
-            queue.dma_start(out=out_scales[:, 4 * quad : 4 * quad + 4, :], in_=y_scales[32 * quad : 32 * quad + 8, :].bitcast(I32))
+            queue.dma_start(out=out_scales[:, 4 * quad : 4 * quad + 4, :], in_=y_scales[32 * quad : 32 * quad + 16, :].bitcast(I32))

@@ -287,7 +287,8 @@ def tile_attend_gtd_pl_kernel(tc, x2, x, w0, wT, us, ts, rw, wt, offs, aoffs, ou
 
         weave(0, 2)
         weave(2, 2)
-        weave(4, 4)
+        weave(4, 2)
+        weave(6, 2)
         quantise(0, 4)
         store_codes(0, 4)
         weave(8, 2)

@@ -27,10 +27,10 @@ DISCOUNT = 0.9
 EARLY = 2
 EARLY_BLOCKS = tuple(range(EARLY))
 LATE_BLOCKS = tuple(range(EARLY, BLOCKS))
+ALL_BLOCKS = tuple(range(BLOCKS))
 WIDTH = 128
 CHUNKS = T // WIDTH
-VECTOR_ROUNDS = 2
-VECTOR_WEAVES = 12
+SCALAR_WEAVES = 12
 SCALE_CHUNKS = CHUNKS // 4
 US, RW, WT = 0, BLOCKS, 2 * BLOCKS
 
@@ -61,6 +61,9 @@ def tile_attend_gtd_pl_kernel(tc, x2, x, w0, wT, us, ts, rw, wt, offs, aoffs, ou
         taken = lists.tile([P, R // 16], U16, name="taken")
         vecs = sb("vecs", [P, P], F32)
         nc.vector.memset(vecs[:], 0.0)
+        own_windows = [sb("window_%d" % t, [P, T], F32) for t in range(2, PACK)]
+        for window in own_windows:
+            nc.vector.memset(window[:], 0.0)
         ts_cut = sb("ts_cut", [P, T // P], F32)
 
         w0_planes = w0.rearrange("(p t) c -> t p c", t=PACK)
@@ -225,40 +228,69 @@ def tile_attend_gtd_pl_kernel(tc, x2, x, w0, wT, us, ts, rw, wt, offs, aoffs, ou
                              start=(b in EARLY_BLOCKS), stop=True)
             nc.scalar.copy(err[:, block(b)], spread)
 
+        late_banks = {}
+
+        def turn_late(t, number, blocks):
+            late_banks[t] = bank(number, "late_bank%d" % t)
+            for b in blocks:
+                nc.tensor.transpose(late_banks[t][:, block(b)], x_sb[b].rearrange("r (p t) -> r t p", t=PACK)[:, t, :], ident[:])
+
         spread_e(0)
         spread_e(1)
         spread_e(2)
-        turn_x(0, LATE_BLOCKS, 2)
+        turn_late(1, 0, LATE_BLOCKS)
         spread_e(3)
-        turn_x(1, LATE_BLOCKS, 7)
-        turn_x(2, LATE_BLOCKS, 5)
-        turn_x(3, LATE_BLOCKS, 2)
+        turn_late(0, 1, LATE_BLOCKS)
+        turn_late(2, 2, ALL_BLOCKS)
+        turn_late(3, 3, ALL_BLOCKS)
 
-        windows = [keep.tile([P, T], F32, name="window_%d" % t, tag="table%d" % t, align_bytes=64) for t in range(PACK)]
-        for t in range(PACK):
+        windows = [keep.tile([P, T], F32, name="window_%d" % t, tag="table%d" % t, align_bytes=64) for t in range(2)]
+        for t in range(2):
             nc.gpsimd.memset(windows[t][:], 0.0)
+        windows = windows + own_windows
         pairs = sb("pairs", [P, CHUNKS, 2, WIDTH, 2], BF16)
         out_planes = out_0.rearrange("(p t) c -> t p c", t=PACK)
-        for t in range(PACK):
-            if t == 0:
-                for h in range(2):
-                    cut = slice(HALF * h, HALF * (h + 1))
-                    entries = taken[:, 2 * LIST_COLUMNS * h : 2 * LIST_COLUMNS * (h + 1)]
-                    nc.vector.tensor_tensor(windows[t][:].indirect(entries), xT[t][:, cut], err[:, cut], ALU.mult)
-            else:
-                nc.vector.tensor_tensor(windows[t][:].indirect(taken[:]), xT[t][:], err[:], ALU.mult)
+
+        def entries(blocks):
+            return taken[:, LIST_COLUMNS * blocks[0] : LIST_COLUMNS * (blocks[-1] + 1)]
+
+        products = [sb("products%d" % t, [P, R], F32) for t in range(PACK)]
+
+        def multiply(t, blocks):
+            turned = xT[t] if blocks == EARLY_BLOCKS else late_banks[t]
+            nc.vector.tensor_tensor(products[t][:, span(blocks)], turned[:, span(blocks)], err[:, span(blocks)], ALU.mult)
+
+        def scatter(t, blocks):
+            nc.scalar.activation(windows[t][:].indirect(entries(blocks)), products[t][:, span(blocks)], COPY)
+
+        def store(t):
             nc.sync.dma_start(out=out_planes[t], in_=windows[t][:])
+
+        def round_plane(t, first, count):
             chunked = windows[t][:].rearrange("p (k c) -> p k c", c=WIDTH)
-            if t < 2:
-                nc.scalar.copy(pairs[:, :, 0, :, t], chunked)
-            elif t == 2:
-                nc.scalar.copy(pairs[:, VECTOR_ROUNDS:, 1, :, 0], chunked[:, VECTOR_ROUNDS:, :])
-            else:
-                for k in range(VECTOR_ROUNDS, CHUNKS, 2):
-                    nc.scalar.copy(pairs[:, k : k + 2, 1, :, 1], chunked[:, k : k + 2, :])
+            nc.vector.tensor_copy(pairs[:, first : first + count, t // 2, :, t % 2], chunked[:, first : first + count, :])
+
+        multiply(1, EARLY_BLOCKS)
+        scatter(1, EARLY_BLOCKS)
+        cut = span(EARLY_BLOCKS)
+        nc.vector.tensor_tensor(windows[0][:].indirect(entries(EARLY_BLOCKS)), xT[0][:, cut], err[:, cut], ALU.mult)
+        multiply(1, LATE_BLOCKS)
+        scatter(1, LATE_BLOCKS)
+        store(1)
+        multiply(2, ALL_BLOCKS)
+        multiply(0, LATE_BLOCKS)
+        nc.vector.tensor_copy(windows[0][:].indirect(entries(LATE_BLOCKS)), products[0][:, span(LATE_BLOCKS)])
+        store(0)
+        multiply(3, ALL_BLOCKS)
         for t in (2, 3):
-            first_chunks = windows[t][:, 0 : VECTOR_ROUNDS * WIDTH].rearrange("p (k c) -> p k c", c=WIDTH)
-            nc.vector.tensor_copy(pairs[:, 0:VECTOR_ROUNDS, 1, :, t - 2], first_chunks)
+            scatter(t, EARLY_BLOCKS)
+            scatter(t, LATE_BLOCKS)
+            store(t)
+        for t in (1, 0, 2):
+            round_plane(t, 0, CHUNKS)
+        round_plane(3, 0, 4)
+        round_plane(3, 4, 6)
+        round_plane(3, 10, 6)
 
         out_words = out_1[0].rearrange("p c l -> p (c l)").bitcast(I32)
         y_scales = sb("y_scales", [P, SCALE_CHUNKS * WIDTH], U8)
@@ -268,7 +300,7 @@ def tile_attend_gtd_pl_kernel(tc, x2, x, w0, wT, us, ts, rw, wt, offs, aoffs, ou
         def weave(first, count):
             dst = grouped[:, first * WIDTH * PACK : (first + count) * WIDTH * PACK]
             src = pairs[:, first : first + count]
-            if first < VECTOR_WEAVES:
+            if first >= SCALAR_WEAVES:
                 nc.vector.tensor_copy(dst.rearrange("p (k c u e) -> p k c u e", k=count, u=2, e=2), src.rearrange("p k u c e -> p k c u e"))
             else:
                 words = src.rearrange("p k u c e -> p k u (c e)").bitcast(F32).rearrange("p k u c -> p k c u")
@@ -285,27 +317,18 @@ def tile_attend_gtd_pl_kernel(tc, x2, x, w0, wT, us, ts, rw, wt, offs, aoffs, ou
             cut = slice(first * WIDTH, (first + count) * WIDTH)
             nc.sync.dma_start(out=out_words[:, cut], in_=y_codes[:, cut].bitcast(I32))
 
-        weave(0, 2)
-        weave(2, 2)
-        weave(4, 2)
-        weave(6, 2)
+        for first in range(0, SCALAR_WEAVES, 2):
+            weave(first, 2)
+        weave(12, 4)
         quantise(0, 4)
         store_codes(0, 4)
-        weave(8, 2)
+        quantise(12, 4)
+        store_codes(12, 4)
         quantise(4, 4)
-        weave(10, 2)
         store_codes(4, 4)
-        weave(12, 2)
-        weave(14, 1)
-        weave(15, 1)
         quantise(8, 2)
         quantise(10, 2)
         store_codes(8, 4)
-        quantise(12, 2)
-        quantise(14, 1)
-        store_codes(12, 3)
-        quantise(15, 1)
-        store_codes(15, 1)
         out_scales = out_2[0].bitcast(I32).rearrange("f (g c) -> g f c", g=4)
         for quad in range(4):
             queue = nc.scalar if quad % 2 else nc.sync

@@ -30,7 +30,8 @@ LATE_BLOCKS = tuple(range(EARLY, BLOCKS))
 ALL_BLOCKS = tuple(range(BLOCKS))
 WIDTH = 128
 CHUNKS = T // WIDTH
-SCALAR_WEAVES = 12
+VECTOR_ROUNDS = 12
+VECTOR_WEAVES = 4
 SCALE_CHUNKS = CHUNKS // 4
 US, RW, WT = 0, BLOCKS, 2 * BLOCKS
 
@@ -237,12 +238,12 @@ def tile_attend_gtd_pl_kernel(tc, x2, x, w0, wT, us, ts, rw, wt, offs, aoffs, ou
 
         spread_e(0)
         spread_e(1)
+        turn_x(0, LATE_BLOCKS, 0)
         spread_e(2)
-        turn_late(1, 0, LATE_BLOCKS)
+        turn_late(1, 1, LATE_BLOCKS)
         spread_e(3)
-        turn_late(0, 1, LATE_BLOCKS)
         turn_late(2, 2, ALL_BLOCKS)
-        turn_late(3, 3, ALL_BLOCKS)
+        turn_x(3, LATE_BLOCKS, 3)
 
         windows = [keep.tile([P, T], F32, name="window_%d" % t, tag="table%d" % t, align_bytes=64) for t in range(2)]
         for t in range(2):
@@ -254,43 +255,48 @@ def tile_attend_gtd_pl_kernel(tc, x2, x, w0, wT, us, ts, rw, wt, offs, aoffs, ou
         def entries(blocks):
             return taken[:, LIST_COLUMNS * blocks[0] : LIST_COLUMNS * (blocks[-1] + 1)]
 
-        products = [sb("products%d" % t, [P, R], F32) for t in range(PACK)]
+        products = {}
 
-        def multiply(t, blocks):
+        def multiply(t, blocks, tag):
+            products[t, blocks[0]] = keep.tile([P, P * len(blocks)], F32, name="products%d_%d" % (t, blocks[0]), tag=tag, align_bytes=64)
             turned = xT[t] if blocks == EARLY_BLOCKS else late_banks[t]
-            nc.vector.tensor_tensor(products[t][:, span(blocks)], turned[:, span(blocks)], err[:, span(blocks)], ALU.mult)
+            nc.vector.tensor_tensor(products[t, blocks[0]][:], turned[:, span(blocks)], err[:, span(blocks)], ALU.mult)
 
-        def scatter(t, blocks):
-            nc.scalar.activation(windows[t][:].indirect(entries(blocks)), products[t][:, span(blocks)], COPY)
+        def scatter(t, blocks, source):
+            nc.scalar.activation(windows[t][:].indirect(entries(blocks)), source, COPY)
+
+        def scatter_fused(t, blocks):
+            nc.vector.tensor_tensor(windows[t][:].indirect(entries(blocks)), xT[t][:, span(blocks)], err[:, span(blocks)], ALU.mult)
 
         def store(t):
             nc.sync.dma_start(out=out_planes[t], in_=windows[t][:])
 
-        def round_plane(t, first, count):
+        def round_plane(copy, t, first, count):
             chunked = windows[t][:].rearrange("p (k c) -> p k c", c=WIDTH)
-            nc.vector.tensor_copy(pairs[:, first : first + count, t // 2, :, t % 2], chunked[:, first : first + count, :])
+            copy(pairs[:, first : first + count, t // 2, :, t % 2], chunked[:, first : first + count, :])
 
-        multiply(1, EARLY_BLOCKS)
-        scatter(1, EARLY_BLOCKS)
-        cut = span(EARLY_BLOCKS)
-        nc.vector.tensor_tensor(windows[0][:].indirect(entries(EARLY_BLOCKS)), xT[0][:, cut], err[:, cut], ALU.mult)
-        multiply(1, LATE_BLOCKS)
-        scatter(1, LATE_BLOCKS)
+        multiply(1, EARLY_BLOCKS, "early_products")
+        scatter(1, EARLY_BLOCKS, products[1, 0][:])
+        scatter_fused(0, EARLY_BLOCKS)
+        multiply(1, LATE_BLOCKS, "late_products")
+        scatter(1, LATE_BLOCKS, products[1, EARLY][:])
         store(1)
-        multiply(2, ALL_BLOCKS)
-        multiply(0, LATE_BLOCKS)
-        nc.vector.tensor_copy(windows[0][:].indirect(entries(LATE_BLOCKS)), products[0][:, span(LATE_BLOCKS)])
+        multiply(2, ALL_BLOCKS, "whole_products")
+        scatter_fused(0, LATE_BLOCKS)
         store(0)
-        multiply(3, ALL_BLOCKS)
+        for blocks in (EARLY_BLOCKS, LATE_BLOCKS):
+            scatter(2, blocks, products[2, 0][:, span(blocks)])
+        store(2)
+        multiply(3, EARLY_BLOCKS, "early_products")
+        scatter_fused(3, LATE_BLOCKS)
+        scatter(3, EARLY_BLOCKS, products[3, 0][:])
+        store(3)
+        for t in (1, 0):
+            round_plane(nc.vector.tensor_copy, t, 0, CHUNKS)
         for t in (2, 3):
-            scatter(t, EARLY_BLOCKS)
-            scatter(t, LATE_BLOCKS)
-            store(t)
-        for t in (1, 0, 2):
-            round_plane(t, 0, CHUNKS)
-        round_plane(3, 0, 4)
-        round_plane(3, 4, 6)
-        round_plane(3, 10, 6)
+            round_plane(nc.scalar.copy, t, VECTOR_ROUNDS, CHUNKS - VECTOR_ROUNDS)
+        for t in (2, 3):
+            round_plane(nc.vector.tensor_copy, t, 0, VECTOR_ROUNDS)
 
         out_words = out_1[0].rearrange("p c l -> p (c l)").bitcast(I32)
         y_scales = sb("y_scales", [P, SCALE_CHUNKS * WIDTH], U8)
@@ -300,7 +306,7 @@ def tile_attend_gtd_pl_kernel(tc, x2, x, w0, wT, us, ts, rw, wt, offs, aoffs, ou
         def weave(first, count):
             dst = grouped[:, first * WIDTH * PACK : (first + count) * WIDTH * PACK]
             src = pairs[:, first : first + count]
-            if first >= SCALAR_WEAVES:
+            if first < VECTOR_WEAVES:
                 nc.vector.tensor_copy(dst.rearrange("p (k c u e) -> p k c u e", k=count, u=2, e=2), src.rearrange("p k u c e -> p k c u e"))
             else:
                 words = src.rearrange("p k u c e -> p k u (c e)").bitcast(F32).rearrange("p k u c -> p k c u")
@@ -317,13 +323,14 @@ def tile_attend_gtd_pl_kernel(tc, x2, x, w0, wT, us, ts, rw, wt, offs, aoffs, ou
             cut = slice(first * WIDTH, (first + count) * WIDTH)
             nc.sync.dma_start(out=out_words[:, cut], in_=y_codes[:, cut].bitcast(I32))
 
-        for first in range(0, SCALAR_WEAVES, 2):
-            weave(first, 2)
         weave(12, 4)
-        quantise(0, 4)
-        store_codes(0, 4)
+        weave(0, 4)
         quantise(12, 4)
         store_codes(12, 4)
+        for first in range(VECTOR_WEAVES, VECTOR_ROUNDS, 2):
+            weave(first, 2)
+        quantise(0, 4)
+        store_codes(0, 4)
         quantise(4, 4)
         store_codes(4, 4)
         quantise(8, 2)

@@ -30,8 +30,9 @@ LATE_BLOCKS = tuple(range(EARLY, BLOCKS))
 ALL_BLOCKS = tuple(range(BLOCKS))
 WIDTH = 128
 CHUNKS = T // WIDTH
-VECTOR_ROUNDS = 12
-VECTOR_WEAVES = 4
+SCALAR_ROUNDS = 6
+SCALAR_WEAVES = 8
+RUN = 4
 SCALE_CHUNKS = CHUNKS // 4
 US, RW, WT = 0, BLOCKS, 2 * BLOCKS
 
@@ -249,7 +250,7 @@ def tile_attend_gtd_pl_kernel(tc, x2, x, w0, wT, us, ts, rw, wt, offs, aoffs, ou
         for t in range(2):
             nc.gpsimd.memset(windows[t][:], 0.0)
         windows = windows + own_windows
-        pairs = sb("pairs", [P, CHUNKS, 2, WIDTH, 2], BF16)
+        rounded = sb("rounded", [P, PACK, T], BF16)
         out_planes = out_0.rearrange("(p t) c -> t p c", t=PACK)
 
         def entries(blocks):
@@ -272,8 +273,8 @@ def tile_attend_gtd_pl_kernel(tc, x2, x, w0, wT, us, ts, rw, wt, offs, aoffs, ou
             nc.sync.dma_start(out=out_planes[t], in_=windows[t][:])
 
         def round_plane(copy, t, first, count):
-            chunked = windows[t][:].rearrange("p (k c) -> p k c", c=WIDTH)
-            copy(pairs[:, first : first + count, t // 2, :, t % 2], chunked[:, first : first + count, :])
+            cut = slice(first * WIDTH, (first + count) * WIDTH)
+            copy(rounded[:, t, cut], windows[t][:, cut])
 
         multiply(1, EARLY_BLOCKS, "early_products")
         scatter(1, EARLY_BLOCKS, products[1, 0][:])
@@ -291,12 +292,10 @@ def tile_attend_gtd_pl_kernel(tc, x2, x, w0, wT, us, ts, rw, wt, offs, aoffs, ou
         scatter_fused(3, LATE_BLOCKS)
         scatter(3, EARLY_BLOCKS, products[3, 0][:])
         store(3)
-        for t in (1, 0):
+        for t in (1, 0, 2):
             round_plane(nc.vector.tensor_copy, t, 0, CHUNKS)
-        for t in (2, 3):
-            round_plane(nc.scalar.copy, t, VECTOR_ROUNDS, CHUNKS - VECTOR_ROUNDS)
-        for t in (2, 3):
-            round_plane(nc.vector.tensor_copy, t, 0, VECTOR_ROUNDS)
+        round_plane(nc.scalar.copy, 3, 0, SCALAR_ROUNDS)
+        round_plane(nc.vector.tensor_copy, 3, SCALAR_ROUNDS, CHUNKS - SCALAR_ROUNDS)
 
         out_words = out_1[0].rearrange("p c l -> p (c l)").bitcast(I32)
         y_scales = sb("y_scales", [P, SCALE_CHUNKS * WIDTH], U8)
@@ -305,12 +304,9 @@ def tile_attend_gtd_pl_kernel(tc, x2, x, w0, wT, us, ts, rw, wt, offs, aoffs, ou
 
         def weave(first, count):
             dst = grouped[:, first * WIDTH * PACK : (first + count) * WIDTH * PACK]
-            src = pairs[:, first : first + count]
-            if first < VECTOR_WEAVES:
-                nc.vector.tensor_copy(dst.rearrange("p (k c u e) -> p k c u e", k=count, u=2, e=2), src.rearrange("p k u c e -> p k c u e"))
-            else:
-                words = src.rearrange("p k u c e -> p k u (c e)").bitcast(F32).rearrange("p k u c -> p k c u")
-                nc.scalar.copy(dst.bitcast(F32).rearrange("p (k c u) -> p k c u", k=count, u=2), words)
+            src = rounded[:, :, first * WIDTH : (first + count) * WIDTH]
+            copy = nc.scalar.copy if first < SCALAR_WEAVES else nc.vector.tensor_copy
+            copy(dst.rearrange("p (c i t) -> p c t i", i=RUN, t=PACK), src.rearrange("p t (c i) -> p c t i", i=RUN))
 
         def quantise(first, count):
             cut = slice(first * WIDTH, (first + count) * WIDTH)
@@ -323,19 +319,22 @@ def tile_attend_gtd_pl_kernel(tc, x2, x, w0, wT, us, ts, rw, wt, offs, aoffs, ou
             cut = slice(first * WIDTH, (first + count) * WIDTH)
             nc.sync.dma_start(out=out_words[:, cut], in_=y_codes[:, cut].bitcast(I32))
 
-        weave(12, 4)
-        weave(0, 4)
-        quantise(12, 4)
-        store_codes(12, 4)
-        for first in range(VECTOR_WEAVES, VECTOR_ROUNDS, 2):
+        for first in range(0, SCALAR_WEAVES, 2):
             weave(first, 2)
-        quantise(0, 4)
-        store_codes(0, 4)
-        quantise(4, 4)
-        store_codes(4, 4)
-        quantise(8, 2)
-        quantise(10, 2)
+        weave(8, 4)
+        weave(12, 2)
+        quantise(8, 4)
         store_codes(8, 4)
+        weave(14, 2)
+        quantise(0, 2)
+        quantise(2, 2)
+        store_codes(0, 4)
+        quantise(12, 2)
+        quantise(14, 2)
+        store_codes(12, 4)
+        quantise(4, 2)
+        quantise(6, 2)
+        store_codes(4, 4)
         out_scales = out_2[0].bitcast(I32).rearrange("f (g c) -> g f c", g=4)
         for quad in range(4):
             queue = nc.scalar if quad % 2 else nc.sync

@@ -31,7 +31,7 @@ ALL_BLOCKS = tuple(range(BLOCKS))
 WIDTH = 128
 CHUNKS = T // WIDTH
 SCALAR_ROUNDS = 6
-SCALAR_WEAVES = 8
+SCALAR_WEAVES = 9
 RUN = 4
 SCALE_CHUNKS = CHUNKS // 4
 US, RW, WT = 0, BLOCKS, 2 * BLOCKS
@@ -63,9 +63,6 @@ def tile_attend_gtd_pl_kernel(tc, x2, x, w0, wT, us, ts, rw, wt, offs, aoffs, ou
         taken = lists.tile([P, R // 16], U16, name="taken")
         vecs = sb("vecs", [P, P], F32)
         nc.vector.memset(vecs[:], 0.0)
-        own_windows = [sb("window_%d" % t, [P, T], F32) for t in range(2, PACK)]
-        for window in own_windows:
-            nc.vector.memset(window[:], 0.0)
         ts_cut = sb("ts_cut", [P, T // P], F32)
 
         w0_planes = w0.rearrange("(p t) c -> t p c", t=PACK)
@@ -109,12 +106,7 @@ def tile_attend_gtd_pl_kernel(tc, x2, x, w0, wT, us, ts, rw, wt, offs, aoffs, ou
         cols = sb("cols", [P, 3 * BLOCKS], F32)
         nc.scalar.activation(cols[:], vec_bank[:, 0 : 3 * BLOCKS], COPY)
 
-        xT = [sb("xT%d" % t, [P, R], F32) for t in range(PACK)]
-        wt_bank = bank(5, "wt_bank")
-        for b in LATE_BLOCKS:
-            nc.tensor.transpose(wt_bank[:, block(b)], cols[:, WT + b : WT + b + 1].to_broadcast([P, P]), ident[:])
-        for t in range(PACK):
-            nc.scalar.copy(xT[t][:, span(LATE_BLOCKS)], wt_bank[:, span(LATE_BLOCKS)])
+        xT = [keep.tile([P, HALF], F32, name="xT%d" % t, tag="turned%d" % t, align_bytes=64) for t in range(PACK)]
         slope = sb("slope", [P, BLOCKS], F32)
         nc.vector.tensor_scalar(out=slope[:], in0=cols[:, WT : WT + BLOCKS], scalar1=-DISCOUNT, scalar2=None, op0=ALU.mult)
         base = sb("base", [P, BLOCKS], F32)
@@ -179,21 +171,26 @@ def tile_attend_gtd_pl_kernel(tc, x2, x, w0, wT, us, ts, rw, wt, offs, aoffs, ou
         terms = [sb("terms%d" % t, [P, R], F32) for t in range(PACK)]
         q_banks = [bank(b, "q_bank%d" % b) for b in range(BLOCKS)]
 
-        def look_up(t, blocks):
-            entries = taken[:, LIST_COLUMNS * blocks[0] : LIST_COLUMNS * (blocks[-1] + 1)]
-            nc.vector.tensor_tensor(terms[t][:, span(blocks)], wT_sb[t][:].indirect(entries), xT[t][:, span(blocks)], ALU.mult)
+        def entries(blocks):
+            return taken[:, LIST_COLUMNS * blocks[0] : LIST_COLUMNS * (blocks[-1] + 1)]
+
+        def look_up_early(t, blocks):
+            cut = span(blocks)
+            nc.vector.tensor_tensor(terms[t][:, cut], wT_sb[t][:].indirect(entries(blocks)), xT[t][:, cut], ALU.mult)
             for b in blocks:
-                if b in EARLY_BLOCKS:
-                    nc.tensor.matmul(q_banks[b][:, 0:P], lhsT=terms[t][:, block(b)], rhs=ident[:], is_transpose=True,
-                                     start=(t == 0), stop=(t == PACK - 1))
-                else:
-                    nc.tensor.transpose(q_banks[b][:, block(t)], terms[t][:, block(b)], ident[:])
+                nc.tensor.matmul(q_banks[b][:, 0:P], lhsT=terms[t][:, block(b)], rhs=ident[:], is_transpose=True,
+                                 start=(t == 0), stop=(t == PACK - 1))
+
+        def look_up_late(t, blocks):
+            nc.scalar.activation(terms[t][:, span(blocks)], wT_sb[t][:].indirect(entries(blocks)), COPY)
+            for b in blocks:
+                nc.tensor.transpose(q_banks[b][:, block(t)], terms[t][:, block(b)], ident[:])
 
         turn_x(2, EARLY_BLOCKS, 6)
         turn_x(3, EARLY_BLOCKS, 7)
-        look_up(0, LATE_BLOCKS)
-        look_up(0, EARLY_BLOCKS)
-        look_up(1, range(BLOCKS))
+        for t in range(2):
+            look_up_late(t, LATE_BLOCKS)
+            look_up_early(t, EARLY_BLOCKS)
         for k in range(2):
             b = 2 + k
             unread = spare.tile([P, I], F32, name="unread", tag="unread")
@@ -205,69 +202,70 @@ def tile_attend_gtd_pl_kernel(tc, x2, x, w0, wT, us, ts, rw, wt, offs, aoffs, ou
         share = [sb("share%d" % b, [P, 1], F32) for b in EARLY_BLOCKS]
         for b in EARLY_BLOCKS:
             nc.scalar.activation(share[b][:], wtarget[b][:], COPY, scale=1.0 / P)
-        look_up(2, range(BLOCKS))
-        look_up(3, EARLY_BLOCKS)
-        for b in LATE_BLOCKS:
-            look_up(3, (b,))
+        look_up_late(2, LATE_BLOCKS)
+        look_up_early(2, EARLY_BLOCKS)
+        look_up_early(3, (0,))
+        look_up_late(3, (2,))
+        look_up_early(3, (1,))
+        look_up_late(3, (3,))
 
-        row_sum = [sb("row_sum%d" % b, [P, 1], F32) for b in range(BLOCKS)]
+        row_sum = [sb("row_sum%d" % b, [P, 1], F32) for b in range(BLOCKS - 1)]
+        row_sum.append(keep.tile([P, 1], F32, name="row_sum3", tag="table2", align_bytes=64))
         err = sb("err", [P, R], F32)
-        e_banks = [bank(number, "e_bank%d" % b) for b, number in enumerate((4, 7, 5, 6))]
+        early_e = bank(4, "early_e")
+        late_e = bank(5, "late_e")
 
-        def spread_e(b):
+        def spread(e_bank, b, column, start, stop):
+            nc.tensor.matmul(e_bank[:, block(b)], lhsT=column[:].to_broadcast([P, P]), rhs=ident[:], is_transpose=True, start=start, stop=stop)
+
+        for b in LATE_BLOCKS:
+            spread(late_e, b, wtarget[b], b == LATE_BLOCKS[0], False)
+        for b in EARLY_BLOCKS:
             unread = spare.tile([P, D], F32, name="unread", tag="unread")
-            spread = e_banks[b][:, 0:P]
-            if b in EARLY_BLOCKS:
-                nc.scalar.activation(unread[:, 0:P], q_banks[b][:, 0:P], IDENTITY, scale=cols[:, WT + b : WT + b + 1], bias=share[b][:],
-                                     accum_out=row_sum[b][:])
-            else:
-                nc.vector.scalar_tensor_tensor(out=unread[:].rearrange("r (p t) -> r p t", t=PACK),
-                                               in0=q_banks[b][:].rearrange("r (t p) -> r p t", t=PACK), scalar=1.0,
-                                               in1=x_sb[b].rearrange("r (p t) -> r p t", t=PACK),
-                                               op0=ALU.mult, op1=ALU.mult, accum_out=row_sum[b][:])
-                nc.tensor.matmul(spread, lhsT=wtarget[b][:].to_broadcast([P, P]), rhs=ident[:], is_transpose=True, start=True, stop=False)
-            nc.tensor.matmul(spread, lhsT=row_sum[b][:].to_broadcast([P, P]), rhs=ident[:], is_transpose=True,
-                             start=(b in EARLY_BLOCKS), stop=True)
-            nc.scalar.copy(err[:, block(b)], spread)
+            nc.scalar.activation(unread[:, 0:P], q_banks[b][:, 0:P], IDENTITY, scale=cols[:, WT + b : WT + b + 1], bias=share[b][:],
+                                 accum_out=row_sum[b][:])
+            spread(early_e, b, row_sum[b], True, True)
+        nc.scalar.copy(err[:, span(EARLY_BLOCKS)], early_e[:, span(EARLY_BLOCKS)])
+        for b in LATE_BLOCKS:
+            unread = spare.tile([P, D], F32, name="unread", tag="unread")
+            nc.vector.scalar_tensor_tensor(out=unread[:].rearrange("r (p t) -> r p t", t=PACK),
+                                           in0=q_banks[b][:].rearrange("r (t p) -> r p t", t=PACK), scalar=cols[:, WT + b : WT + b + 1],
+                                           in1=x_sb[b].rearrange("r (p t) -> r p t", t=PACK),
+                                           op0=ALU.mult, op1=ALU.mult, accum_out=row_sum[b][:])
+            spread(late_e, b, row_sum[b], False, b == LATE_BLOCKS[-1])
+        nc.scalar.copy(err[:, span(LATE_BLOCKS)], late_e[:, span(LATE_BLOCKS)])
 
-        late_banks = {}
+        late_x = []
+        for number in (4, 5):
+            late_bank = bank(number, "late_bank%d" % number)
+            for half in range(2):
+                t = len(late_x)
+                late_x.append(late_bank[:, HALF * half : HALF * (half + 1)])
+                for n, b in enumerate(LATE_BLOCKS):
+                    nc.tensor.transpose(late_x[t][:, block(n)], x_sb[b].rearrange("r (p t) -> r t p", t=PACK)[:, t, :], ident[:])
 
-        def turn_late(t, number, blocks):
-            late_banks[t] = bank(number, "late_bank%d" % t)
-            for b in blocks:
-                nc.tensor.transpose(late_banks[t][:, block(b)], x_sb[b].rearrange("r (p t) -> r t p", t=PACK)[:, t, :], ident[:])
+        early_product = keep.tile([P, HALF], F32, name="early_product", tag="table3", align_bytes=64)
+        nc.vector.tensor_tensor(early_product[:], xT[1][:], err[:, span(EARLY_BLOCKS)], ALU.mult)
+        windows = {}
 
-        spread_e(0)
-        spread_e(1)
-        turn_x(0, LATE_BLOCKS, 0)
-        spread_e(2)
-        turn_late(1, 1, LATE_BLOCKS)
-        spread_e(3)
-        turn_late(2, 2, ALL_BLOCKS)
-        turn_x(3, LATE_BLOCKS, 3)
-
-        windows = [keep.tile([P, T], F32, name="window_%d" % t, tag="table%d" % t, align_bytes=64) for t in range(2)]
-        for t in range(2):
+        def clear(t):
+            windows[t] = keep.tile([P, T], F32, name="window_%d" % t, tag="table%d" % t, align_bytes=64)
             nc.gpsimd.memset(windows[t][:], 0.0)
-        windows = windows + own_windows
-        rounded = sb("rounded", [P, PACK, T], BF16)
+
+        for t in range(3):
+            clear(t)
         out_planes = out_0.rearrange("(p t) c -> t p c", t=PACK)
 
-        def entries(blocks):
-            return taken[:, LIST_COLUMNS * blocks[0] : LIST_COLUMNS * (blocks[-1] + 1)]
+        late_products = [sb("late_product%d" % t, [P, HALF], F32) for t in range(PACK)]
 
-        products = {}
-
-        def multiply(t, blocks, tag):
-            products[t, blocks[0]] = keep.tile([P, P * len(blocks)], F32, name="products%d_%d" % (t, blocks[0]), tag=tag, align_bytes=64)
-            turned = xT[t] if blocks == EARLY_BLOCKS else late_banks[t]
-            nc.vector.tensor_tensor(products[t, blocks[0]][:], turned[:, span(blocks)], err[:, span(blocks)], ALU.mult)
+        def multiply(t):
+            nc.vector.tensor_tensor(late_products[t][:], late_x[t], err[:, span(LATE_BLOCKS)], ALU.mult)
 
         def scatter(t, blocks, source):
-            nc.scalar.activation(windows[t][:].indirect(entries(blocks)), source, COPY)
+            nc.scalar.activation(windows[t][:].indirect(entries(blocks)), source[:], COPY)
 
-        def scatter_fused(t, blocks):
-            nc.vector.tensor_tensor(windows[t][:].indirect(entries(blocks)), xT[t][:, span(blocks)], err[:, span(blocks)], ALU.mult)
+        def scatter_fused(t):
+            nc.vector.tensor_tensor(windows[t][:].indirect(entries(EARLY_BLOCKS)), xT[t][:], err[:, span(EARLY_BLOCKS)], ALU.mult)
 
         def store(t):
             nc.sync.dma_start(out=out_planes[t], in_=windows[t][:])
@@ -276,23 +274,22 @@ def tile_attend_gtd_pl_kernel(tc, x2, x, w0, wT, us, ts, rw, wt, offs, aoffs, ou
             cut = slice(first * WIDTH, (first + count) * WIDTH)
             copy(rounded[:, t, cut], windows[t][:, cut])
 
-        multiply(1, EARLY_BLOCKS, "early_products")
-        scatter(1, EARLY_BLOCKS, products[1, 0][:])
-        scatter_fused(0, EARLY_BLOCKS)
-        multiply(1, LATE_BLOCKS, "late_products")
-        scatter(1, LATE_BLOCKS, products[1, EARLY][:])
-        store(1)
-        multiply(2, ALL_BLOCKS, "whole_products")
-        scatter_fused(0, LATE_BLOCKS)
-        store(0)
-        for blocks in (EARLY_BLOCKS, LATE_BLOCKS):
-            scatter(2, blocks, products[2, 0][:, span(blocks)])
-        store(2)
-        multiply(3, EARLY_BLOCKS, "early_products")
-        scatter_fused(3, LATE_BLOCKS)
-        scatter(3, EARLY_BLOCKS, products[3, 0][:])
-        store(3)
-        for t in (1, 0, 2):
+        scatter(1, EARLY_BLOCKS, early_product)
+        clear(3)
+        scatter_fused(0)
+        for t in range(3):
+            multiply(t)
+        for t in range(2):
+            scatter(t, LATE_BLOCKS, late_products[t])
+            store(t)
+        scatter_fused(2)
+        multiply(3)
+        scatter_fused(3)
+        for t in range(2, PACK):
+            scatter(t, LATE_BLOCKS, late_products[t])
+            store(t)
+        rounded = keep.tile([P, PACK, T], BF16, name="rounded", tag="turned3", align_bytes=64)
+        for t in range(3):
             round_plane(nc.vector.tensor_copy, t, 0, CHUNKS)
         round_plane(nc.scalar.copy, 3, 0, SCALAR_ROUNDS)
         round_plane(nc.vector.tensor_copy, 3, SCALAR_ROUNDS, CHUNKS - SCALAR_ROUNDS)
@@ -319,22 +316,24 @@ def tile_attend_gtd_pl_kernel(tc, x2, x, w0, wT, us, ts, rw, wt, offs, aoffs, ou
             cut = slice(first * WIDTH, (first + count) * WIDTH)
             nc.sync.dma_start(out=out_words[:, cut], in_=y_codes[:, cut].bitcast(I32))
 
-        for first in range(0, SCALAR_WEAVES, 2):
+        for first in range(0, 8, 2):
             weave(first, 2)
-        weave(8, 4)
-        weave(12, 2)
-        quantise(8, 4)
-        store_codes(8, 4)
-        weave(14, 2)
+        weave(8, 1)
+        weave(12, 4)
+        weave(9, 3)
+        quantise(12, 4)
+        store_codes(12, 4)
         quantise(0, 2)
         quantise(2, 2)
         store_codes(0, 4)
-        quantise(12, 2)
-        quantise(14, 2)
-        store_codes(12, 4)
+        quantise(9, 1)
+        quantise(10, 2)
+        store_codes(9, 3)
         quantise(4, 2)
         quantise(6, 2)
         store_codes(4, 4)
+        quantise(8, 1)
+        store_codes(8, 1)
         out_scales = out_2[0].bitcast(I32).rearrange("f (g c) -> g f c", g=4)
         for quad in range(4):
             queue = nc.scalar if quad % 2 else nc.sync

@@ -31,7 +31,7 @@ ALL_BLOCKS = tuple(range(BLOCKS))
 WIDTH = 128
 CHUNKS = T // WIDTH
 SCALAR_ROUNDS = 6
-SCALAR_WEAVES = 9
+SCALAR_WEAVES = 8
 RUN = 4
 SCALE_CHUNKS = CHUNKS // 4
 US, RW, WT = 0, BLOCKS, 2 * BLOCKS
@@ -91,6 +91,10 @@ def tile_attend_gtd_pl_kernel(tc, x2, x, w0, wT, us, ts, rw, wt, offs, aoffs, ou
 
         ident = sb("ident", [P, P], F32)
         make_identity(nc, ident[:])
+        windows = {}
+        for t in range(2, PACK):
+            windows[t] = sb("window_%d" % t, [P, T], F32)
+            nc.gpsimd.memset(windows[t][:], 0.0)
 
         ts_all = sb("ts_all", [P, T], F32)
         ts_view = ts_all[:].rearrange("q (p g m) -> q p g m", g=4, m=4)
@@ -106,7 +110,7 @@ def tile_attend_gtd_pl_kernel(tc, x2, x, w0, wT, us, ts, rw, wt, offs, aoffs, ou
         cols = sb("cols", [P, 3 * BLOCKS], F32)
         nc.scalar.activation(cols[:], vec_bank[:, 0 : 3 * BLOCKS], COPY)
 
-        xT = [keep.tile([P, HALF], F32, name="xT%d" % t, tag="turned%d" % t, align_bytes=64) for t in range(PACK)]
+        xT = [sb("xT%d" % t, [P, HALF], F32) for t in range(PACK)]
         slope = sb("slope", [P, BLOCKS], F32)
         nc.vector.tensor_scalar(out=slope[:], in0=cols[:, WT : WT + BLOCKS], scalar1=-DISCOUNT, scalar2=None, op0=ALU.mult)
         base = sb("base", [P, BLOCKS], F32)
@@ -209,8 +213,7 @@ def tile_attend_gtd_pl_kernel(tc, x2, x, w0, wT, us, ts, rw, wt, offs, aoffs, ou
         look_up_early(3, (1,))
         look_up_late(3, (3,))
 
-        row_sum = [sb("row_sum%d" % b, [P, 1], F32) for b in range(BLOCKS - 1)]
-        row_sum.append(keep.tile([P, 1], F32, name="row_sum3", tag="table2", align_bytes=64))
+        row_sum = [sb("row_sum%d" % b, [P, 1], F32) for b in range(BLOCKS)]
         err = sb("err", [P, R], F32)
         early_e = bank(4, "early_e")
         late_e = bank(5, "late_e")
@@ -235,37 +238,27 @@ def tile_attend_gtd_pl_kernel(tc, x2, x, w0, wT, us, ts, rw, wt, offs, aoffs, ou
             spread(late_e, b, row_sum[b], False, b == LATE_BLOCKS[-1])
         nc.scalar.copy(err[:, span(LATE_BLOCKS)], late_e[:, span(LATE_BLOCKS)])
 
-        late_x = []
-        for number in (4, 5):
-            late_bank = bank(number, "late_bank%d" % number)
-            for half in range(2):
-                t = len(late_x)
-                late_x.append(late_bank[:, HALF * half : HALF * (half + 1)])
-                for n, b in enumerate(LATE_BLOCKS):
-                    nc.tensor.transpose(late_x[t][:, block(n)], x_sb[b].rearrange("r (p t) -> r t p", t=PACK)[:, t, :], ident[:])
+        def turn_into(target, t, blocks):
+            for n, b in enumerate(blocks):
+                nc.tensor.transpose(target[:, block(n)], x_sb[b].rearrange("r (p t) -> r t p", t=PACK)[:, t, :], ident[:])
 
-        early_product = keep.tile([P, HALF], F32, name="early_product", tag="table3", align_bytes=64)
+        late_bank = bank(3, "late_bank")
+        for t in range(2):
+            turn_into(late_bank[:, HALF * t : HALF * (t + 1)], t, LATE_BLOCKS)
+        whole_banks = {}
+        for t in range(2, PACK):
+            whole_banks[t] = bank(2 + t, "whole_bank%d" % t)
+            turn_into(whole_banks[t], t, ALL_BLOCKS)
+
+        early_product = sb("early_product", [P, HALF], F32)
         nc.vector.tensor_tensor(early_product[:], xT[1][:], err[:, span(EARLY_BLOCKS)], ALU.mult)
-        windows = {}
-
-        def clear(t):
+        for t in range(2):
             windows[t] = keep.tile([P, T], F32, name="window_%d" % t, tag="table%d" % t, align_bytes=64)
             nc.gpsimd.memset(windows[t][:], 0.0)
-
-        for t in range(3):
-            clear(t)
         out_planes = out_0.rearrange("(p t) c -> t p c", t=PACK)
 
-        late_products = [sb("late_product%d" % t, [P, HALF], F32) for t in range(PACK)]
-
-        def multiply(t):
-            nc.vector.tensor_tensor(late_products[t][:], late_x[t], err[:, span(LATE_BLOCKS)], ALU.mult)
-
         def scatter(t, blocks, source):
-            nc.scalar.activation(windows[t][:].indirect(entries(blocks)), source[:], COPY)
-
-        def scatter_fused(t):
-            nc.vector.tensor_tensor(windows[t][:].indirect(entries(EARLY_BLOCKS)), xT[t][:], err[:, span(EARLY_BLOCKS)], ALU.mult)
+            nc.scalar.activation(windows[t][:].indirect(entries(blocks)), source, COPY)
 
         def store(t):
             nc.sync.dma_start(out=out_planes[t], in_=windows[t][:])
@@ -274,22 +267,28 @@ def tile_attend_gtd_pl_kernel(tc, x2, x, w0, wT, us, ts, rw, wt, offs, aoffs, ou
             cut = slice(first * WIDTH, (first + count) * WIDTH)
             copy(rounded[:, t, cut], windows[t][:, cut])
 
-        scatter(1, EARLY_BLOCKS, early_product)
-        clear(3)
-        scatter_fused(0)
-        for t in range(3):
-            multiply(t)
+        scatter(1, EARLY_BLOCKS, early_product[:])
+        nc.vector.tensor_tensor(windows[0][:].indirect(entries(EARLY_BLOCKS)), xT[0][:], err[:, span(EARLY_BLOCKS)], ALU.mult)
         for t in range(2):
-            scatter(t, LATE_BLOCKS, late_products[t])
+            late_product = sb("late_product%d" % t, [P, HALF], F32)
+            nc.vector.tensor_tensor(late_product[:], late_bank[:, HALF * t : HALF * (t + 1)], err[:, span(LATE_BLOCKS)], ALU.mult)
+            scatter(t, LATE_BLOCKS, late_product[:])
             store(t)
-        scatter_fused(2)
-        multiply(3)
-        scatter_fused(3)
-        for t in range(2, PACK):
-            scatter(t, LATE_BLOCKS, late_products[t])
-            store(t)
-        rounded = keep.tile([P, PACK, T], BF16, name="rounded", tag="turned3", align_bytes=64)
-        for t in range(3):
+        rounded = sb("rounded", [P, PACK, T], BF16)
+        product = sb("product2", [P, R], F32)
+        nc.vector.tensor_tensor(product[:], whole_banks[2][:], err[:], ALU.mult)
+        nc.vector.tensor_copy(windows[2][:].indirect(entries(EARLY_BLOCKS)), product[:, span(EARLY_BLOCKS)])
+        scatter(2, LATE_BLOCKS, product[:, span(LATE_BLOCKS)])
+        store(2)
+        last_early = rounded[:, 1, 0 : 2 * HALF].bitcast(F32)
+        last_late = sb("last_late", [P, HALF], F32)
+        for target, blocks in ((last_early, EARLY_BLOCKS), (last_late[:], LATE_BLOCKS)):
+            nc.vector.tensor_tensor(target, whole_banks[3][:, span(blocks)], err[:, span(blocks)], ALU.mult)
+        nc.vector.tensor_copy(windows[3][:].indirect(entries(EARLY_BLOCKS)), last_early)
+        scatter(3, LATE_BLOCKS, last_late[:])
+        store(3)
+        nc.gpsimd.tensor_scalar(out=rounded[:, 0, :], in0=windows[0][:], scalar1=1.0, scalar2=-0.0, op0=ALU.mult, op1=ALU.add)
+        for t in range(1, 3):
             round_plane(nc.vector.tensor_copy, t, 0, CHUNKS)
         round_plane(nc.scalar.copy, 3, 0, SCALAR_ROUNDS)
         round_plane(nc.vector.tensor_copy, 3, SCALAR_ROUNDS, CHUNKS - SCALAR_ROUNDS)
@@ -316,24 +315,22 @@ def tile_attend_gtd_pl_kernel(tc, x2, x, w0, wT, us, ts, rw, wt, offs, aoffs, ou
             cut = slice(first * WIDTH, (first + count) * WIDTH)
             nc.sync.dma_start(out=out_words[:, cut], in_=y_codes[:, cut].bitcast(I32))
 
-        for first in range(0, 8, 2):
+        for first in range(0, SCALAR_WEAVES, 2):
             weave(first, 2)
-        weave(8, 1)
-        weave(12, 4)
-        weave(9, 3)
-        quantise(12, 4)
-        store_codes(12, 4)
+        weave(8, 4)
+        weave(12, 2)
+        quantise(8, 4)
+        store_codes(8, 4)
+        weave(14, 2)
         quantise(0, 2)
         quantise(2, 2)
         store_codes(0, 4)
-        quantise(9, 1)
-        quantise(10, 2)
-        store_codes(9, 3)
+        quantise(12, 2)
+        quantise(14, 2)
+        store_codes(12, 4)
         quantise(4, 2)
         quantise(6, 2)
         store_codes(4, 4)
-        quantise(8, 1)
-        store_codes(8, 1)
         out_scales = out_2[0].bitcast(I32).rearrange("f (g c) -> g f c", g=4)
         for quad in range(4):
             queue = nc.scalar if quad % 2 else nc.sync

@@ -91,10 +91,6 @@ def tile_attend_gtd_pl_kernel(tc, x2, x, w0, wT, us, ts, rw, wt, offs, aoffs, ou
 
         ident = sb("ident", [P, P], F32)
         make_identity(nc, ident[:])
-        windows = {}
-        for t in range(2, PACK):
-            windows[t] = sb("window_%d" % t, [P, T], F32)
-            nc.gpsimd.memset(windows[t][:], 0.0)
 
         ts_all = sb("ts_all", [P, T], F32)
         ts_view = ts_all[:].rearrange("q (p g m) -> q p g m", g=4, m=4)
@@ -252,7 +248,8 @@ def tile_attend_gtd_pl_kernel(tc, x2, x, w0, wT, us, ts, rw, wt, offs, aoffs, ou
 
         early_product = sb("early_product", [P, HALF], F32)
         nc.vector.tensor_tensor(early_product[:], xT[1][:], err[:, span(EARLY_BLOCKS)], ALU.mult)
-        for t in range(2):
+        windows = {}
+        for t in range(PACK):
             windows[t] = keep.tile([P, T], F32, name="window_%d" % t, tag="table%d" % t, align_bytes=64)
             nc.gpsimd.memset(windows[t][:], 0.0)
         out_planes = out_0.rearrange("(p t) c -> t p c", t=PACK)

@@ -56,8 +56,8 @@ def tile_attend_gtd_pl_kernel(tc, x2, x, w0, wT, us, ts, rw, wt, offs, aoffs, ou
         def sb(name, shape, dtype):
             return keep.tile(shape, dtype, name=name, align_bytes=64)
 
-        def bank(number, name):
-            return psum.tile([P, 512], F32, name=name, tag="b%d" % number)
+        def bank(number, name, count=1):
+            return psum.tile([P, 512 * count], F32, name=name, offset=2048 * number)
 
         slots = lists.tile([P, I // 16], U16, name="slots")
         taken = lists.tile([P, R // 16], U16, name="taken")
@@ -211,28 +211,25 @@ def tile_attend_gtd_pl_kernel(tc, x2, x, w0, wT, us, ts, rw, wt, offs, aoffs, ou
 
         row_sum = [sb("row_sum%d" % b, [P, 1], F32) for b in range(BLOCKS)]
         err = sb("err", [P, R], F32)
-        early_e = bank(4, "early_e")
-        late_e = bank(5, "late_e")
+        e_banks = [bank(number, "e_bank%d" % b) for b, number in enumerate((0, 1, 4))] + [bank(5, "e_bank3", count=3)]
 
-        def spread(e_bank, b, column, start, stop):
-            nc.tensor.matmul(e_bank[:, block(b)], lhsT=column[:].to_broadcast([P, P]), rhs=ident[:], is_transpose=True, start=start, stop=stop)
+        def spread(b, column, start, stop):
+            nc.tensor.matmul(e_banks[b][:, 0:P], lhsT=column[:].to_broadcast([P, P]), rhs=ident[:], is_transpose=True, start=start, stop=stop)
 
         for b in LATE_BLOCKS:
-            spread(late_e, b, wtarget[b], b == LATE_BLOCKS[0], False)
-        for b in EARLY_BLOCKS:
+            spread(b, wtarget[b], True, False)
+        for b in ALL_BLOCKS:
             unread = spare.tile([P, D], F32, name="unread", tag="unread")
-            nc.scalar.activation(unread[:, 0:P], q_banks[b][:, 0:P], IDENTITY, scale=cols[:, WT + b : WT + b + 1], bias=share[b][:],
-                                 accum_out=row_sum[b][:])
-            spread(early_e, b, row_sum[b], True, True)
-        nc.scalar.copy(err[:, span(EARLY_BLOCKS)], early_e[:, span(EARLY_BLOCKS)])
-        for b in LATE_BLOCKS:
-            unread = spare.tile([P, D], F32, name="unread", tag="unread")
-            nc.vector.scalar_tensor_tensor(out=unread[:].rearrange("r (p t) -> r p t", t=PACK),
-                                           in0=q_banks[b][:].rearrange("r (t p) -> r p t", t=PACK), scalar=cols[:, WT + b : WT + b + 1],
-                                           in1=x_sb[b].rearrange("r (p t) -> r p t", t=PACK),
-                                           op0=ALU.mult, op1=ALU.mult, accum_out=row_sum[b][:])
-            spread(late_e, b, row_sum[b], False, b == LATE_BLOCKS[-1])
-        nc.scalar.copy(err[:, span(LATE_BLOCKS)], late_e[:, span(LATE_BLOCKS)])
+            if b in EARLY_BLOCKS:
+                nc.scalar.activation(unread[:, 0:P], q_banks[b][:, 0:P], IDENTITY, scale=cols[:, WT + b : WT + b + 1], bias=share[b][:],
+                                     accum_out=row_sum[b][:])
+            else:
+                nc.vector.scalar_tensor_tensor(out=unread[:].rearrange("r (p t) -> r p t", t=PACK),
+                                               in0=q_banks[b][:].rearrange("r (t p) -> r p t", t=PACK), scalar=cols[:, WT + b : WT + b + 1],
+                                               in1=x_sb[b].rearrange("r (p t) -> r p t", t=PACK),
+                                               op0=ALU.mult, op1=ALU.mult, accum_out=row_sum[b][:])
+            spread(b, row_sum[b], b in EARLY_BLOCKS, True)
+            nc.scalar.copy(err[:, block(b)], e_banks[b][:, 0:P])
 
         def turn_into(target, t, blocks):
             for n, b in enumerate(blocks):
@@ -241,9 +238,8 @@ def tile_attend_gtd_pl_kernel(tc, x2, x, w0, wT, us, ts, rw, wt, offs, aoffs, ou
         late_bank = bank(3, "late_bank")
         for t in range(2):
             turn_into(late_bank[:, HALF * t : HALF * (t + 1)], t, LATE_BLOCKS)
-        whole_banks = {}
+        whole_banks = {t: bank(4 + t, "whole_bank%d" % t) for t in range(2, PACK)}
         for t in range(2, PACK):
-            whole_banks[t] = bank(2 + t, "whole_bank%d" % t)
             turn_into(whole_banks[t], t, ALL_BLOCKS)
 
         early_product = sb("early_product", [P, HALF], F32)

@@ -32,6 +32,7 @@ WIDTH = 128
 CHUNKS = T // WIDTH
 SCALAR_ROUNDS = 6
 SCALAR_WEAVES = 8
+GPSIMD_ROUNDS = 4
 RUN = 4
 SCALE_CHUNKS = CHUNKS // 4
 US, RW, WT = 0, BLOCKS, 2 * BLOCKS
@@ -63,14 +64,15 @@ def tile_attend_gtd_pl_kernel(tc, x2, x, w0, wT, us, ts, rw, wt, offs, aoffs, ou
         taken = lists.tile([P, R // 16], U16, name="taken")
         vecs = sb("vecs", [P, P], F32)
         nc.vector.memset(vecs[:], 0.0)
-        ts_cut = sb("ts_cut", [P, T // P], F32)
+        ts_rows = sb("ts_rows", [P, P], F32)
+        nc.vector.memset(ts_rows[:], 0.0)
 
         w0_planes = w0.rearrange("(p t) c -> t p c", t=PACK)
         w0_sb = [sb("w0_%d" % t, [P, T], F32) for t in range(PACK)]
         for t in range(PACK):
             nc.sync.dma_start(out=w0_sb[t][:], in_=w0_planes[t])
             if t == 0:
-                nc.sync.dma_start(out=ts_cut[:], in_=ts[0].rearrange("(p m) -> p m", m=T // P))
+                nc.sync.dma_start(out=ts_rows[0 : T // P, :], in_=ts[0].rearrange("(m p) -> m p", p=P))
                 nc.sync.dma_start(slots[:], offs)
                 for first, vec in ((US, us), (RW, rw), (WT, wt)):
                     nc.sync.dma_start(out=vecs[first : first + BLOCKS, :], in_=vec.rearrange("(b p) o -> b (p o)", p=P))
@@ -85,7 +87,7 @@ def tile_attend_gtd_pl_kernel(tc, x2, x, w0, wT, us, ts, rw, wt, offs, aoffs, ou
         for t in range(PACK):
             nc.sync.dma_start(out=wT_sb[t][:], in_=wT_planes[t])
             if t == 0:
-                nc.sync.dma_start(out=x_early[:], in_=x[span(EARLY_BLOCKS), :].rearrange("(b p) d -> p b d", p=P))
+                nc.sync.dma_start(out=x_early[:], in_=x[span(EARLY_BLOCKS), :].rearrange("(p b) d -> p b d", p=P))
         for b in LATE_BLOCKS:
             nc.sync.dma_start(out=x_sb[b], in_=x[block(b), :])
 
@@ -93,13 +95,16 @@ def tile_attend_gtd_pl_kernel(tc, x2, x, w0, wT, us, ts, rw, wt, offs, aoffs, ou
         make_identity(nc, ident[:])
 
         ts_all = sb("ts_all", [P, T], F32)
-        ts_view = ts_all[:].rearrange("q (p g m) -> q p g m", g=4, m=4)
+        cut_bank = bank(5, "cut_bank")
+        nc.tensor.transpose(cut_bank[:, 0:P], ts_rows[:], ident[:])
+        ts_cut = sb("ts_cut", [P, T // P], F32)
+        nc.scalar.activation(ts_cut[:], cut_bank[:, 0 : T // P], COPY)
         for g in range(4):
             ts_bank = bank(g, "ts_bank%d" % g)
             for m in range(4):
                 col = 4 * g + m
                 nc.tensor.transpose(ts_bank[:, block(m)], ts_cut[:, col : col + 1].to_broadcast([P, P]), ident[:])
-            nc.scalar.activation(ts_view[:, :, g, :], ts_bank[:].rearrange("q (m p) -> q p m", m=4), COPY)
+            nc.scalar.activation(ts_all[:, 512 * g : 512 * (g + 1)], ts_bank[:], COPY)
 
         vec_bank = bank(4, "vec_bank")
         nc.tensor.transpose(vec_bank[:, 0:P], vecs[:], ident[:])
@@ -139,11 +144,17 @@ def tile_attend_gtd_pl_kernel(tc, x2, x, w0, wT, us, ts, rw, wt, offs, aoffs, ou
             cut = slice(HALF * h, HALF * (h + 1))
             nc.vector.quantize_mx(out=x2_codes[:, cut].bitcast(FP8X4), scales=x2_scales[:, cut], in_=x2_bf[h][:].rearrange("p r t -> p (r t)"))
 
+        def in_pairs(ap):
+            return ap.rearrange("q (p j) -> q p j", j=EARLY)
+
+        def turned_early(tile):
+            return tile[:, 0:HALF].rearrange("q (j p) -> q p j", j=EARLY)
+
         def turn_x(t, blocks, number):
             xt_bank = bank(number, "xt_bank%d_%d" % (t, blocks[0]))
             for b in blocks:
                 nc.tensor.transpose(xt_bank[:, block(b)], x_sb[b].rearrange("r (p t) -> r t p", t=PACK)[:, t, :], ident[:])
-            nc.scalar.copy(xT[t][:, span(blocks)], xt_bank[:, span(blocks)])
+            nc.scalar.copy(in_pairs(xT[t][:]), turned_early(xt_bank))
 
         largest = sb("largest", [P, BLOCKS], F32)
         row_banks = [bank(4 + b, "row_bank%d" % b) for b in range(2)]
@@ -269,20 +280,25 @@ def tile_attend_gtd_pl_kernel(tc, x2, x, w0, wT, us, ts, rw, wt, offs, aoffs, ou
             store(t)
         rounded = sb("rounded", [P, PACK, T], BF16)
         product = sb("product2", [P, R], F32)
-        nc.vector.tensor_tensor(product[:], whole_banks[2][:], err[:], ALU.mult)
+        nc.vector.tensor_tensor(in_pairs(product[:, span(EARLY_BLOCKS)]), turned_early(whole_banks[2]), in_pairs(err[:, span(EARLY_BLOCKS)]), ALU.mult)
+        nc.vector.tensor_tensor(product[:, span(LATE_BLOCKS)], whole_banks[2][:, span(LATE_BLOCKS)], err[:, span(LATE_BLOCKS)], ALU.mult)
         nc.vector.tensor_copy(windows[2][:].indirect(entries(EARLY_BLOCKS)), product[:, span(EARLY_BLOCKS)])
         scatter(2, LATE_BLOCKS, product[:, span(LATE_BLOCKS)])
         store(2)
         last_early = rounded[:, 1, 0 : 2 * HALF].bitcast(F32)
         last_late = sb("last_late", [P, HALF], F32)
-        for target, blocks in ((last_early, EARLY_BLOCKS), (last_late[:], LATE_BLOCKS)):
-            nc.vector.tensor_tensor(target, whole_banks[3][:, span(blocks)], err[:, span(blocks)], ALU.mult)
+        nc.vector.tensor_tensor(in_pairs(last_early), turned_early(whole_banks[3]), in_pairs(err[:, span(EARLY_BLOCKS)]), ALU.mult)
+        nc.vector.tensor_tensor(last_late[:], whole_banks[3][:, span(LATE_BLOCKS)], err[:, span(LATE_BLOCKS)], ALU.mult)
         nc.vector.tensor_copy(windows[3][:].indirect(entries(EARLY_BLOCKS)), last_early)
         scatter(3, LATE_BLOCKS, last_late[:])
         store(3)
-        nc.gpsimd.tensor_scalar(out=rounded[:, 0, :], in0=windows[0][:], scalar1=1.0, scalar2=-0.0, op0=ALU.mult, op1=ALU.add)
-        for t in range(1, 3):
-            round_plane(nc.vector.tensor_copy, t, 0, CHUNKS)
+        def gpsimd_copy(out, in_):
+            nc.gpsimd.tensor_scalar(out=out, in0=in_, scalar1=1.0, scalar2=-0.0, op0=ALU.mult, op1=ALU.add)
+
+        round_plane(gpsimd_copy, 0, 0, CHUNKS)
+        round_plane(gpsimd_copy, 1, CHUNKS - GPSIMD_ROUNDS, GPSIMD_ROUNDS)
+        round_plane(nc.vector.tensor_copy, 1, 0, CHUNKS - GPSIMD_ROUNDS)
+        round_plane(nc.vector.tensor_copy, 2, 0, CHUNKS)
         round_plane(nc.scalar.copy, 3, 0, SCALAR_ROUNDS)
         round_plane(nc.vector.tensor_copy, 3, SCALAR_ROUNDS, CHUNKS - SCALAR_ROUNDS)
 

@@ -69,13 +69,19 @@ def tile_attend_gtd_pl_kernel(tc, x2, x, w0, wT, us, ts, rw, wt, offs, aoffs, ou
 
         w0_planes = w0.rearrange("(p t) c -> t p c", t=PACK)
         w0_sb = [sb("w0_%d" % t, [P, T], F32) for t in range(PACK)]
-        for t in range(PACK):
-            nc.sync.dma_start(out=w0_sb[t][:], in_=w0_planes[t])
-            if t == 0:
-                nc.sync.dma_start(out=ts_rows[0 : T // P, :], in_=ts[0].rearrange("(m p) -> m p", p=P))
-                nc.sync.dma_start(slots[:], offs)
-                for first, vec in ((US, us), (RW, rw), (WT, wt)):
-                    nc.sync.dma_start(out=vecs[first : first + BLOCKS, :], in_=vec.rearrange("(b p) o -> b (p o)", p=P))
+
+        def load_vector(first, vec):
+            nc.sync.dma_start(out=vecs[first : first + BLOCKS, :], in_=vec.rearrange("(b p) o -> b (p o)", p=P))
+
+        nc.sync.dma_start(out=w0_sb[0][:], in_=w0_planes[0])
+        nc.sync.dma_start(out=ts_rows[0 : T // P, :], in_=ts[0].rearrange("(m p) -> m p", p=P))
+        nc.sync.dma_start(slots[:], offs)
+        nc.sync.dma_start(out=w0_sb[1][:], in_=w0_planes[1])
+        load_vector(US, us)
+        load_vector(RW, rw)
+        nc.sync.dma_start(out=w0_sb[2][:], in_=w0_planes[2])
+        load_vector(WT, wt)
+        nc.sync.dma_start(out=w0_sb[3][:], in_=w0_planes[3])
         nc.sync.dma_start(taken[:], aoffs)
         x2_sb = sb("x2_sb", [P, PACK, R], F32)
         nc.sync.dma_start(out=x2_sb[:], in_=x2.rearrange("(p t) r -> p t r", t=PACK))

@@ -30,9 +30,9 @@ LATE_BLOCKS = tuple(range(EARLY, BLOCKS))
 ALL_BLOCKS = tuple(range(BLOCKS))
 WIDTH = 128
 CHUNKS = T // WIDTH
-SCALAR_ROUNDS = 6
+SCALAR_ROUNDS = 12
 SCALAR_WEAVES = 8
-GPSIMD_ROUNDS = 4
+GPSIMD_ROUNDS = 10
 RUN = 4
 SCALE_CHUNKS = CHUNKS // 4
 US, RW, WT = 0, BLOCKS, 2 * BLOCKS
@@ -117,7 +117,7 @@ def tile_attend_gtd_pl_kernel(tc, x2, x, w0, wT, us, ts, rw, wt, offs, aoffs, ou
         cols = sb("cols", [P, 3 * BLOCKS], F32)
         nc.scalar.activation(cols[:], vec_bank[:, 0 : 3 * BLOCKS], COPY)
 
-        xT = [sb("xT%d" % t, [P, HALF], F32) for t in range(PACK)]
+        xT = [keep.tile([P, HALF], F32, name="xT%d" % t, tag="xT%d" % t, align_bytes=64) for t in range(PACK)]
         slope = sb("slope", [P, BLOCKS], F32)
         nc.vector.tensor_scalar(out=slope[:], in0=cols[:, WT : WT + BLOCKS], scalar1=-DISCOUNT, scalar2=None, op0=ALU.mult)
         base = sb("base", [P, BLOCKS], F32)
@@ -142,7 +142,7 @@ def tile_attend_gtd_pl_kernel(tc, x2, x, w0, wT, us, ts, rw, wt, offs, aoffs, ou
 
         x2_codes = sb("x2_codes", [P, R], U32)
         x2_scales = sb("x2_scales", [P, R], U8)
-        x2_bf = [sb("x2_bf%d" % h, [P, HALF, PACK], BF16) for h in range(2)]
+        x2_bf = [keep.tile([P, HALF, PACK], BF16, name="x2_bf%d" % h, tag="x2_bf%d" % h, align_bytes=64) for h in range(2)]
         for h, copy in enumerate((nc.vector.tensor_copy, nc.scalar.copy)):
             src = x2_sb[:, :, HALF * h : HALF * (h + 1)].rearrange("p t (c i) -> p c t i", i=4)
             copy(x2_bf[h][:].rearrange("p (c i) t -> p c t i", i=4), src)
@@ -168,7 +168,7 @@ def tile_attend_gtd_pl_kernel(tc, x2, x, w0, wT, us, ts, rw, wt, offs, aoffs, ou
             nc.tensor.matmul_mx(out=row_banks[b][:], lhsT=x2_codes[:, block(b)].bitcast(FP8X4), lhsT_scale=x2_scales[:, block(b)],
                                 rhs=w0_codes[:].bitcast(FP8X4), rhs_scale=w0_scales[:], start=True, stop=True)
         turn_x(0, EARLY_BLOCKS, 6)
-        scaled_rows = sb("scaled_rows", [P, 2, I], F32)
+        scaled_rows = keep.tile([P, 2, I], F32, name="scaled_rows", tag="scaled_rows", align_bytes=64)
         for b in range(2):
             nc.vector.scalar_tensor_tensor(out=scaled_rows[:, b, :], in0=row_banks[b][:], scalar=cols[:, US + b : US + b + 1],
                                            in1=ts_listed[:], op0=ALU.mult, op1=ALU.mult)
@@ -252,18 +252,17 @@ def tile_attend_gtd_pl_kernel(tc, x2, x, w0, wT, us, ts, rw, wt, offs, aoffs, ou
             for n, b in enumerate(blocks):
                 nc.tensor.transpose(target[:, block(n)], x_sb[b].rearrange("r (p t) -> r t p", t=PACK)[:, t, :], ident[:])
 
-        late_bank = bank(3, "late_bank")
-        for t in range(2):
-            turn_into(late_bank[:, HALF * t : HALF * (t + 1)], t, LATE_BLOCKS)
-        whole_banks = {t: bank(4 + t, "whole_bank%d" % t) for t in range(2, PACK)}
-        for t in range(2, PACK):
-            turn_into(whole_banks[t], t, ALL_BLOCKS)
+        late_banks = [bank(3, "late_bank0"), bank(6, "late_bank1")]
+        late_order = (0, 3, 1, 2)
+        late_x = {t: late_banks[n // 2][:, HALF * (n % 2) : HALF * (n % 2 + 1)] for n, t in enumerate(late_order)}
+        for t in late_order:
+            turn_into(late_x[t], t, LATE_BLOCKS)
 
         early_product = sb("early_product", [P, HALF], F32)
         nc.vector.tensor_tensor(early_product[:], xT[1][:], err[:, span(EARLY_BLOCKS)], ALU.mult)
         windows = {}
-        for t in range(PACK):
-            windows[t] = keep.tile([P, T], F32, name="window_%d" % t, tag="table%d" % t, align_bytes=64)
+        for t, tag in zip((0, 1, 3, 2), ("x2_bf1", "scaled_rows", "table0", "table1")):
+            windows[t] = keep.tile([P, T], F32, name="window_%d" % t, tag=tag, align_bytes=64)
             nc.gpsimd.memset(windows[t][:], 0.0)
         out_planes = out_0.rearrange("(p t) c -> t p c", t=PACK)
 
@@ -279,33 +278,34 @@ def tile_attend_gtd_pl_kernel(tc, x2, x, w0, wT, us, ts, rw, wt, offs, aoffs, ou
 
         scatter(1, EARLY_BLOCKS, early_product[:])
         nc.vector.tensor_tensor(windows[0][:].indirect(entries(EARLY_BLOCKS)), xT[0][:], err[:, span(EARLY_BLOCKS)], ALU.mult)
-        for t in range(2):
-            late_product = sb("late_product%d" % t, [P, HALF], F32)
-            nc.vector.tensor_tensor(late_product[:], late_bank[:, HALF * t : HALF * (t + 1)], err[:, span(LATE_BLOCKS)], ALU.mult)
-            scatter(t, LATE_BLOCKS, late_product[:])
-            store(t)
         rounded = sb("rounded", [P, PACK, T], BF16)
-        product = sb("product2", [P, R], F32)
-        nc.vector.tensor_tensor(in_pairs(product[:, span(EARLY_BLOCKS)]), turned_early(whole_banks[2]), in_pairs(err[:, span(EARLY_BLOCKS)]), ALU.mult)
-        nc.vector.tensor_tensor(product[:, span(LATE_BLOCKS)], whole_banks[2][:, span(LATE_BLOCKS)], err[:, span(LATE_BLOCKS)], ALU.mult)
-        nc.vector.tensor_copy(windows[2][:].indirect(entries(EARLY_BLOCKS)), product[:, span(EARLY_BLOCKS)])
-        scatter(2, LATE_BLOCKS, product[:, span(LATE_BLOCKS)])
-        store(2)
-        last_early = rounded[:, 1, 0 : 2 * HALF].bitcast(F32)
-        last_late = sb("last_late", [P, HALF], F32)
-        nc.vector.tensor_tensor(in_pairs(last_early), turned_early(whole_banks[3]), in_pairs(err[:, span(EARLY_BLOCKS)]), ALU.mult)
-        nc.vector.tensor_tensor(last_late[:], whole_banks[3][:, span(LATE_BLOCKS)], err[:, span(LATE_BLOCKS)], ALU.mult)
-        nc.vector.tensor_copy(windows[3][:].indirect(entries(EARLY_BLOCKS)), last_early)
-        scatter(3, LATE_BLOCKS, last_late[:])
+        product2 = rounded[:].rearrange("p t c -> p (t c)")[:, 2 * T - R : 2 * T + R].bitcast(F32)
+        early3 = keep.tile([P, HALF], F32, name="early3", tag="xT1", align_bytes=64)
+        nc.gpsimd.tensor_tensor(early3[:], xT[3][:], err[:, span(EARLY_BLOCKS)], ALU.mult)
+        nc.gpsimd.tensor_tensor(product2[:, span(EARLY_BLOCKS)], xT[2][:], err[:, span(EARLY_BLOCKS)], ALU.mult)
+        late_products = [sb("late_product%d" % t, [P, HALF], F32)[:] for t in range(2)]
+        late_products += [product2[:, span(LATE_BLOCKS)], sb("late_product3", [P, HALF], F32)[:]]
+        for t in late_order:
+            nc.vector.tensor_tensor(late_products[t], late_x[t], err[:, span(LATE_BLOCKS)], ALU.mult)
+        scatter(0, LATE_BLOCKS, late_products[0])
+        store(0)
+        nc.vector.tensor_copy(windows[1][:].indirect(entries(LATE_BLOCKS)), late_products[1])
+        store(1)
+        scatter(3, LATE_BLOCKS, late_products[3])
+        scatter(3, EARLY_BLOCKS, early3[:])
         store(3)
+        nc.vector.tensor_copy(windows[2][:].indirect(taken[:]), product2)
+        store(2)
+
         def gpsimd_copy(out, in_):
             nc.gpsimd.tensor_scalar(out=out, in0=in_, scalar1=1.0, scalar2=-0.0, op0=ALU.mult, op1=ALU.add)
 
         round_plane(gpsimd_copy, 0, 0, CHUNKS)
-        round_plane(gpsimd_copy, 1, CHUNKS - GPSIMD_ROUNDS, GPSIMD_ROUNDS)
-        round_plane(nc.vector.tensor_copy, 1, 0, CHUNKS - GPSIMD_ROUNDS)
+        round_plane(gpsimd_copy, 1, 0, GPSIMD_ROUNDS)
+        round_plane(nc.scalar.copy, 3, SCALAR_WEAVES, SCALAR_ROUNDS - SCALAR_WEAVES)
+        round_plane(nc.scalar.copy, 3, 0, SCALAR_WEAVES)
         round_plane(nc.vector.tensor_copy, 2, 0, CHUNKS)
-        round_plane(nc.scalar.copy, 3, 0, SCALAR_ROUNDS)
+        round_plane(nc.vector.tensor_copy, 1, GPSIMD_ROUNDS, CHUNKS - GPSIMD_ROUNDS)
         round_plane(nc.vector.tensor_copy, 3, SCALAR_ROUNDS, CHUNKS - SCALAR_ROUNDS)
 
         out_words = out_1[0].rearrange("p c l -> p (c l)").bitcast(I32)
@@ -330,22 +330,22 @@ def tile_attend_gtd_pl_kernel(tc, x2, x, w0, wT, us, ts, rw, wt, offs, aoffs, ou
             cut = slice(first * WIDTH, (first + count) * WIDTH)
             nc.sync.dma_start(out=out_words[:, cut], in_=y_codes[:, cut].bitcast(I32))
 
-        for first in range(0, SCALAR_WEAVES, 2):
+        for first in (4, 6, 0, 2):
             weave(first, 2)
         weave(8, 4)
         weave(12, 2)
         quantise(8, 4)
         store_codes(8, 4)
         weave(14, 2)
-        quantise(0, 2)
-        quantise(2, 2)
-        store_codes(0, 4)
-        quantise(12, 2)
-        quantise(14, 2)
-        store_codes(12, 4)
         quantise(4, 2)
         quantise(6, 2)
         store_codes(4, 4)
+        quantise(12, 2)
+        quantise(14, 2)
+        store_codes(12, 4)
+        quantise(0, 2)
+        quantise(2, 2)
+        store_codes(0, 4)
         out_scales = out_2[0].bitcast(I32).rearrange("f (g c) -> g f c", g=4)
         for quad in range(4):
             queue = nc.scalar if quad % 2 else nc.sync

@@ -344,9 +344,9 @@ def tile_attend_gtd_pl_kernel(tc, x2, x, w0, wT, us, ts, rw, wt, offs, aoffs, ou
         quantise(14, 2)
         store_codes(12, 4)
         quantise(0, 2)
+        store_codes(0, 2)
         quantise(2, 2)
-        store_codes(0, 4)
+        store_codes(2, 2)
         out_scales = out_2[0].bitcast(I32).rearrange("f (g c) -> g f c", g=4)
         for quad in range(4):
-            queue = nc.scalar if quad % 2 else nc.sync
-            queue.dma_start(out=out_scales[:, 4 * quad : 4 * quad + 4, :], in_=y_scales[32 * quad : 32 * quad + 16, :].bitcast(I32))
+            nc.sync.dma_start(out=out_scales[:, 4 * quad : 4 * quad + 4, :], in_=y_scales[32 * quad : 32 * quad + 16, :].bitcast(I32))

@@ -117,7 +117,9 @@ def tile_attend_gtd_pl_kernel(tc, x2, x, w0, wT, us, ts, rw, wt, offs, aoffs, ou
         cols = sb("cols", [P, 3 * BLOCKS], F32)
         nc.scalar.activation(cols[:], vec_bank[:, 0 : 3 * BLOCKS], COPY)
 
-        xT = [keep.tile([P, HALF], F32, name="xT%d" % t, tag="xT%d" % t, align_bytes=64) for t in range(PACK)]
+        xT = [keep.tile([P, HALF], F32, name="xT%d" % t, tag="xT%d" % t, align_bytes=64)[:] for t in range(2)]
+        xT_pair = sb("xT_pair", [P, 2, HALF], F32)
+        xT += [xT_pair[:, k, :] for k in range(2)]
         slope = sb("slope", [P, BLOCKS], F32)
         nc.vector.tensor_scalar(out=slope[:], in0=cols[:, WT : WT + BLOCKS], scalar1=-DISCOUNT, scalar2=None, op0=ALU.mult)
         base = sb("base", [P, BLOCKS], F32)
@@ -160,7 +162,7 @@ def tile_attend_gtd_pl_kernel(tc, x2, x, w0, wT, us, ts, rw, wt, offs, aoffs, ou
             xt_bank = bank(number, "xt_bank%d_%d" % (t, blocks[0]))
             for b in blocks:
                 nc.tensor.transpose(xt_bank[:, block(b)], x_sb[b].rearrange("r (p t) -> r t p", t=PACK)[:, t, :], ident[:])
-            nc.scalar.copy(in_pairs(xT[t][:]), turned_early(xt_bank))
+            nc.scalar.copy(in_pairs(xT[t]), turned_early(xt_bank))
 
         largest = sb("largest", [P, BLOCKS], F32)
         row_banks = [bank(4 + b, "row_bank%d" % b) for b in range(2)]
@@ -259,7 +261,7 @@ def tile_attend_gtd_pl_kernel(tc, x2, x, w0, wT, us, ts, rw, wt, offs, aoffs, ou
             turn_into(late_x[t], t, LATE_BLOCKS)
 
         early_product = sb("early_product", [P, HALF], F32)
-        nc.vector.tensor_tensor(early_product[:], xT[1][:], err[:, span(EARLY_BLOCKS)], ALU.mult)
+        nc.vector.tensor_tensor(early_product[:], xT[1], err[:, span(EARLY_BLOCKS)], ALU.mult)
         windows = {}
         for t, tag in zip((0, 1, 3, 2), ("x2_bf1", "scaled_rows", "table0", "table1")):
             windows[t] = keep.tile([P, T], F32, name="window_%d" % t, tag=tag, align_bytes=64)
@@ -277,12 +279,13 @@ def tile_attend_gtd_pl_kernel(tc, x2, x, w0, wT, us, ts, rw, wt, offs, aoffs, ou
             copy(rounded[:, t, cut], windows[t][:, cut])
 
         scatter(1, EARLY_BLOCKS, early_product[:])
-        nc.vector.tensor_tensor(windows[0][:].indirect(entries(EARLY_BLOCKS)), xT[0][:], err[:, span(EARLY_BLOCKS)], ALU.mult)
-        rounded = sb("rounded", [P, PACK, T], BF16)
-        product2 = rounded[:].rearrange("p t c -> p (t c)")[:, 2 * T - R : 2 * T + R].bitcast(F32)
-        early3 = keep.tile([P, HALF], F32, name="early3", tag="xT1", align_bytes=64)
-        nc.gpsimd.tensor_tensor(early3[:], xT[3][:], err[:, span(EARLY_BLOCKS)], ALU.mult)
-        nc.gpsimd.tensor_tensor(product2[:, span(EARLY_BLOCKS)], xT[2][:], err[:, span(EARLY_BLOCKS)], ALU.mult)
+        nc.vector.tensor_tensor(windows[0][:].indirect(entries(EARLY_BLOCKS)), xT[0], err[:, span(EARLY_BLOCKS)], ALU.mult)
+        rounded = keep.tile([P, PACK, T], BF16, name="rounded", tag="xT1", align_bytes=64)
+        words = rounded[:].rearrange("p t c -> p (t c)").bitcast(F32)
+        product2 = words[:, T - HALF : T + HALF]
+        early_pair = words[:, T - HALF : 2 * T - HALF].rearrange("p (k c) -> p k c", k=2)[:, :, 0:HALF]
+        early3 = early_pair[:, 1, :]
+        nc.gpsimd.tensor_tensor(early_pair, xT_pair[:], err[:, span(EARLY_BLOCKS)].unsqueeze(1).to_broadcast([P, 2, HALF]), ALU.mult)
         late_products = [sb("late_product%d" % t, [P, HALF], F32)[:] for t in range(2)]
         late_products += [product2[:, span(LATE_BLOCKS)], sb("late_product3", [P, HALF], F32)[:]]
         for t in late_order:
@@ -292,7 +295,7 @@ def tile_attend_gtd_pl_kernel(tc, x2, x, w0, wT, us, ts, rw, wt, offs, aoffs, ou
         nc.vector.tensor_copy(windows[1][:].indirect(entries(LATE_BLOCKS)), late_products[1])
         store(1)
         scatter(3, LATE_BLOCKS, late_products[3])
-        scatter(3, EARLY_BLOCKS, early3[:])
+        scatter(3, EARLY_BLOCKS, early3)
         store(3)
         nc.vector.tensor_copy(windows[2][:].indirect(taken[:]), product2)
         store(2)

@@ -32,7 +32,7 @@ WIDTH = 128
 CHUNKS = T // WIDTH
 SCALAR_ROUNDS = 12
 SCALAR_WEAVES = 8
-GPSIMD_ROUNDS = 10
+GPSIMD_ROUNDS = 7
 RUN = 4
 SCALE_CHUNKS = CHUNKS // 4
 US, RW, WT = 0, BLOCKS, 2 * BLOCKS
@@ -230,7 +230,7 @@ def tile_attend_gtd_pl_kernel(tc, x2, x, w0, wT, us, ts, rw, wt, offs, aoffs, ou
 
         row_sum = [sb("row_sum%d" % b, [P, 1], F32) for b in range(BLOCKS)]
         err = sb("err", [P, R], F32)
-        e_banks = [bank(number, "e_bank%d" % b) for b, number in enumerate((0, 1, 4))] + [bank(5, "e_bank3", count=3)]
+        e_banks = [bank(number, "e_bank%d" % b) for b, number in enumerate((0, 1, 4))] + [bank(5, "e_bank3", count=2)]
 
         def spread(b, column, start, stop):
             nc.tensor.matmul(e_banks[b][:, 0:P], lhsT=column[:].to_broadcast([P, P]), rhs=ident[:], is_transpose=True, start=start, stop=stop)
@@ -255,10 +255,14 @@ def tile_attend_gtd_pl_kernel(tc, x2, x, w0, wT, us, ts, rw, wt, offs, aoffs, ou
                 nc.tensor.transpose(target[:, block(n)], x_sb[b].rearrange("r (p t) -> r t p", t=PACK)[:, t, :], ident[:])
 
         late_banks = [bank(3, "late_bank0"), bank(6, "late_bank1")]
-        late_order = (0, 3, 1, 2)
+        late_order = (0, 1, 3)
         late_x = {t: late_banks[n // 2][:, HALF * (n % 2) : HALF * (n % 2 + 1)] for n, t in enumerate(late_order)}
         for t in late_order:
             turn_into(late_x[t], t, LATE_BLOCKS)
+        late_bank2 = bank(7, "late_bank2")
+        turn_into(late_bank2, 2, LATE_BLOCKS)
+        late_x2 = sb("late_x2", [P, HALF], F32)
+        nc.scalar.copy(late_x2[:], late_bank2[:, 0:HALF])
 
         early_product = sb("early_product", [P, HALF], F32)
         nc.vector.tensor_tensor(early_product[:], xT[1], err[:, span(EARLY_BLOCKS)], ALU.mult)
@@ -286,8 +290,8 @@ def tile_attend_gtd_pl_kernel(tc, x2, x, w0, wT, us, ts, rw, wt, offs, aoffs, ou
         early_pair = words[:, T - HALF : 2 * T - HALF].rearrange("p (k c) -> p k c", k=2)[:, :, 0:HALF]
         early3 = early_pair[:, 1, :]
         nc.gpsimd.tensor_tensor(early_pair, xT_pair[:], err[:, span(EARLY_BLOCKS)].unsqueeze(1).to_broadcast([P, 2, HALF]), ALU.mult)
-        late_products = [sb("late_product%d" % t, [P, HALF], F32)[:] for t in range(2)]
-        late_products += [product2[:, span(LATE_BLOCKS)], sb("late_product3", [P, HALF], F32)[:]]
+        nc.gpsimd.tensor_tensor(product2[:, span(LATE_BLOCKS)], late_x2[:], err[:, span(LATE_BLOCKS)], ALU.mult)
+        late_products = {t: sb("late_product%d" % t, [P, HALF], F32)[:] for t in late_order}
         for t in late_order:
             nc.vector.tensor_tensor(late_products[t], late_x[t], err[:, span(LATE_BLOCKS)], ALU.mult)
         scatter(0, LATE_BLOCKS, late_products[0])

@@ -144,7 +144,7 @@ def tile_attend_gtd_pl_kernel(tc, x2, x, w0, wT, us, ts, rw, wt, offs, aoffs, ou
 
         x2_codes = sb("x2_codes", [P, R], U32)
         x2_scales = sb("x2_scales", [P, R], U8)
-        x2_bf = [keep.tile([P, HALF, PACK], BF16, name="x2_bf%d" % h, tag="x2_bf%d" % h, align_bytes=64) for h in range(2)]
+        x2_bf = [sb("x2_bf%d" % h, [P, HALF, PACK], BF16) for h in range(2)]
         for h, copy in enumerate((nc.vector.tensor_copy, nc.scalar.copy)):
             src = x2_sb[:, :, HALF * h : HALF * (h + 1)].rearrange("p t (c i) -> p c t i", i=4)
             copy(x2_bf[h][:].rearrange("p (c i) t -> p c t i", i=4), src)
@@ -267,7 +267,7 @@ def tile_attend_gtd_pl_kernel(tc, x2, x, w0, wT, us, ts, rw, wt, offs, aoffs, ou
         early_product = sb("early_product", [P, HALF], F32)
         nc.vector.tensor_tensor(early_product[:], xT[1], err[:, span(EARLY_BLOCKS)], ALU.mult)
         windows = {}
-        for t, tag in zip((0, 1, 3, 2), ("x2_bf1", "scaled_rows", "table0", "table1")):
+        for t, tag in zip((0, 1, 3, 2), ("scaled_rows", "table0", "table1", "table2")):
             windows[t] = keep.tile([P, T], F32, name="window_%d" % t, tag=tag, align_bytes=64)
             nc.gpsimd.memset(windows[t][:], 0.0)
         out_planes = out_0.rearrange("(p t) c -> t p c", t=PACK)

@@ -57,8 +57,8 @@ def tile_attend_gtd_pl_kernel(tc, x2, x, w0, wT, us, ts, rw, wt, offs, aoffs, ou
         def sb(name, shape, dtype):
             return keep.tile(shape, dtype, name=name, align_bytes=64)
 
-        def bank(number, name, count=1):
-            return psum.tile([P, 512 * count], F32, name=name, offset=2048 * number)
+        def bank(number, name):
+            return psum.tile([P, 512], F32, name=name, offset=2048 * number)
 
         slots = lists.tile([P, I // 16], U16, name="slots")
         taken = lists.tile([P, R // 16], U16, name="taken")
@@ -223,17 +223,20 @@ def tile_attend_gtd_pl_kernel(tc, x2, x, w0, wT, us, ts, rw, wt, offs, aoffs, ou
             nc.scalar.activation(share[b][:], wtarget[b][:], COPY, scale=1.0 / P)
         look_up_late(2, LATE_BLOCKS)
         look_up_early(2, EARLY_BLOCKS)
-        look_up_early(3, (0,))
         look_up_late(3, (2,))
+        look_up_early(3, (0,))
         look_up_early(3, (1,))
         look_up_late(3, (3,))
 
-        row_sum = [sb("row_sum%d" % b, [P, 1], F32) for b in range(BLOCKS)]
+        row_sum = [keep.tile([P, 1], F32, name="row_sum%d" % b, tag="row_sum%d" % b, align_bytes=64) for b in range(BLOCKS)]
         err = sb("err", [P, R], F32)
-        e_banks = [bank(number, "e_bank%d" % b) for b, number in enumerate((0, 1, 4))] + [bank(5, "e_bank3", count=2)]
+        e_banks = [bank(number, "e_bank%d" % b) for b, number in enumerate((0, 1, 4))] + [bank(5, "e_bank3")]
 
-        def spread(b, column, start, stop):
-            nc.tensor.matmul(e_banks[b][:, 0:P], lhsT=column[:].to_broadcast([P, P]), rhs=ident[:], is_transpose=True, start=start, stop=stop)
+        opening_bank = bank(6, "opening_bank")
+
+        def spread(b, column, start, stop, target=None):
+            target = e_banks[b][:, 0:P] if target is None else target
+            nc.tensor.matmul(target, lhsT=column[:].to_broadcast([P, P]), rhs=ident[:], is_transpose=True, start=start, stop=stop)
 
         for b in LATE_BLOCKS:
             spread(b, wtarget[b], True, False)
@@ -248,12 +251,16 @@ def tile_attend_gtd_pl_kernel(tc, x2, x, w0, wT, us, ts, rw, wt, offs, aoffs, ou
                                                in1=x_sb[b].rearrange("r (p t) -> r p t", t=PACK),
                                                op0=ALU.mult, op1=ALU.mult, accum_out=row_sum[b][:])
             spread(b, row_sum[b], b in EARLY_BLOCKS, True)
+            if b in EARLY_BLOCKS:
+                spread(b, row_sum[b], True, True, opening_bank[:, block(b)])
             nc.scalar.copy(err[:, block(b)], e_banks[b][:, 0:P])
 
         def turn_into(target, t, blocks):
             for n, b in enumerate(blocks):
                 nc.tensor.transpose(target[:, block(n)], x_sb[b].rearrange("r (p t) -> r t p", t=PACK)[:, t, :], ident[:])
 
+        early_product = sb("early_product", [P, HALF], F32)
+        nc.vector.tensor_tensor(early_product[:], opening_bank[:, 0:HALF], xT[1], ALU.mult)
         late_banks = [bank(3, "late_bank0"), bank(6, "late_bank1")]
         late_order = (0, 1, 3)
         late_x = {t: late_banks[n // 2][:, HALF * (n % 2) : HALF * (n % 2 + 1)] for n, t in enumerate(late_order)}
@@ -261,11 +268,9 @@ def tile_attend_gtd_pl_kernel(tc, x2, x, w0, wT, us, ts, rw, wt, offs, aoffs, ou
             turn_into(late_x[t], t, LATE_BLOCKS)
         late_bank2 = bank(7, "late_bank2")
         turn_into(late_bank2, 2, LATE_BLOCKS)
-        late_x2 = sb("late_x2", [P, HALF], F32)
+        late_x2 = keep.tile([P, HALF], F32, name="late_x2", tag="row_sum1", align_bytes=64)
         nc.scalar.copy(late_x2[:], late_bank2[:, 0:HALF])
 
-        early_product = sb("early_product", [P, HALF], F32)
-        nc.vector.tensor_tensor(early_product[:], xT[1], err[:, span(EARLY_BLOCKS)], ALU.mult)
         windows = {}
         for t, tag in zip((0, 1, 3, 2), ("scaled_rows", "table0", "table1", "table2")):
             windows[t] = keep.tile([P, T], F32, name="window_%d" % t, tag=tag, align_bytes=64)

@@ -64,27 +64,24 @@ def tile_attend_gtd_pl_kernel(tc, x2, x, w0, wT, us, ts, rw, wt, offs, aoffs, ou
         taken = lists.tile([P, R // 16], U16, name="taken")
         vecs = sb("vecs", [P, P], F32)
         nc.vector.memset(vecs[:], 0.0)
-        ts_rows = sb("ts_rows", [P, P], F32)
-        nc.vector.memset(ts_rows[:], 0.0)
+        ts_cut = keep.tile([P, T // P], F32, name="ts_cut", tag="ts_cut", align_bytes=64)
 
-        w0_planes = w0.rearrange("(p t) c -> t p c", t=PACK)
-        w0_sb = [sb("w0_%d" % t, [P, T], F32) for t in range(PACK)]
+        w0_pairs = w0.rearrange("(p h t) c -> h p (t c)", h=2, t=2)
+        w0_sb = [sb("w0_%d" % h, [P, 2 * T], F32) for h in range(2)]
 
         def load_vector(first, vec):
             nc.sync.dma_start(out=vecs[first : first + BLOCKS, :], in_=vec.rearrange("(b p) o -> b (p o)", p=P))
 
-        nc.sync.dma_start(out=w0_sb[0][:], in_=w0_planes[0])
-        nc.sync.dma_start(out=ts_rows[0 : T // P, :], in_=ts[0].rearrange("(m p) -> m p", p=P))
+        nc.sync.dma_start(out=ts_cut[:], in_=ts[0].rearrange("(p m) -> p m", p=P))
+        nc.sync.dma_start(out=w0_sb[0][:], in_=w0_pairs[0])
         nc.sync.dma_start(slots[:], offs)
-        nc.sync.dma_start(out=w0_sb[1][:], in_=w0_planes[1])
         load_vector(US, us)
+        nc.sync.dma_start(out=w0_sb[1][:], in_=w0_pairs[1])
         load_vector(RW, rw)
-        nc.sync.dma_start(out=w0_sb[2][:], in_=w0_planes[2])
         load_vector(WT, wt)
-        nc.sync.dma_start(out=w0_sb[3][:], in_=w0_planes[3])
-        nc.sync.dma_start(taken[:], aoffs)
         x2_sb = sb("x2_sb", [P, PACK, R], F32)
         nc.sync.dma_start(out=x2_sb[:], in_=x2.rearrange("(p t) r -> p t r", t=PACK))
+        nc.sync.dma_start(taken[:], aoffs)
         x_early = sb("x_early", [P, EARLY, D], F32)
         x_late = [sb("x_late%d" % b, [P, D], F32) for b in LATE_BLOCKS]
         x_sb = [x_early[:, b, :] for b in EARLY_BLOCKS] + [tile[:] for tile in x_late]
@@ -101,16 +98,13 @@ def tile_attend_gtd_pl_kernel(tc, x2, x, w0, wT, us, ts, rw, wt, offs, aoffs, ou
         make_identity(nc, ident[:])
 
         ts_all = sb("ts_all", [P, T], F32)
-        cut_bank = bank(5, "cut_bank")
-        nc.tensor.transpose(cut_bank[:, 0:P], ts_rows[:], ident[:])
-        ts_cut = sb("ts_cut", [P, T // P], F32)
-        nc.scalar.activation(ts_cut[:], cut_bank[:, 0 : T // P], COPY)
         for g in range(4):
             ts_bank = bank(g, "ts_bank%d" % g)
             for m in range(4):
                 col = 4 * g + m
                 nc.tensor.transpose(ts_bank[:, block(m)], ts_cut[:, col : col + 1].to_broadcast([P, P]), ident[:])
-            nc.scalar.activation(ts_all[:, 512 * g : 512 * (g + 1)], ts_bank[:], COPY)
+            nc.scalar.activation(ts_all[:].rearrange("q (p m) -> q p m", p=P)[:, :, 4 * g : 4 * g + 4],
+                                 ts_bank[:].rearrange("q (m p) -> q p m", p=P), COPY)
 
         vec_bank = bank(4, "vec_bank")
         nc.tensor.transpose(vec_bank[:, 0:P], vecs[:], ident[:])
@@ -126,11 +120,12 @@ def tile_attend_gtd_pl_kernel(tc, x2, x, w0, wT, us, ts, rw, wt, offs, aoffs, ou
         nc.vector.scalar_tensor_tensor(out=base[:], in0=cols[:, RW : RW + BLOCKS], scalar=-1.0, in1=cols[:, WT : WT + BLOCKS],
                                        op0=ALU.mult, op1=ALU.mult)
 
-        w0_bf = sb("w0_bf", [P, I, PACK], BF16)
+        w0_bf = keep.tile([P, I, PACK], BF16, name="w0_bf", tag="ts_cut", align_bytes=64)
         ts_listed = sb("ts_listed", [P, I], F32)
-        for t in range(PACK):
-            nc.vector.tensor_copy(w0_bf[:, :, t], w0_sb[t][:].indirect(slots[:]))
-            if t == 1:
+        for h in range(2):
+            nc.scalar.activation(w0_bf[:, :, h], w0_sb[h][:].indirect(slots[:]), COPY)
+            nc.vector.tensor_copy(w0_bf[:, :, 2 + h], w0_sb[h][:, T : 2 * T].indirect(slots[:]))
+            if h == 0:
                 nc.vector.tensor_copy(ts_listed[:], ts_all[:].indirect(slots[:]))
         w0_codes = sb("w0_codes", [P, I], U32)
         w0_scales = sb("w0_scales", [P, I], U8)
@@ -146,8 +141,8 @@ def tile_attend_gtd_pl_kernel(tc, x2, x, w0, wT, us, ts, rw, wt, offs, aoffs, ou
         x2_scales = sb("x2_scales", [P, R], U8)
         x2_bf = [sb("x2_bf%d" % h, [P, HALF, PACK], BF16) for h in range(2)]
         for h, copy in enumerate((nc.vector.tensor_copy, nc.scalar.copy)):
-            src = x2_sb[:, :, HALF * h : HALF * (h + 1)].rearrange("p t (c i) -> p c t i", i=4)
-            copy(x2_bf[h][:].rearrange("p (c i) t -> p c t i", i=4), src)
+            src = x2_sb[:, :, HALF * h : HALF * (h + 1)].rearrange("p (u t) (c i) -> p c t u i", t=2, i=4)
+            copy(x2_bf[h][:].rearrange("p (c i) (t u) -> p c t u i", t=2, i=4), src)
         for h in range(2):
             cut = slice(HALF * h, HALF * (h + 1))
             nc.vector.quantize_mx(out=x2_codes[:, cut].bitcast(FP8X4), scales=x2_scales[:, cut], in_=x2_bf[h][:].rearrange("p r t -> p (r t)"))

@@ -24,6 +24,7 @@ BLOCKS = 4
 HALF = R // 2
 LIST_COLUMNS = P // 16
 DISCOUNT = 0.9
+TS_PLACE = 0
 EARLY = 2
 EARLY_BLOCKS = tuple(range(EARLY))
 LATE_BLOCKS = tuple(range(EARLY, BLOCKS))
@@ -52,6 +53,7 @@ def tile_attend_gtd_pl_kernel(tc, x2, x, w0, wT, us, ts, rw, wt, offs, aoffs, ou
         lists = ctx.enter_context(tc.tile_pool(name="lists", bufs=1))
         keep = ctx.enter_context(tc.tile_pool(name="keep", bufs=1))
         spare = ctx.enter_context(tc.tile_pool(name="spare", bufs=BLOCKS))
+        placed = ctx.enter_context(tc.tile_pool(name="placed", bufs=1))
         psum = ctx.enter_context(tc.psum_pool(name="psum", bufs=1))
 
         def sb(name, shape, dtype):
@@ -64,7 +66,7 @@ def tile_attend_gtd_pl_kernel(tc, x2, x, w0, wT, us, ts, rw, wt, offs, aoffs, ou
         taken = lists.tile([P, R // 16], U16, name="taken")
         vecs = sb("vecs", [P, P], F32)
         nc.vector.memset(vecs[:], 0.0)
-        ts_cut = keep.tile([P, T // P], F32, name="ts_cut", tag="ts_cut", align_bytes=64)
+        ts_cut = sb("ts_cut", [P, T // P], F32)
 
         w0_pairs = w0.rearrange("(p h t) c -> h p (t c)", h=2, t=2)
         w0_sb = [sb("w0_%d" % h, [P, 2 * T], F32) for h in range(2)]
@@ -97,7 +99,7 @@ def tile_attend_gtd_pl_kernel(tc, x2, x, w0, wT, us, ts, rw, wt, offs, aoffs, ou
         ident = sb("ident", [P, P], F32)
         make_identity(nc, ident[:])
 
-        ts_all = sb("ts_all", [P, T], F32)
+        ts_all = placed.tile([P, T], F32, name="ts_all", offset=TS_PLACE)
         for g in range(4):
             ts_bank = bank(g, "ts_bank%d" % g)
             for m in range(4):
@@ -115,21 +117,30 @@ def tile_attend_gtd_pl_kernel(tc, x2, x, w0, wT, us, ts, rw, wt, offs, aoffs, ou
         xT_pair = sb("xT_pair", [P, 2, HALF], F32)
         xT += [xT_pair[:, k, :] for k in range(2)]
         slope = sb("slope", [P, BLOCKS], F32)
-        nc.vector.tensor_scalar(out=slope[:], in0=cols[:, WT : WT + BLOCKS], scalar1=-DISCOUNT, scalar2=None, op0=ALU.mult)
         base = sb("base", [P, BLOCKS], F32)
-        nc.vector.scalar_tensor_tensor(out=base[:], in0=cols[:, RW : RW + BLOCKS], scalar=-1.0, in1=cols[:, WT : WT + BLOCKS],
-                                       op0=ALU.mult, op1=ALU.mult)
+        for blocks, part in ((EARLY_BLOCKS, 1.0 / P), (LATE_BLOCKS, 1.0)):
+            cut = slice(blocks[0], blocks[-1] + 1)
+            weights = cols[:, WT + cut.start : WT + cut.stop]
+            nc.vector.tensor_scalar(out=slope[:, cut], in0=weights, scalar1=-DISCOUNT * part, scalar2=None, op0=ALU.mult)
+            nc.vector.scalar_tensor_tensor(out=base[:, cut], in0=cols[:, RW + cut.start : RW + cut.stop], scalar=-part, in1=weights,
+                                           op0=ALU.mult, op1=ALU.mult)
 
-        w0_bf = keep.tile([P, I, PACK], BF16, name="w0_bf", tag="ts_cut", align_bytes=64)
         ts_listed = sb("ts_listed", [P, I], F32)
+        nc.vector.tensor_copy(ts_listed[:], ts_all[:].indirect(slots[:]))
+        w0_bf = [placed.tile([P, HALF, PACK], BF16, name="w0_bf%d" % k, offset=TS_PLACE + HALF * PACK * 2 * k, align_bytes=64) for k in range(2)]
+
+        def listed(k):
+            return slots[:, 2 * LIST_COLUMNS * k : 2 * LIST_COLUMNS * (k + 1)]
+
         for h in range(2):
-            nc.scalar.activation(w0_bf[:, :, h], w0_sb[h][:].indirect(slots[:]), COPY)
-            nc.vector.tensor_copy(w0_bf[:, :, 2 + h], w0_sb[h][:, T : 2 * T].indirect(slots[:]))
-            if h == 0:
-                nc.vector.tensor_copy(ts_listed[:], ts_all[:].indirect(slots[:]))
+            for k in range(2):
+                nc.scalar.activation(w0_bf[k][:, :, h], w0_sb[h][:].indirect(listed(k)), COPY)
+                nc.vector.tensor_copy(w0_bf[1 - k][:, :, 2 + h], w0_sb[h][:, T : 2 * T].indirect(listed(1 - k)))
         w0_codes = sb("w0_codes", [P, I], U32)
         w0_scales = sb("w0_scales", [P, I], U8)
-        nc.vector.quantize_mx(out=w0_codes[:].bitcast(FP8X4), scales=w0_scales[:], in_=w0_bf[:].rearrange("p i t -> p (i t)"))
+        for k in range(2):
+            cut = slice(HALF * k, HALF * (k + 1))
+            nc.vector.quantize_mx(out=w0_codes[:, cut].bitcast(FP8X4), scales=w0_scales[:, cut], in_=w0_bf[k][:].rearrange("p i t -> p (i t)"))
 
         tscol_bank = bank(4, "tscol_bank")
         for j in range(BLOCKS):
@@ -139,7 +150,7 @@ def tile_attend_gtd_pl_kernel(tc, x2, x, w0, wT, us, ts, rw, wt, offs, aoffs, ou
 
         x2_codes = sb("x2_codes", [P, R], U32)
         x2_scales = sb("x2_scales", [P, R], U8)
-        x2_bf = [sb("x2_bf%d" % h, [P, HALF, PACK], BF16) for h in range(2)]
+        x2_bf = [sb("x2_bf0", [P, HALF, PACK], BF16), keep.tile([P, HALF, PACK], BF16, name="x2_bf1", tag="scaled_rows", align_bytes=64)]
         for h, copy in enumerate((nc.vector.tensor_copy, nc.scalar.copy)):
             src = x2_sb[:, :, HALF * h : HALF * (h + 1)].rearrange("p (u t) (c i) -> p c t u i", t=2, i=4)
             copy(x2_bf[h][:].rearrange("p (c i) (t u) -> p c t u i", t=2, i=4), src)
@@ -182,6 +193,16 @@ def tile_attend_gtd_pl_kernel(tc, x2, x, w0, wT, us, ts, rw, wt, offs, aoffs, ou
             for j in range(BLOCKS):
                 nc.tensor.transpose(z_banks[k][:, block(j)], scaled_slots[j][:, block(k)], ident[:])
 
+        for k in range(2):
+            b = 2 + k
+            unread = spare.tile([P, I], F32, name="unread", tag="unread")
+            nc.vector.tensor_scalar(out=unread[:], in0=z_banks[k][:], scalar1=cols[:, US + b : US + b + 1], scalar2=None,
+                                    op0=ALU.mult, op1=ALU.max, accum_out=largest[:, b : b + 1])
+        sloped = sb("sloped", [P, BLOCKS], F32)
+        nc.vector.tensor_tensor(sloped[:], largest[:], slope[:], ALU.mult)
+        wtarget = sb("wtarget", [P, BLOCKS], F32)
+        nc.vector.tensor_tensor(wtarget[:], sloped[:], base[:], ALU.add)
+
         terms = [sb("terms%d" % t, [P, R], F32) for t in range(PACK)]
         q_banks = [bank(b, "q_bank%d" % b) for b in range(BLOCKS)]
 
@@ -205,17 +226,6 @@ def tile_attend_gtd_pl_kernel(tc, x2, x, w0, wT, us, ts, rw, wt, offs, aoffs, ou
         for t in range(2):
             look_up_late(t, LATE_BLOCKS)
             look_up_early(t, EARLY_BLOCKS)
-        for k in range(2):
-            b = 2 + k
-            unread = spare.tile([P, I], F32, name="unread", tag="unread")
-            nc.vector.tensor_scalar(out=unread[:], in0=z_banks[k][:], scalar1=cols[:, US + b : US + b + 1], scalar2=None,
-                                    op0=ALU.mult, op1=ALU.max, accum_out=largest[:, b : b + 1])
-        wtarget = [sb("wtarget%d" % b, [P, 1], F32) for b in range(BLOCKS)]
-        for b in range(BLOCKS):
-            nc.scalar.activation(wtarget[b][:], largest[:, b : b + 1], IDENTITY, scale=slope[:, b : b + 1], bias=base[:, b : b + 1])
-        share = [sb("share%d" % b, [P, 1], F32) for b in EARLY_BLOCKS]
-        for b in EARLY_BLOCKS:
-            nc.scalar.activation(share[b][:], wtarget[b][:], COPY, scale=1.0 / P)
         look_up_late(2, LATE_BLOCKS)
         look_up_early(2, EARLY_BLOCKS)
         look_up_late(3, (2,))
@@ -231,23 +241,23 @@ def tile_attend_gtd_pl_kernel(tc, x2, x, w0, wT, us, ts, rw, wt, offs, aoffs, ou
 
         def spread(b, column, start, stop, target=None):
             target = e_banks[b][:, 0:P] if target is None else target
-            nc.tensor.matmul(target, lhsT=column[:].to_broadcast([P, P]), rhs=ident[:], is_transpose=True, start=start, stop=stop)
+            nc.tensor.matmul(target, lhsT=column.to_broadcast([P, P]), rhs=ident[:], is_transpose=True, start=start, stop=stop)
 
         for b in LATE_BLOCKS:
-            spread(b, wtarget[b], True, False)
+            spread(b, wtarget[:, b : b + 1], True, False)
         for b in ALL_BLOCKS:
             unread = spare.tile([P, D], F32, name="unread", tag="unread")
             if b in EARLY_BLOCKS:
-                nc.scalar.activation(unread[:, 0:P], q_banks[b][:, 0:P], IDENTITY, scale=cols[:, WT + b : WT + b + 1], bias=share[b][:],
+                nc.scalar.activation(unread[:, 0:P], q_banks[b][:, 0:P], IDENTITY, scale=cols[:, WT + b : WT + b + 1], bias=wtarget[:, b : b + 1],
                                      accum_out=row_sum[b][:])
             else:
                 nc.vector.scalar_tensor_tensor(out=unread[:].rearrange("r (p t) -> r p t", t=PACK),
                                                in0=q_banks[b][:].rearrange("r (t p) -> r p t", t=PACK), scalar=cols[:, WT + b : WT + b + 1],
                                                in1=x_sb[b].rearrange("r (p t) -> r p t", t=PACK),
                                                op0=ALU.mult, op1=ALU.mult, accum_out=row_sum[b][:])
-            spread(b, row_sum[b], b in EARLY_BLOCKS, True)
+            spread(b, row_sum[b][:], b in EARLY_BLOCKS, True)
             if b in EARLY_BLOCKS:
-                spread(b, row_sum[b], True, True, opening_bank[:, block(b)])
+                spread(b, row_sum[b][:], True, True, opening_bank[:, block(b)])
             nc.scalar.copy(err[:, block(b)], e_banks[b][:, 0:P])
 
         def turn_into(target, t, blocks):

from contextlib import ExitStack

import concourse.mybir as mybir
from concourse.masks import make_identity

D, R, I, T = 512, 512, 512, 2048
FLOPS = 2 * D * R * I
BYTES = 4 * (2 * D * R + 2 * D * T + T + 3 * R + D * T) + 2 * 2 * 128 * 32 + D * T + 16 * T

F32 = mybir.dt.float32
BF16 = mybir.dt.bfloat16
U32 = mybir.dt.uint32
I32 = mybir.dt.int32
U16 = mybir.dt.uint16
U8 = mybir.dt.uint8
FP8X4 = mybir.dt.float8_e4m3fn_x4
ALU = mybir.AluOpType
COPY = mybir.ActivationFunctionType.Copy
IDENTITY = mybir.ActivationFunctionType.Identity

P = 128
PACK = 4
BLOCKS = 4
HALF = R // 2
LIST_COLUMNS = P // 16
DISCOUNT = 0.9
TS_PLACE = 0
EARLY = 2
EARLY_BLOCKS = tuple(range(EARLY))
LATE_BLOCKS = tuple(range(EARLY, BLOCKS))
ALL_BLOCKS = tuple(range(BLOCKS))
WIDTH = 128
CHUNKS = T // WIDTH
SCALAR_ROUNDS = 12
SCALAR_WEAVES = 8
GPSIMD_ROUNDS = 7
RUN = 4
SCALE_CHUNKS = CHUNKS // 4
US, RW, WT = 0, BLOCKS, 2 * BLOCKS


def block(b):
    return slice(P * b, P * (b + 1))


def span(blocks):
    return slice(P * blocks[0], P * (blocks[-1] + 1))


def tile_attend_gtd_pl_kernel(tc, x2, x, w0, wT, us, ts, rw, wt, offs, aoffs, out_0, out_1, out_2):
    nc = tc.nc
    with ExitStack() as ctx:
        lists = ctx.enter_context(tc.tile_pool(name="lists", bufs=1))
        keep = ctx.enter_context(tc.tile_pool(name="keep", bufs=1))
        spare = ctx.enter_context(tc.tile_pool(name="spare", bufs=BLOCKS))
        placed = ctx.enter_context(tc.tile_pool(name="placed", bufs=1))
        psum = ctx.enter_context(tc.psum_pool(name="psum", bufs=1))

        def sb(name, shape, dtype):
            return keep.tile(shape, dtype, name=name, align_bytes=64)

        def bank(number, name):
            return psum.tile([P, 512], F32, name=name, offset=2048 * number)

        slots = lists.tile([P, I // 16], U16, name="slots")
        taken = lists.tile([P, R // 16], U16, name="taken")
        vecs = sb("vecs", [P, P], F32)
        nc.vector.memset(vecs[:], 0.0)
        ts_cut = sb("ts_cut", [P, T // P], F32)

        w0_pairs = w0.rearrange("(p h t) c -> h p (t c)", h=2, t=2)
        w0_sb = [sb("w0_%d" % h, [P, 2 * T], F32) for h in range(2)]

        def load_vector(first, vec):
            nc.sync.dma_start(out=vecs[first : first + BLOCKS, :], in_=vec.rearrange("(b p) o -> b (p o)", p=P))

        nc.sync.dma_start(out=ts_cut[:], in_=ts[0].rearrange("(p m) -> p m", p=P))
        nc.sync.dma_start(out=w0_sb[0][:], in_=w0_pairs[0])
        nc.sync.dma_start(slots[:], offs)
        load_vector(US, us)
        nc.sync.dma_start(out=w0_sb[1][:], in_=w0_pairs[1])
        load_vector(RW, rw)
        load_vector(WT, wt)
        x2_sb = sb("x2_sb", [P, PACK, R], F32)
        nc.sync.dma_start(out=x2_sb[:], in_=x2.rearrange("(p t) r -> p t r", t=PACK))
        nc.sync.dma_start(taken[:], aoffs)
        x_early = sb("x_early", [P, EARLY, D], F32)
        x_late = [sb("x_late%d" % b, [P, D], F32) for b in LATE_BLOCKS]
        x_sb = [x_early[:, b, :] for b in EARLY_BLOCKS] + [tile[:] for tile in x_late]
        wT_planes = wT.rearrange("(p t) c -> t p c", t=PACK)
        wT_sb = [keep.tile([P, T], F32, name="wT_%d" % t, tag="table%d" % t, align_bytes=64) for t in range(PACK)]
        for t in range(PACK):
            nc.sync.dma_start(out=wT_sb[t][:], in_=wT_planes[t])
            if t == 0:
                nc.sync.dma_start(out=x_early[:], in_=x[span(EARLY_BLOCKS), :].rearrange("(p b) d -> p b d", p=P))
        for b in LATE_BLOCKS:
            nc.sync.dma_start(out=x_sb[b], in_=x[block(b), :])

        ident = sb("ident", [P, P], F32)
        make_identity(nc, ident[:])

        ts_all = placed.tile([P, T], F32, name="ts_all", offset=TS_PLACE)
        for g in range(4):
            ts_bank = bank(g, "ts_bank%d" % g)
            for m in range(4):
                col = 4 * g + m
                nc.tensor.transpose(ts_bank[:, block(m)], ts_cut[:, col : col + 1].to_broadcast([P, P]), ident[:])
            nc.scalar.activation(ts_all[:].rearrange("q (p m) -> q p m", p=P)[:, :, 4 * g : 4 * g + 4],
                                 ts_bank[:].rearrange("q (m p) -> q p m", p=P), COPY)

        vec_bank = bank(4, "vec_bank")
        nc.tensor.transpose(vec_bank[:, 0:P], vecs[:], ident[:])
        cols = sb("cols", [P, 3 * BLOCKS], F32)
        nc.scalar.activation(cols[:], vec_bank[:, 0 : 3 * BLOCKS], COPY)

        xT = [keep.tile([P, HALF], F32, name="xT%d" % t, tag="xT%d" % t, align_bytes=64)[:] for t in range(2)]
        xT_pair = sb("xT_pair", [P, 2, HALF], F32)
        xT += [xT_pair[:, k, :] for k in range(2)]
        slope = sb("slope", [P, BLOCKS], F32)
        base = sb("base", [P, BLOCKS], F32)
        for blocks, part in ((EARLY_BLOCKS, 1.0 / P), (LATE_BLOCKS, 1.0)):
            cut = slice(blocks[0], blocks[-1] + 1)
            weights = cols[:, WT + cut.start : WT + cut.stop]
            nc.vector.tensor_scalar(out=slope[:, cut], in0=weights, scalar1=-DISCOUNT * part, scalar2=None, op0=ALU.mult)
            nc.vector.scalar_tensor_tensor(out=base[:, cut], in0=cols[:, RW + cut.start : RW + cut.stop], scalar=-part, in1=weights,
                                           op0=ALU.mult, op1=ALU.mult)

        ts_listed = sb("ts_listed", [P, I], F32)
        nc.vector.tensor_copy(ts_listed[:], ts_all[:].indirect(slots[:]))
        w0_bf = [placed.tile([P, HALF, PACK], BF16, name="w0_bf%d" % k, offset=TS_PLACE + HALF * PACK * 2 * k, align_bytes=64) for k in range(2)]

        def listed(k):
            return slots[:, 2 * LIST_COLUMNS * k : 2 * LIST_COLUMNS * (k + 1)]

        for h in range(2):
            for k in range(2):
                nc.scalar.activation(w0_bf[k][:, :, h], w0_sb[h][:].indirect(listed(k)), COPY)
                nc.vector.tensor_copy(w0_bf[1 - k][:, :, 2 + h], w0_sb[h][:, T : 2 * T].indirect(listed(1 - k)))
        w0_codes = sb("w0_codes", [P, I], U32)
        w0_scales = sb("w0_scales", [P, I], U8)
        for k in range(2):
            cut = slice(HALF * k, HALF * (k + 1))
            nc.vector.quantize_mx(out=w0_codes[:, cut].bitcast(FP8X4), scales=w0_scales[:, cut], in_=w0_bf[k][:].rearrange("p i t -> p (i t)"))

        tscol_bank = bank(4, "tscol_bank")
        for j in range(BLOCKS):
            nc.tensor.transpose(tscol_bank[:, block(j)], ts_listed[:, block(j)], ident[:])
        ts_col = sb("ts_col", [P, BLOCKS], F32)
        nc.scalar.activation(ts_col[:], tscol_bank[:].rearrange("p (j q) -> p j q", j=BLOCKS)[:, :, 0], COPY)

        x2_codes = sb("x2_codes", [P, R], U32)
        x2_scales = sb("x2_scales", [P, R], U8)
        x2_bf = [sb("x2_bf0", [P, HALF, PACK], BF16), keep.tile([P, HALF, PACK], BF16, name="x2_bf1", tag="scaled_rows", align_bytes=64)]
        for h, copy in enumerate((nc.vector.tensor_copy, nc.scalar.copy)):
            src = x2_sb[:, :, HALF * h : HALF * (h + 1)].rearrange("p (u t) (c i) -> p c t u i", t=2, i=4)
            copy(x2_bf[h][:].rearrange("p (c i) (t u) -> p c t u i", t=2, i=4), src)
        for h in range(2):
            cut = slice(HALF * h, HALF * (h + 1))
            nc.vector.quantize_mx(out=x2_codes[:, cut].bitcast(FP8X4), scales=x2_scales[:, cut], in_=x2_bf[h][:].rearrange("p r t -> p (r t)"))

        def in_pairs(ap):
            return ap.rearrange("q (p j) -> q p j", j=EARLY)

        def turned_early(tile):
            return tile[:, 0:HALF].rearrange("q (j p) -> q p j", j=EARLY)

        def turn_x(t, blocks, number):
            xt_bank = bank(number, "xt_bank%d_%d" % (t, blocks[0]))
            for b in blocks:
                nc.tensor.transpose(xt_bank[:, block(b)], x_sb[b].rearrange("r (p t) -> r t p", t=PACK)[:, t, :], ident[:])
            nc.scalar.copy(in_pairs(xT[t]), turned_early(xt_bank))

        largest = sb("largest", [P, BLOCKS], F32)
        row_banks = [bank(4 + b, "row_bank%d" % b) for b in range(2)]
        for b in range(2):
            nc.tensor.matmul_mx(out=row_banks[b][:], lhsT=x2_codes[:, block(b)].bitcast(FP8X4), lhsT_scale=x2_scales[:, block(b)],
                                rhs=w0_codes[:].bitcast(FP8X4), rhs_scale=w0_scales[:], start=True, stop=True)
        turn_x(0, EARLY_BLOCKS, 6)
        scaled_rows = keep.tile([P, 2, I], F32, name="scaled_rows", tag="scaled_rows", align_bytes=64)
        for b in range(2):
            nc.vector.scalar_tensor_tensor(out=scaled_rows[:, b, :], in0=row_banks[b][:], scalar=cols[:, US + b : US + b + 1],
                                           in1=ts_listed[:], op0=ALU.mult, op1=ALU.mult)
        nc.vector.tensor_reduce(out=largest[:, 0:2], in_=scaled_rows[:], axis=mybir.AxisListType.X, op=ALU.max)
        scaled_slots = [sb("scaled_slots%d" % j, [P, HALF], F32) for j in range(BLOCKS)]
        for j in range(BLOCKS):
            slot_bank = bank(j, "slot_bank%d" % j)
            nc.tensor.matmul_mx(out=slot_bank[:, 0:HALF], lhsT=w0_codes[:, block(j)].bitcast(FP8X4), lhsT_scale=w0_scales[:, block(j)],
                                rhs=x2_codes[:, HALF:R].bitcast(FP8X4), rhs_scale=x2_scales[:, HALF:R], start=True, stop=True)
            nc.scalar.activation(scaled_slots[j][:], slot_bank[:, 0:HALF], COPY, scale=ts_col[:, j : j + 1])
        turn_x(1, EARLY_BLOCKS, 7)
        z_banks = [bank(4 + k, "z_bank%d" % k) for k in range(2)]
        for k in range(2):
            for j in range(BLOCKS):
                nc.tensor.transpose(z_banks[k][:, block(j)], scaled_slots[j][:, block(k)], ident[:])

        for k in range(2):
            b = 2 + k
            unread = spare.tile([P, I], F32, name="unread", tag="unread")
            nc.vector.tensor_scalar(out=unread[:], in0=z_banks[k][:], scalar1=cols[:, US + b : US + b + 1], scalar2=None,
                                    op0=ALU.mult, op1=ALU.max, accum_out=largest[:, b : b + 1])
        sloped = sb("sloped", [P, BLOCKS], F32)
        nc.vector.tensor_tensor(sloped[:], largest[:], slope[:], ALU.mult)
        wtarget = sb("wtarget", [P, BLOCKS], F32)
        nc.vector.tensor_tensor(wtarget[:], sloped[:], base[:], ALU.add)

        terms = [sb("terms%d" % t, [P, R], F32) for t in range(PACK)]
        q_banks = [bank(b, "q_bank%d" % b) for b in range(BLOCKS)]

        def entries(blocks):
            return taken[:, LIST_COLUMNS * blocks[0] : LIST_COLUMNS * (blocks[-1] + 1)]

        def look_up_early(t, blocks):
            cut = span(blocks)
            nc.vector.tensor_tensor(terms[t][:, cut], wT_sb[t][:].indirect(entries(blocks)), xT[t][:, cut], ALU.mult)
            for b in blocks:
                nc.tensor.matmul(q_banks[b][:, 0:P], lhsT=terms[t][:, block(b)], rhs=ident[:], is_transpose=True,
                                 start=(t == 0), stop=(t == PACK - 1))

        def look_up_late(t, blocks):
            nc.scalar.activation(terms[t][:, span(blocks)], wT_sb[t][:].indirect(entries(blocks)), COPY)
            for b in blocks:
                nc.tensor.transpose(q_banks[b][:, block(t)], terms[t][:, block(b)], ident[:])

        turn_x(2, EARLY_BLOCKS, 6)
        turn_x(3, EARLY_BLOCKS, 7)
        for t in range(2):
            look_up_late(t, LATE_BLOCKS)
            look_up_early(t, EARLY_BLOCKS)
        look_up_late(2, LATE_BLOCKS)
        look_up_early(2, EARLY_BLOCKS)
        look_up_late(3, (2,))
        look_up_early(3, (0,))
        look_up_early(3, (1,))
        look_up_late(3, (3,))

        row_sum = [keep.tile([P, 1], F32, name="row_sum%d" % b, tag="row_sum%d" % b, align_bytes=64) for b in range(BLOCKS)]
        err = sb("err", [P, R], F32)
        e_banks = [bank(number, "e_bank%d" % b) for b, number in enumerate((0, 1, 4))] + [bank(5, "e_bank3")]

        opening_bank = bank(6, "opening_bank")

        def spread(b, column, start, stop, target=None):
            target = e_banks[b][:, 0:P] if target is None else target
            nc.tensor.matmul(target, lhsT=column.to_broadcast([P, P]), rhs=ident[:], is_transpose=True, start=start, stop=stop)

        for b in LATE_BLOCKS:
            spread(b, wtarget[:, b : b + 1], True, False)
        for b in ALL_BLOCKS:
            unread = spare.tile([P, D], F32, name="unread", tag="unread")
            if b in EARLY_BLOCKS:
                nc.scalar.activation(unread[:, 0:P], q_banks[b][:, 0:P], IDENTITY, scale=cols[:, WT + b : WT + b + 1], bias=wtarget[:, b : b + 1],
                                     accum_out=row_sum[b][:])
            else:
                nc.vector.scalar_tensor_tensor(out=unread[:].rearrange("r (p t) -> r p t", t=PACK),
                                               in0=q_banks[b][:].rearrange("r (t p) -> r p t", t=PACK), scalar=cols[:, WT + b : WT + b + 1],
                                               in1=x_sb[b].rearrange("r (p t) -> r p t", t=PACK),
                                               op0=ALU.mult, op1=ALU.mult, accum_out=row_sum[b][:])
            spread(b, row_sum[b][:], b in EARLY_BLOCKS, True)
            if b in EARLY_BLOCKS:
                spread(b, row_sum[b][:], True, True, opening_bank[:, block(b)])
            nc.scalar.copy(err[:, block(b)], e_banks[b][:, 0:P])

        def turn_into(target, t, blocks):
            for n, b in enumerate(blocks):
                nc.tensor.transpose(target[:, block(n)], x_sb[b].rearrange("r (p t) -> r t p", t=PACK)[:, t, :], ident[:])

        early_product = sb("early_product", [P, HALF], F32)
        nc.vector.tensor_tensor(early_product[:], opening_bank[:, 0:HALF], xT[1], ALU.mult)
        late_banks = [bank(3, "late_bank0"), bank(6, "late_bank1")]
        late_order = (0, 1, 3)
        late_x = {t: late_banks[n // 2][:, HALF * (n % 2) : HALF * (n % 2 + 1)] for n, t in enumerate(late_order)}
        for t in late_order:
            turn_into(late_x[t], t, LATE_BLOCKS)
        late_bank2 = bank(7, "late_bank2")
        turn_into(late_bank2, 2, LATE_BLOCKS)
        late_x2 = keep.tile([P, HALF], F32, name="late_x2", tag="row_sum1", align_bytes=64)
        nc.scalar.copy(late_x2[:], late_bank2[:, 0:HALF])

        windows = {}
        for t, tag in zip((0, 1, 3, 2), ("scaled_rows", "table0", "table1", "table2")):
            windows[t] = keep.tile([P, T], F32, name="window_%d" % t, tag=tag, align_bytes=64)
            nc.gpsimd.memset(windows[t][:], 0.0)
        out_planes = out_0.rearrange("(p t) c -> t p c", t=PACK)

        def scatter(t, blocks, source):
            nc.scalar.activation(windows[t][:].indirect(entries(blocks)), source, COPY)

        def store(t):
            nc.sync.dma_start(out=out_planes[t], in_=windows[t][:])

        def round_plane(copy, t, first, count):
            cut = slice(first * WIDTH, (first + count) * WIDTH)
            copy(rounded[:, t, cut], windows[t][:, cut])

        scatter(1, EARLY_BLOCKS, early_product[:])
        nc.vector.tensor_tensor(windows[0][:].indirect(entries(EARLY_BLOCKS)), xT[0], err[:, span(EARLY_BLOCKS)], ALU.mult)
        rounded = keep.tile([P, PACK, T], BF16, name="rounded", tag="xT1", align_bytes=64)
        words = rounded[:].rearrange("p t c -> p (t c)").bitcast(F32)
        product2 = words[:, T - HALF : T + HALF]
        early_pair = words[:, T - HALF : 2 * T - HALF].rearrange("p (k c) -> p k c", k=2)[:, :, 0:HALF]
        early3 = early_pair[:, 1, :]
        nc.gpsimd.tensor_tensor(early_pair, xT_pair[:], err[:, span(EARLY_BLOCKS)].unsqueeze(1).to_broadcast([P, 2, HALF]), ALU.mult)
        nc.gpsimd.tensor_tensor(product2[:, span(LATE_BLOCKS)], late_x2[:], err[:, span(LATE_BLOCKS)], ALU.mult)
        late_products = {t: sb("late_product%d" % t, [P, HALF], F32)[:] for t in late_order}
        for t in late_order:
            nc.vector.tensor_tensor(late_products[t], late_x[t], err[:, span(LATE_BLOCKS)], ALU.mult)
        scatter(0, LATE_BLOCKS, late_products[0])
        store(0)
        nc.vector.tensor_copy(windows[1][:].indirect(entries(LATE_BLOCKS)), late_products[1])
        store(1)
        scatter(3, LATE_BLOCKS, late_products[3])
        scatter(3, EARLY_BLOCKS, early3)
        store(3)
        nc.vector.tensor_copy(windows[2][:].indirect(taken[:]), product2)
        store(2)

        def gpsimd_copy(out, in_):
            nc.gpsimd.tensor_scalar(out=out, in0=in_, scalar1=1.0, scalar2=-0.0, op0=ALU.mult, op1=ALU.add)

        round_plane(gpsimd_copy, 0, 0, CHUNKS)
        round_plane(gpsimd_copy, 1, 0, GPSIMD_ROUNDS)
        round_plane(nc.scalar.copy, 3, SCALAR_WEAVES, SCALAR_ROUNDS - SCALAR_WEAVES)
        round_plane(nc.scalar.copy, 3, 0, SCALAR_WEAVES)
        round_plane(nc.vector.tensor_copy, 2, 0, CHUNKS)
        round_plane(nc.vector.tensor_copy, 1, GPSIMD_ROUNDS, CHUNKS - GPSIMD_ROUNDS)
        round_plane(nc.vector.tensor_copy, 3, SCALAR_ROUNDS, CHUNKS - SCALAR_ROUNDS)

        out_words = out_1[0].rearrange("p c l -> p (c l)").bitcast(I32)
        y_scales = sb("y_scales", [P, SCALE_CHUNKS * WIDTH], U8)
        grouped = sb("grouped", [P, T * PACK], BF16)
        y_codes = sb("y_codes", [P, T], U32)

        def weave(first, count):
            dst = grouped[:, first * WIDTH * PACK : (first + count) * WIDTH * PACK]
            src = rounded[:, :, first * WIDTH : (first + count) * WIDTH]
            copy = nc.scalar.copy if first < SCALAR_WEAVES else nc.vector.tensor_copy
            copy(dst.rearrange("p (c i t) -> p c t i", i=RUN, t=PACK), src.rearrange("p t (c i) -> p c t i", i=RUN))

        def quantise(first, count):
            cut = slice(first * WIDTH, (first + count) * WIDTH)
            place = first % SCALE_CHUNKS
            nc.vector.quantize_mx(out=y_codes[:, cut].bitcast(FP8X4),
                                  scales=y_scales[4 * (first // SCALE_CHUNKS) : P, place * WIDTH : (place + count) * WIDTH],
                                  in_=grouped[:, first * WIDTH * PACK : (first + count) * WIDTH * PACK])

        def store_codes(first, count):
            cut = slice(first * WIDTH, (first + count) * WIDTH)
            nc.sync.dma_start(out=out_words[:, cut], in_=y_codes[:, cut].bitcast(I32))

        for first in (4, 6, 0, 2):
            weave(first, 2)
        weave(8, 4)
        weave(12, 2)
        quantise(8, 4)
        store_codes(8, 4)
        weave(14, 2)
        quantise(4, 2)
        quantise(6, 2)
        store_codes(4, 4)
        quantise(12, 2)
        quantise(14, 2)
        store_codes(12, 4)
        quantise(0, 2)
        store_codes(0, 2)
        quantise(2, 2)
        store_codes(2, 2)
        out_scales = out_2[0].bitcast(I32).rearrange("f (g c) -> g f c", g=4)
        for quad in range(4):
            nc.sync.dma_start(out=out_scales[:, 4 * quad : 4 * quad + 4, :], in_=y_scales[32 * quad : 32 * quad + 16, :].bitcast(I32))
